import numpy as np
import ml_dtypes


def mxq(x, axis, fmt="e4m3"):
    dtype, down = {"e4m3": (ml_dtypes.float8_e4m3fn, 7), "e5m2": (ml_dtypes.float8_e5m2, 14)}[fmt]
    v = np.moveaxis(np.asarray(x, np.float32).astype(ml_dtypes.bfloat16).astype(np.float64), axis, -1)
    blocks = v.reshape(v.shape[:-1] + (-1, 32))
    amax = np.abs(blocks).max(-1, keepdims=True)
    byte = np.maximum(np.where(amax > 0, np.frexp(amax)[1] - 1 + 127, 0) - down, 1)
    scale = np.exp2(byte - 127.0)
    codes = (blocks / scale).astype(np.float32).astype(dtype).astype(np.float64)
    return np.moveaxis((codes * scale).reshape(v.shape), -1, axis)


WIDE = False


def mx_kscale(k):
    if not WIDE:
        return np.ones(k)
    levels = np.array([30, -30])
    if k % 512:
        return np.exp2(np.random.permutation(np.resize(levels, k // 32))).repeat(32)
    a = np.empty((k // 512, 16))
    for p in range(k // 512):
        a[p, :8] = np.random.permutation(np.resize(levels, 8))
        for g in range(8):
            far = levels[np.abs(levels - a[p, g]) >= 10]
            a[p, g + 8] = far[np.random.randint(len(far))]
    return np.exp2(a.ravel()).repeat(32)


def f64(x):
    return np.asarray(x).astype(np.float64)


K, L, M, N = 2048, 512, 256, 1536


def setup_inputs():
    n = np.random.standard_normal
    s1 = mx_kscale(K)[:, None]
    s2 = mx_kscale(L)[:, None]
    m1, m2 = np.exp(0.5 * n((1, M))), np.exp(0.5 * n((1, N)))
    return {
        "x": (n((K, M)) / np.sqrt(K) * s1).astype(np.float32),
        "xt": (n((K, N)) / s1).astype(np.float32),
        "g": (m1 * n((L, M)) / np.sqrt(L) * s2).astype(np.float32),
        "gt": (m2 * n((L, N)) / s2).astype(np.float32),
    }


def reference(x, xt, g, gt):
    x_ = mxq(f64(x), 0, "e4m3")
    xt_ = mxq(f64(xt), 0, "e4m3")
    g_ = mxq(f64(g), 0, "e5m2")
    gt_ = mxq(f64(gt), 0, "e5m2")
    y = x_.T @ xt_
    u = g_.T @ gt_
    y = y * u
    return y

@@ -1,0 +1,187 @@
+from contextlib import ExitStack
+from functools import partial
+
+import concourse.mybir as mybir
+
+K, L, M, N = 2048, 512, 256, 1536
+FLOPS = 2 * M * N * (K + L)
+
+F32 = mybir.dt.float32
+BF16 = mybir.dt.bfloat16
+U32 = mybir.dt.uint32
+U8 = mybir.dt.uint8
+E4M3X4 = mybir.dt.float8_e4m3fn_x4
+E5M2X4 = mybir.dt.float8_e5m2_x4
+MULT = mybir.AluOpType.mult
+
+P = 128
+PACK = 4
+K_PASS = P * PACK
+PASSES = K // K_PASS
+LAST = PASSES - 1
+BLOCK = 512
+M_TILES = M // P
+
+CHUNKS = [(0, 512, 256), (512, 512, 288), (1024, 256, 0), (1280, 256, 0)]
+
+
+def tile_mix_ghost_none_kernel(tc, x, xt, g, gt, out):
+    nc = tc.nc
+    with ExitStack() as ctx:
+        ctx.enter_context(tc.manual_schedule())
+        raws = ctx.enter_context(tc.tile_pool(name="raws", bufs=1))
+        keep = ctx.enter_context(tc.tile_pool(name="keep", bufs=1))
+        group_pool = ctx.enter_context(tc.tile_pool(name="groups", bufs=4))
+        psum = ctx.enter_context(tc.psum_pool(name="psum", bufs=8))
+
+        def rows(ap, c):
+            return ap[c * K_PASS : (c + 1) * K_PASS, :].rearrange("(p j) n -> p j n", j=PACK)
+
+        g_raw = raws.tile([P, PACK, M], F32, name="g_raw")
+        gt_raw = raws.tile([P, PACK, N], F32, name="gt_raw")
+        x_early = raws.tile([P, LAST, PACK, M], F32, name="x_early")
+        x_last = raws.tile([P, PACK, M], F32, name="x_last")
+        xt_raw = [raws.tile([P, PACK, N], F32, name="xt_raw%d" % c) for c in range(LAST)]
+        chunk_raw = [raws.tile([P, PACK, w], F32, name="chunk_raw%d" % q) for q, (n0, w, v) in enumerate(CHUNKS)]
+        x_raw = [x_early[:, c] for c in range(LAST)] + [x_last[:]]
+
+        nc.sync.dma_start(out=g_raw[:], in_=rows(g, 0))
+        nc.sync.dma_start(out=gt_raw[:], in_=rows(gt, 0))
+        nc.sync.dma_start(
+            out=x_early[:].rearrange("p c j m -> p c (j m)"),
+            in_=x[: LAST * K_PASS, :].rearrange("(c p j) m -> p c (j m)", p=P, j=PACK),
+        )
+        for c in range(LAST):
+            nc.sync.dma_start(out=xt_raw[c][:], in_=rows(xt, c))
+        nc.sync.dma_start(out=x_last[:], in_=rows(x, LAST))
+        for q, (n0, w, v) in enumerate(CHUNKS):
+            nc.sync.dma_start(out=chunk_raw[q][:], in_=rows(xt, LAST)[:, :, n0 : n0 + w])
+
+        g_codes = keep.tile([P, M], U32, align_bytes=256, name="g_codes")
+        g_scales = keep.tile([P, M], U8, align_bytes=256, name="g_scales")
+        gt_codes = keep.tile([P, N], U32, align_bytes=256, name="gt_codes")
+        gt_scales = keep.tile([P, N], U8, align_bytes=256, name="gt_scales")
+        x_codes = keep.tile([P, PASSES, M], U32, align_bytes=256, name="x_codes")
+        x_scales = keep.tile([P, PASSES, M], U8, align_bytes=256, name="x_scales")
+        xt_codes = keep.tile([P, PASSES, N], U32, align_bytes=256, name="xt_codes")
+        xt_scales = keep.tile([P, PASSES, N], U8, align_bytes=256, name="xt_scales")
+        u = keep.tile([P, M_TILES, N], F32, name="u")
+        res = keep.tile([P, M_TILES, N], F32, name="res")
+
+        def round_block(raw, width, split):
+            grouped = group_pool.tile([P, BLOCK, PACK], BF16, align_bytes=256, name="grouped")
+            for copy, lo, hi in ((nc.vector.tensor_copy, 0, split), (nc.scalar.copy, split, width)):
+                if lo < hi:
+                    copy(
+                        out=grouped[:, lo:hi, :].rearrange("p (c i) t -> p c t i", i=4),
+                        in_=raw[:, :, lo:hi].rearrange("p t (c i) -> p c t i", i=4),
+                    )
+            return grouped
+
+        def quantize(grouped, width, codes, scales, fmt):
+            nc.vector.quantize_mx(
+                out=codes.bitcast(fmt),
+                scales=scales,
+                in_=grouped[:, :width, :].rearrange("p w j -> p (w j)"),
+            )
+
+        def product(banks, lhs, rhs, fmt, start, stop):
+            (lhs_codes, lhs_scales), (rhs_codes, rhs_scales) = lhs, rhs
+            for m in range(M_TILES):
+                mc = slice(m * P, (m + 1) * P)
+                nc.tensor.matmul_mx(
+                    out=banks[m],
+                    lhsT=lhs_codes[:, mc].bitcast(fmt),
+                    lhsT_scale=lhs_scales[:, mc],
+                    rhs=rhs_codes.bitcast(fmt),
+                    rhs_scale=rhs_scales,
+                    start=start,
+                    stop=stop,
+                )
+
+        def u_block(cols):
+            banks = [psum.tile([P, BLOCK], F32, name="bank") for m in range(M_TILES)]
+            product([bank[:] for bank in banks], (g_codes[:], g_scales[:]), (gt_codes[:, cols], gt_scales[:, cols]), E5M2X4, True, True)
+            for m in range(M_TILES):
+                nc.scalar.copy(out=u[:, m, cols], in_=banks[m][:])
+
+        acc = []
+
+        def a_chunk(c, q):
+            n0, w, v = CHUNKS[q]
+            cols = slice(n0, n0 + w)
+            if c == 0:
+                acc.append([psum.tile([P, BLOCK], F32, name="bank") for m in range(M_TILES)])
+            product(
+                [bank[:, :w] for bank in acc[q]],
+                (x_codes[:, c, :], x_scales[:, c, :]),
+                (xt_codes[:, c, cols], xt_scales[:, c, cols]),
+                E4M3X4,
+                c == 0,
+                c == LAST,
+            )
+
+        def a_chunks(c, qs):
+            for q in qs:
+                a_chunk(c, q)
+
+        def nothing():
+            return None
+
+        def multiply(q, m):
+            n0, w, v = CHUNKS[q]
+            cols = slice(n0, n0 + w)
+            nc.vector.tensor_tensor(out=res[:, m, cols], in0=acc[q][m][:, :w], in1=u[:, m, cols], op=MULT)
+            nc.sync.dma_start(out=out[m * P : (m + 1) * P, cols], in_=res[:, m, cols])
+
+        def x_block(c):
+            return (x_raw[c], M, 128, x_codes[:, c, :], x_scales[:, c, :], E4M3X4, nothing)
+
+        def xt_blocks(c):
+            found = []
+            for b, qs in enumerate(((0,), (1,), (2, 3))):
+                cols = slice(b * BLOCK, (b + 1) * BLOCK)
+                found.append((xt_raw[c][:, :, cols], BLOCK, 288, xt_codes[:, c, cols], xt_scales[:, c, cols], E4M3X4, partial(a_chunks, c, qs)))
+            return found
+
+        def chunk_block(q):
+            n0, w, v = CHUNKS[q]
+            cols = slice(n0, n0 + w)
+            return (chunk_raw[q][:], w, v, xt_codes[:, LAST, cols], xt_scales[:, LAST, cols], E4M3X4, partial(a_chunk, LAST, q))
+
+        def begin(block):
+            raw, width, split = block[:3]
+            return (round_block(raw, width, split), block)
+
+        def end(begun):
+            grouped, (raw, width, split, codes, scales, fmt, use) = begun
+            quantize(grouped, width, codes, scales, fmt)
+            use()
+
+        def run(blocks):
+            begun = begin(blocks[0])
+            for block in blocks[1:]:
+                following = begin(block)
+                end(begun)
+                begun = following
+            return begun
+
+        first = [(g_raw[:], M, 128, g_codes[:], g_scales[:], E5M2X4, nothing)]
+        for b in range(N // BLOCK):
+            cols = slice(b * BLOCK, (b + 1) * BLOCK)
+            first.append((gt_raw[:, :, cols], BLOCK, 256, gt_codes[:, cols], gt_scales[:, cols], E5M2X4, partial(u_block, cols)))
+        end(run(first))
+        end(run([x_block(c) for c in range(LAST)]))
+        for c in range(LAST - 1):
+            end(run(xt_blocks(c)))
+        begun = run(xt_blocks(LAST - 1) + [x_block(LAST), chunk_block(0)])
+        end(begun)
+        begun = begin(chunk_block(1))
+        multiply(0, 0)
+        for q in range(1, len(CHUNKS)):
+            end(begun)
+            if q + 1 < len(CHUNKS):
+                begun = begin(chunk_block(q + 1))
+            multiply(q - 1, 1)
+            multiply(q, 0)
+        multiply(len(CHUNKS) - 1, 1)

@@ -19,10 +19,20 @@ PACK = 4
 K_PASS = P * PACK
 PASSES = K // K_PASS
 LAST = PASSES - 1
-BLOCK = 512
+WIDE = 512
 M_TILES = M // P
+NARROW = WIDE // M_TILES
 
-CHUNKS = [(0, 512, 256), (512, 512, 288), (1024, 256, 0), (1280, 256, 0)]
+X_EARLY = 3
+CHUNK_WIDTHS = (512, 512, 256, 256)
+BLOCK_W = (256, 256, 256, 256, 256, 256)
+TAIL_SPLIT = (176, 64, 128, 96, 48, 64)
+STORE_AFTER = (0, 1, 2, 3)
+WIDE_SPLIT = 288
+X_SPLIT = 128
+LEAD = 2
+SEPARATE = (4, 5)
+ORDER = [("r", 0), ("p", 0), ("q", 0), ("r", 1), ("q", 1), ("m", 0), ("r", 2), ("r", 3), ("q", 2), ("m", 1), ("q", 3), ("r", 4), ("m", 2), ("q", 4), ("m", 3), ("r", 5), ("a", 4), ("q", 5), ("b", 4), ("a", 5), ("b", 5)]
 
 
 def tile_mix_ghost_none_kernel(tc, x, xt, g, gt, out):
@@ -37,25 +47,25 @@ def tile_mix_ghost_none_kernel(tc, x, xt, g, gt, out):
         def rows(ap, c):
             return ap[c * K_PASS : (c + 1) * K_PASS, :].rearrange("(p j) n -> p j n", j=PACK)
 
+        starts = [sum(BLOCK_W[:b]) for b in range(len(BLOCK_W))]
+        chunk_starts = [sum(CHUNK_WIDTHS[:q]) for q in range(len(CHUNK_WIDTHS))]
+
         g_raw = raws.tile([P, PACK, M], F32, name="g_raw")
         gt_raw = raws.tile([P, PACK, N], F32, name="gt_raw")
-        x_early = raws.tile([P, LAST, PACK, M], F32, name="x_early")
-        x_last = raws.tile([P, PACK, M], F32, name="x_last")
+        x_raw = [raws.tile([P, PACK, M], F32, name="x_raw%d" % c) for c in range(PASSES)]
         xt_raw = [raws.tile([P, PACK, N], F32, name="xt_raw%d" % c) for c in range(LAST)]
-        chunk_raw = [raws.tile([P, PACK, w], F32, name="chunk_raw%d" % q) for q, (n0, w, v) in enumerate(CHUNKS)]
-        x_raw = [x_early[:, c] for c in range(LAST)] + [x_last[:]]
+        chunk_raw = [raws.tile([P, PACK, w], F32, name="chunk_raw%d" % q) for q, w in enumerate(CHUNK_WIDTHS)]
 
         nc.sync.dma_start(out=g_raw[:], in_=rows(g, 0))
         nc.sync.dma_start(out=gt_raw[:], in_=rows(gt, 0))
-        nc.sync.dma_start(
-            out=x_early[:].rearrange("p c j m -> p c (j m)"),
-            in_=x[: LAST * K_PASS, :].rearrange("(c p j) m -> p c (j m)", p=P, j=PACK),
-        )
+        for c in range(X_EARLY):
+            nc.sync.dma_start(out=x_raw[c][:], in_=rows(x, c))
         for c in range(LAST):
             nc.sync.dma_start(out=xt_raw[c][:], in_=rows(xt, c))
-        nc.sync.dma_start(out=x_last[:], in_=rows(x, LAST))
-        for q, (n0, w, v) in enumerate(CHUNKS):
-            nc.sync.dma_start(out=chunk_raw[q][:], in_=rows(xt, LAST)[:, :, n0 : n0 + w])
+        for c in range(X_EARLY, PASSES):
+            nc.sync.dma_start(out=x_raw[c][:], in_=rows(x, c))
+        for q, w in enumerate(CHUNK_WIDTHS):
+            nc.sync.dma_start(out=chunk_raw[q][:], in_=rows(xt, LAST)[:, :, chunk_starts[q] : chunk_starts[q] + w])
 
         g_codes = keep.tile([P, M], U32, align_bytes=256, name="g_codes")
         g_scales = keep.tile([P, M], U8, align_bytes=256, name="g_scales")
@@ -69,7 +79,7 @@ def tile_mix_ghost_none_kernel(tc, x, xt, g, gt, out):
         res = keep.tile([P, M_TILES, N], F32, name="res")
 
         def round_block(raw, width, split):
-            grouped = group_pool.tile([P, BLOCK, PACK], BF16, align_bytes=256, name="grouped")
+            grouped = group_pool.tile([P, WIDE, PACK], BF16, align_bytes=256, name="grouped")
             for copy, lo, hi in ((nc.vector.tensor_copy, 0, split), (nc.scalar.copy, split, width)):
                 if lo < hi:
                     copy(
@@ -85,69 +95,96 @@ def tile_mix_ghost_none_kernel(tc, x, xt, g, gt, out):
                 in_=grouped[:, :width, :].rearrange("p w j -> p (w j)"),
             )
 
-        def product(banks, lhs, rhs, fmt, start, stop):
-            (lhs_codes, lhs_scales), (rhs_codes, rhs_scales) = lhs, rhs
+        def u_block(cols):
+            for m in range(M_TILES):
+                mc = slice(m * P, (m + 1) * P)
+                bank = psum.tile([P, WIDE], F32, name="bank")
+                nc.tensor.matmul_mx(
+                    out=bank[:],
+                    lhsT=g_codes[:, mc].bitcast(E5M2X4),
+                    lhsT_scale=g_scales[:, mc],
+                    rhs=gt_codes[:, cols].bitcast(E5M2X4),
+                    rhs_scale=gt_scales[:, cols],
+                    start=True,
+                    stop=True,
+                )
+                nc.scalar.copy(out=u[:, m, cols], in_=bank[:])
+
+        acc = {}
+
+        def a_block(c, b):
+            w = BLOCK_W[b]
+            cols = slice(starts[b], starts[b] + w)
+            if c == 0:
+                acc[b] = [psum.tile([P, WIDE], F32, name="bank") for m in range(M_TILES if b in SEPARATE else 1)]
             for m in range(M_TILES):
                 mc = slice(m * P, (m + 1) * P)
                 nc.tensor.matmul_mx(
-                    out=banks[m],
-                    lhsT=lhs_codes[:, mc].bitcast(fmt),
-                    lhsT_scale=lhs_scales[:, mc],
-                    rhs=rhs_codes.bitcast(fmt),
-                    rhs_scale=rhs_scales,
-                    start=start,
-                    stop=stop,
+                    out=acc[b][m][:, :w] if b in SEPARATE else acc[b][0][:, m * w : (m + 1) * w],
+                    lhsT=x_codes[:, c, mc].bitcast(E4M3X4),
+                    lhsT_scale=x_scales[:, c, mc],
+                    rhs=xt_codes[:, c, cols].bitcast(E4M3X4),
+                    rhs_scale=xt_scales[:, c, cols],
+                    start=c == 0 and (m == 0 or b in SEPARATE),
+                    stop=c == LAST and (m == M_TILES - 1 or b in SEPARATE),
                 )
 
-        def u_block(cols):
-            banks = [psum.tile([P, BLOCK], F32, name="bank") for m in range(M_TILES)]
-            product([bank[:] for bank in banks], (g_codes[:], g_scales[:]), (gt_codes[:, cols], gt_scales[:, cols]), E5M2X4, True, True)
-            for m in range(M_TILES):
-                nc.scalar.copy(out=u[:, m, cols], in_=banks[m][:])
+        x_done = []
+        xt_done = []
+        next_pass = [0] * len(BLOCK_W)
 
-        acc = []
-
-        def a_chunk(c, q):
-            n0, w, v = CHUNKS[q]
-            cols = slice(n0, n0 + w)
-            if c == 0:
-                acc.append([psum.tile([P, BLOCK], F32, name="bank") for m in range(M_TILES)])
-            product(
-                [bank[:, :w] for bank in acc[q]],
-                (x_codes[:, c, :], x_scales[:, c, :]),
-                (xt_codes[:, c, cols], xt_scales[:, c, cols]),
-                E4M3X4,
-                c == 0,
-                c == LAST,
-            )
-
-        def a_chunks(c, qs):
-            for q in qs:
-                a_chunk(c, q)
+        def advance(done, key):
+            done.append(key)
+            for c in range(PASSES):
+                for b in range(len(BLOCK_W)):
+                    have = any(cc == c and lo <= starts[b] < hi for cc, lo, hi in xt_done)
+                    if next_pass[b] == c and c in x_done and have:
+                        a_block(c, b)
+                        next_pass[b] = c + 1
 
         def nothing():
             return None
 
-        def multiply(q, m):
-            n0, w, v = CHUNKS[q]
-            cols = slice(n0, n0 + w)
-            nc.vector.tensor_tensor(out=res[:, m, cols], in0=acc[q][m][:, :w], in1=u[:, m, cols], op=MULT)
+        stored = [0]
+
+        def multiply(b):
+            w = BLOCK_W[b]
+            cols = slice(starts[b], starts[b] + w)
+            nc.vector.tensor_tensor(
+                out=res[:, :, cols],
+                in0=acc[b][0][:, : M_TILES * w].rearrange("p (m n) -> p m n", m=M_TILES),
+                in1=u[:, :, cols],
+                op=MULT,
+            )
+            if b in STORE_AFTER:
+                done = slice(stored[-1], starts[b] + w)
+                nc.sync.dma_start(out=out[:, done].rearrange("(m p) n -> p m n", p=P), in_=res[:, :, done])
+                stored.append(starts[b] + w)
+
+        def multiply_half(b, m):
+            w = BLOCK_W[b]
+            cols = slice(starts[b], starts[b] + w)
+            nc.vector.tensor_tensor(out=res[:, m, cols], in0=acc[b][m][:, :w], in1=u[:, m, cols], op=MULT)
             nc.sync.dma_start(out=out[m * P : (m + 1) * P, cols], in_=res[:, m, cols])
 
         def x_block(c):
-            return (x_raw[c], M, 128, x_codes[:, c, :], x_scales[:, c, :], E4M3X4, nothing)
+            use = partial(advance, x_done, c)
+            return (x_raw[c][:], M, X_SPLIT, x_codes[:, c, :], x_scales[:, c, :], E4M3X4, use)
 
         def xt_blocks(c):
             found = []
-            for b, qs in enumerate(((0,), (1,), (2, 3))):
-                cols = slice(b * BLOCK, (b + 1) * BLOCK)
-                found.append((xt_raw[c][:, :, cols], BLOCK, 288, xt_codes[:, c, cols], xt_scales[:, c, cols], E4M3X4, partial(a_chunks, c, qs)))
+            for b in range(N // WIDE):
+                cols = slice(b * WIDE, (b + 1) * WIDE)
+                use = partial(advance, xt_done, (c, cols.start, cols.stop))
+                found.append((xt_raw[c][:, :, cols], WIDE, WIDE_SPLIT, xt_codes[:, c, cols], xt_scales[:, c, cols], E4M3X4, use))
             return found
 
-        def chunk_block(q):
-            n0, w, v = CHUNKS[q]
-            cols = slice(n0, n0 + w)
-            return (chunk_raw[q][:], w, v, xt_codes[:, LAST, cols], xt_scales[:, LAST, cols], E4M3X4, partial(a_chunk, LAST, q))
+        def tail_block(b):
+            w = BLOCK_W[b]
+            q = max(i for i in range(len(CHUNK_WIDTHS)) if chunk_starts[i] <= starts[b])
+            o = starts[b] - chunk_starts[q]
+            cols = slice(starts[b], starts[b] + w)
+            return (chunk_raw[q][:, :, o : o + w], w, TAIL_SPLIT[b], xt_codes[:, LAST, cols], xt_scales[:, LAST, cols], E4M3X4, partial(advance, xt_done, (LAST, cols.start, cols.stop)))
 
         def begin(block):
             raw, width, split = block[:3]
@@ -166,22 +203,32 @@ def tile_mix_ghost_none_kernel(tc, x, xt, g, gt, out):
                 begun = following
             return begun
 
-        first = [(g_raw[:], M, 128, g_codes[:], g_scales[:], E5M2X4, nothing)]
-        for b in range(N // BLOCK):
-            cols = slice(b * BLOCK, (b + 1) * BLOCK)
-            first.append((gt_raw[:, :, cols], BLOCK, 256, gt_codes[:, cols], gt_scales[:, cols], E5M2X4, partial(u_block, cols)))
+        first = [(g_raw[:], M, X_SPLIT, g_codes[:], g_scales[:], E5M2X4, nothing)]
+        for b in range(N // WIDE):
+            cols = slice(b * WIDE, (b + 1) * WIDE)
+            first.append((gt_raw[:, :, cols], WIDE, 256, gt_codes[:, cols], gt_scales[:, cols], E5M2X4, partial(u_block, cols)))
         end(run(first))
-        end(run([x_block(c) for c in range(LAST)]))
+        if X_EARLY:
+            end(run([x_block(c) for c in range(X_EARLY)]))
         for c in range(LAST - 1):
             end(run(xt_blocks(c)))
-        begun = run(xt_blocks(LAST - 1) + [x_block(LAST), chunk_block(0)])
-        end(begun)
-        begun = begin(chunk_block(1))
-        multiply(0, 0)
-        for q in range(1, len(CHUNKS)):
-            end(begun)
-            if q + 1 < len(CHUNKS):
-                begun = begin(chunk_block(q + 1))
-            multiply(q - 1, 1)
-            multiply(q, 0)
-        multiply(len(CHUNKS) - 1, 1)
+        late = [x_block(c) for c in range(X_EARLY, PASSES)]
+        third = xt_blocks(LAST - 1)
+        mixed = []
+        for i in range(max(len(third), len(late) + LEAD)):
+            mixed = mixed + third[i : i + 1] + (late[i - LEAD : i - LEAD + 1] if i >= LEAD else [])
+        before = run(mixed)
+        begun = {}
+        for kind, b in ORDER:
+            if kind == "r":
+                begun[b] = begin(tail_block(b))
+            if kind == "p":
+                end(before)
+            if kind == "q":
+                end(begun[b])
+            if kind == "m":
+                multiply(b)
+            if kind == "a":
+                multiply_half(b, 0)
+            if kind == "b":
+                multiply_half(b, 1)

@@ -19,20 +19,20 @@ PACK = 4
 K_PASS = P * PACK
 PASSES = K // K_PASS
 LAST = PASSES - 1
-WIDE = 512
 M_TILES = M // P
-NARROW = WIDE // M_TILES
+BANK = 512
+BANKS = 8
+STRIP = BANK // M_TILES
+STRIPS = N // STRIP
+LINE = 4
+STAGED = 4
 
-X_EARLY = 3
-CHUNK_WIDTHS = (512, 512, 256, 256)
-BLOCK_W = (256, 256, 256, 256, 256, 256)
-TAIL_SPLIT = (176, 64, 128, 96, 48, 64)
-STORE_AFTER = (0, 1, 2, 3)
-WIDE_SPLIT = 288
-X_SPLIT = 128
-LEAD = 2
-SEPARATE = (4, 5)
-ORDER = [("r", 0), ("p", 0), ("q", 0), ("r", 1), ("q", 1), ("m", 0), ("r", 2), ("r", 3), ("q", 2), ("m", 1), ("q", 3), ("r", 4), ("m", 2), ("q", 4), ("m", 3), ("r", 5), ("a", 4), ("q", 5), ("b", 4), ("a", 5), ("b", 5)]
+CHUNK_STRIPS = (2, 2, 1, 1)
+FIRST_SPLIT_STRIP = STRIPS - (BANKS - STRIPS)
+
+SHARE_WHOLE_PASS = 288
+SHARE_SECOND_STRIP = 96
+SHARE_LONE_STRIP = 64
 
 
 def tile_mix_ghost_none_kernel(tc, x, xt, g, gt, out):
@@ -41,31 +41,35 @@ def tile_mix_ghost_none_kernel(tc, x, xt, g, gt, out):
         ctx.enter_context(tc.manual_schedule())
         raws = ctx.enter_context(tc.tile_pool(name="raws", bufs=1))
         keep = ctx.enter_context(tc.tile_pool(name="keep", bufs=1))
-        group_pool = ctx.enter_context(tc.tile_pool(name="groups", bufs=4))
-        psum = ctx.enter_context(tc.psum_pool(name="psum", bufs=8))
+        staging = ctx.enter_context(tc.tile_pool(name="staging", bufs=STAGED))
+        psum = ctx.enter_context(tc.psum_pool(name="psum", bufs=BANKS))
 
         def rows(ap, c):
-            return ap[c * K_PASS : (c + 1) * K_PASS, :].rearrange("(p j) n -> p j n", j=PACK)
+            return ap[c * K_PASS : (c + 1) * K_PASS, :].rearrange("(p t) n -> p t n", t=PACK)
 
-        starts = [sum(BLOCK_W[:b]) for b in range(len(BLOCK_W))]
-        chunk_starts = [sum(CHUNK_WIDTHS[:q]) for q in range(len(CHUNK_WIDTHS))]
+        def strip_cols(first, count=1):
+            return slice(first * STRIP, (first + count) * STRIP)
+
+        chunk_first = [sum(CHUNK_STRIPS[:q]) for q in range(len(CHUNK_STRIPS))]
 
         g_raw = raws.tile([P, PACK, M], F32, name="g_raw")
         gt_raw = raws.tile([P, PACK, N], F32, name="gt_raw")
-        x_raw = [raws.tile([P, PACK, M], F32, name="x_raw%d" % c) for c in range(PASSES)]
+        x_early = raws.tile([P, LAST, PACK, M], F32, name="x_early")
+        x_last = raws.tile([P, PACK, M], F32, name="x_last")
         xt_raw = [raws.tile([P, PACK, N], F32, name="xt_raw%d" % c) for c in range(LAST)]
-        chunk_raw = [raws.tile([P, PACK, w], F32, name="chunk_raw%d" % q) for q, w in enumerate(CHUNK_WIDTHS)]
+        chunk_raw = [raws.tile([P, PACK, n * STRIP], F32, name="chunk_raw%d" % q) for q, n in enumerate(CHUNK_STRIPS)]
 
         nc.sync.dma_start(out=g_raw[:], in_=rows(g, 0))
         nc.sync.dma_start(out=gt_raw[:], in_=rows(gt, 0))
-        for c in range(X_EARLY):
-            nc.sync.dma_start(out=x_raw[c][:], in_=rows(x, c))
+        nc.sync.dma_start(
+            out=x_early[:].rearrange("p c t m -> p c (t m)"),
+            in_=x[: LAST * K_PASS, :].rearrange("(c p t) m -> p c (t m)", p=P, t=PACK),
+        )
         for c in range(LAST):
             nc.sync.dma_start(out=xt_raw[c][:], in_=rows(xt, c))
-        for c in range(X_EARLY, PASSES):
-            nc.sync.dma_start(out=x_raw[c][:], in_=rows(x, c))
-        for q, w in enumerate(CHUNK_WIDTHS):
-            nc.sync.dma_start(out=chunk_raw[q][:], in_=rows(xt, LAST)[:, :, chunk_starts[q] : chunk_starts[q] + w])
+        nc.sync.dma_start(out=x_last[:], in_=rows(x, LAST))
+        for q, n in enumerate(CHUNK_STRIPS):
+            nc.sync.dma_start(out=chunk_raw[q][:], in_=rows(xt, LAST)[:, :, strip_cols(chunk_first[q], n)])
 
         g_codes = keep.tile([P, M], U32, align_bytes=256, name="g_codes")
         g_scales = keep.tile([P, M], U8, align_bytes=256, name="g_scales")
@@ -78,31 +82,39 @@ def tile_mix_ghost_none_kernel(tc, x, xt, g, gt, out):
         u = keep.tile([P, M_TILES, N], F32, name="u")
         res = keep.tile([P, M_TILES, N], F32, name="res")
 
-        def round_block(raw, width, split):
-            grouped = group_pool.tile([P, WIDE, PACK], BF16, align_bytes=256, name="grouped")
-            for copy, lo, hi in ((nc.vector.tensor_copy, 0, split), (nc.scalar.copy, split, width)):
-                if lo < hi:
-                    copy(
-                        out=grouped[:, lo:hi, :].rearrange("p (c i) t -> p c t i", i=4),
-                        in_=raw[:, :, lo:hi].rearrange("p t (c i) -> p c t i", i=4),
-                    )
-            return grouped
+        def round_piece(piece):
+            raw, share = piece[:2]
+            width = raw.shape[2]
+            grouped = staging.tile([P, BANK, PACK], BF16, align_bytes=256, name="grouped")
+            for copy, lo, hi in ((nc.vector.tensor_copy, 0, share), (nc.scalar.copy, share, width)):
+                copy(
+                    out=grouped[:, lo:hi, :].rearrange("p (c i) t -> p c t i", i=LINE),
+                    in_=raw[:, :, lo:hi].rearrange("p t (c i) -> p c t i", i=LINE),
+                )
+            return grouped[:, :width, :].rearrange("p n t -> p (n t)"), piece
 
-        def quantize(grouped, width, codes, scales, fmt):
-            nc.vector.quantize_mx(
-                out=codes.bitcast(fmt),
-                scales=scales,
-                in_=grouped[:, :width, :].rearrange("p w j -> p (w j)"),
-            )
+        def quantize_piece(rounded):
+            grouped, (raw, share, codes, scales, fmt, matmuls) = rounded
+            nc.vector.quantize_mx(out=codes.bitcast(fmt), scales=scales, in_=grouped)
+            for matmul in matmuls:
+                matmul()
 
-        def u_block(cols):
+        def run(pieces):
+            rounded = round_piece(pieces[0])
+            for piece in pieces[1:]:
+                following = round_piece(piece)
+                quantize_piece(rounded)
+                rounded = following
+            return rounded
+
+        def u_columns(cols):
             for m in range(M_TILES):
-                mc = slice(m * P, (m + 1) * P)
-                bank = psum.tile([P, WIDE], F32, name="bank")
+                tile_m = slice(m * P, (m + 1) * P)
+                bank = psum.tile([P, BANK], F32, name="bank")
                 nc.tensor.matmul_mx(
                     out=bank[:],
-                    lhsT=g_codes[:, mc].bitcast(E5M2X4),
-                    lhsT_scale=g_scales[:, mc],
+                    lhsT=g_codes[:, tile_m].bitcast(E5M2X4),
+                    lhsT_scale=g_scales[:, tile_m],
                     rhs=gt_codes[:, cols].bitcast(E5M2X4),
                     rhs_scale=gt_scales[:, cols],
                     start=True,
@@ -110,125 +122,75 @@ def tile_mix_ghost_none_kernel(tc, x, xt, g, gt, out):
                 )
                 nc.scalar.copy(out=u[:, m, cols], in_=bank[:])
 
-        acc = {}
+        strip_banks = []
 
-        def a_block(c, b):
-            w = BLOCK_W[b]
-            cols = slice(starts[b], starts[b] + w)
+        def a_pass(c, s):
+            split = s >= FIRST_SPLIT_STRIP
             if c == 0:
-                acc[b] = [psum.tile([P, WIDE], F32, name="bank") for m in range(M_TILES if b in SEPARATE else 1)]
+                strip_banks.append([psum.tile([P, BANK], F32, name="bank") for m in range(M_TILES if split else 1)])
             for m in range(M_TILES):
-                mc = slice(m * P, (m + 1) * P)
+                tile_m = slice(m * P, (m + 1) * P)
                 nc.tensor.matmul_mx(
-                    out=acc[b][m][:, :w] if b in SEPARATE else acc[b][0][:, m * w : (m + 1) * w],
-                    lhsT=x_codes[:, c, mc].bitcast(E4M3X4),
-                    lhsT_scale=x_scales[:, c, mc],
-                    rhs=xt_codes[:, c, cols].bitcast(E4M3X4),
-                    rhs_scale=xt_scales[:, c, cols],
-                    start=c == 0 and (m == 0 or b in SEPARATE),
-                    stop=c == LAST and (m == M_TILES - 1 or b in SEPARATE),
+                    out=strip_banks[s][m][:, :STRIP] if split else strip_banks[s][0][:, strip_cols(m)],
+                    lhsT=x_codes[:, c, tile_m].bitcast(E4M3X4),
+                    lhsT_scale=x_scales[:, c, tile_m],
+                    rhs=xt_codes[:, c, strip_cols(s)].bitcast(E4M3X4),
+                    rhs_scale=xt_scales[:, c, strip_cols(s)],
+                    start=c == 0 and (split or m == 0),
+                    stop=c == LAST and (split or m == M_TILES - 1),
                 )
 
-        x_done = []
-        xt_done = []
-        next_pass = [0] * len(BLOCK_W)
+        def multiply_and_store(s, bank):
+            tiles = slice(bank, bank + 1) if s >= FIRST_SPLIT_STRIP else slice(0, M_TILES)
+            count = tiles.stop - tiles.start
+            sums = strip_banks[s][bank][:, : count * STRIP].rearrange("p (m n) -> p m n", m=count)
+            cols = strip_cols(s)
+            nc.vector.tensor_tensor(out=res[:, tiles, cols], in0=sums, in1=u[:, tiles, cols], op=MULT)
+            nc.sync.dma_start(out=out.rearrange("(m p) n -> p m n", p=P)[:, tiles, cols], in_=res[:, tiles, cols])
 
-        def advance(done, key):
-            done.append(key)
-            for c in range(PASSES):
-                for b in range(len(BLOCK_W)):
-                    have = any(cc == c and lo <= starts[b] < hi for cc, lo, hi in xt_done)
-                    if next_pass[b] == c and c in x_done and have:
-                        a_block(c, b)
-                        next_pass[b] = c + 1
+        def x_piece(c):
+            raw = x_last[:] if c == LAST else x_early[:, c]
+            return (raw, M // 2, x_codes[:, c, :], x_scales[:, c, :], E4M3X4, [])
 
-        def nothing():
-            return None
+        def xt_pieces(c):
+            pieces = []
+            for s in range(0, STRIPS, M_TILES):
+                cols = strip_cols(s, M_TILES)
+                matmuls = [partial(a_pass, c, s + i) for i in range(M_TILES)]
+                pieces.append((xt_raw[c][:, :, cols], SHARE_WHOLE_PASS, xt_codes[:, c, cols], xt_scales[:, c, cols], E4M3X4, matmuls))
+            return pieces
 
-        stored = [0]
+        def chunk_piece(q, i):
+            s = chunk_first[q] + i
+            share = SHARE_LONE_STRIP if CHUNK_STRIPS[q] == 1 else (STRIP // 2, SHARE_SECOND_STRIP)[i]
+            cols = strip_cols(s)
+            return (chunk_raw[q][:, :, strip_cols(i)], share, xt_codes[:, LAST, cols], xt_scales[:, LAST, cols], E4M3X4, [partial(a_pass, LAST, s)])
 
-        def multiply(b):
-            w = BLOCK_W[b]
-            cols = slice(starts[b], starts[b] + w)
-            nc.vector.tensor_tensor(
-                out=res[:, :, cols],
-                in0=acc[b][0][:, : M_TILES * w].rearrange("p (m n) -> p m n", m=M_TILES),
-                in1=u[:, :, cols],
-                op=MULT,
-            )
-            if b in STORE_AFTER:
-                done = slice(stored[-1], starts[b] + w)
-                nc.sync.dma_start(out=out[:, done].rearrange("(m p) n -> p m n", p=P), in_=res[:, :, done])
-                stored.append(starts[b] + w)
-
-        def multiply_half(b, m):
-            w = BLOCK_W[b]
-            cols = slice(starts[b], starts[b] + w)
-            nc.vector.tensor_tensor(out=res[:, m, cols], in0=acc[b][m][:, :w], in1=u[:, m, cols], op=MULT)
-            nc.sync.dma_start(out=out[m * P : (m + 1) * P, cols], in_=res[:, m, cols])
-
-        def x_block(c):
-            use = partial(advance, x_done, c)
-            return (x_raw[c][:], M, X_SPLIT, x_codes[:, c, :], x_scales[:, c, :], E4M3X4, use)
-
-        def xt_blocks(c):
-            found = []
-            for b in range(N // WIDE):
-                cols = slice(b * WIDE, (b + 1) * WIDE)
-                use = partial(advance, xt_done, (c, cols.start, cols.stop))
-                found.append((xt_raw[c][:, :, cols], WIDE, WIDE_SPLIT, xt_codes[:, c, cols], xt_scales[:, c, cols], E4M3X4, use))
-            return found
-
-        def tail_block(b):
-            w = BLOCK_W[b]
-            q = max(i for i in range(len(CHUNK_WIDTHS)) if chunk_starts[i] <= starts[b])
-            o = starts[b] - chunk_starts[q]
-            cols = slice(starts[b], starts[b] + w)
-            return (chunk_raw[q][:, :, o : o + w], w, TAIL_SPLIT[b], xt_codes[:, LAST, cols], xt_scales[:, LAST, cols], E4M3X4, partial(advance, xt_done, (LAST, cols.start, cols.stop)))
-
-        def begin(block):
-            raw, width, split = block[:3]
-            return (round_block(raw, width, split), block)
-
-        def end(begun):
-            grouped, (raw, width, split, codes, scales, fmt, use) = begun
-            quantize(grouped, width, codes, scales, fmt)
-            use()
-
-        def run(blocks):
-            begun = begin(blocks[0])
-            for block in blocks[1:]:
-                following = begin(block)
-                end(begun)
-                begun = following
-            return begun
-
-        first = [(g_raw[:], M, X_SPLIT, g_codes[:], g_scales[:], E5M2X4, nothing)]
-        for b in range(N // WIDE):
-            cols = slice(b * WIDE, (b + 1) * WIDE)
-            first.append((gt_raw[:, :, cols], WIDE, 256, gt_codes[:, cols], gt_scales[:, cols], E5M2X4, partial(u_block, cols)))
-        end(run(first))
-        if X_EARLY:
-            end(run([x_block(c) for c in range(X_EARLY)]))
+        u_pieces = [(g_raw[:], M // 2, g_codes[:], g_scales[:], E5M2X4, [])]
+        for n0 in range(0, N, BANK):
+            cols = slice(n0, n0 + BANK)
+            u_pieces.append((gt_raw[:, :, cols], BANK // 2, gt_codes[:, cols], gt_scales[:, cols], E5M2X4, [partial(u_columns, cols)]))
+        quantize_piece(run(u_pieces))
+        quantize_piece(run([x_piece(c) for c in range(LAST)]))
         for c in range(LAST - 1):
-            end(run(xt_blocks(c)))
-        late = [x_block(c) for c in range(X_EARLY, PASSES)]
-        third = xt_blocks(LAST - 1)
-        mixed = []
-        for i in range(max(len(third), len(late) + LEAD)):
-            mixed = mixed + third[i : i + 1] + (late[i - LEAD : i - LEAD + 1] if i >= LEAD else [])
-        before = run(mixed)
-        begun = {}
-        for kind, b in ORDER:
-            if kind == "r":
-                begun[b] = begin(tail_block(b))
-            if kind == "p":
-                end(before)
-            if kind == "q":
-                end(begun[b])
-            if kind == "m":
-                multiply(b)
-            if kind == "a":
-                multiply_half(b, 0)
-            if kind == "b":
-                multiply_half(b, 1)
+            quantize_piece(run(xt_pieces(c)))
+
+        waiting = [partial(quantize_piece, run(xt_pieces(LAST - 1) + [x_piece(LAST)]))]
+        for q, count in enumerate(CHUNK_STRIPS):
+            rounded = []
+            for i in range(count):
+                rounded.append(round_piece(chunk_piece(q, i)))
+                if q == 0 and i == 0:
+                    waiting.pop(0)()
+            for i in range(count):
+                if count == 1:
+                    waiting.pop(0)()
+                older = len(waiting)
+                quantize_piece(rounded[i])
+                s = chunk_first[q] + i
+                waiting.extend(partial(multiply_and_store, s, bank) for bank in range(len(strip_banks[s])))
+                narrower_next = i == count - 1 and q + 1 < len(CHUNK_STRIPS) and CHUNK_STRIPS[q + 1] < count
+                if older and not narrower_next:
+                    waiting.pop(0)()
+        for step in waiting:
+            step()

@@ -54,20 +54,17 @@ def tile_mix_ghost_none_kernel(tc, x, xt, g, gt, out):
 
         g_raw = raws.tile([P, PACK, M], F32, name="g_raw")
         gt_raw = raws.tile([P, PACK, N], F32, name="gt_raw")
-        x_early = raws.tile([P, LAST, PACK, M], F32, name="x_early")
-        x_last = raws.tile([P, PACK, M], F32, name="x_last")
+        x_raw = [raws.tile([P, PACK, M], F32, name="x_raw%d" % c) for c in range(PASSES)]
         xt_raw = [raws.tile([P, PACK, N], F32, name="xt_raw%d" % c) for c in range(LAST)]
         chunk_raw = [raws.tile([P, PACK, n * STRIP], F32, name="chunk_raw%d" % q) for q, n in enumerate(CHUNK_STRIPS)]
 
         nc.sync.dma_start(out=g_raw[:], in_=rows(g, 0))
         nc.sync.dma_start(out=gt_raw[:], in_=rows(gt, 0))
-        nc.sync.dma_start(
-            out=x_early[:].rearrange("p c t m -> p c (t m)"),
-            in_=x[: LAST * K_PASS, :].rearrange("(c p t) m -> p c (t m)", p=P, t=PACK),
-        )
+        for c in range(LAST):
+            nc.sync.dma_start(out=x_raw[c][:], in_=rows(x, c))
         for c in range(LAST):
             nc.sync.dma_start(out=xt_raw[c][:], in_=rows(xt, c))
-        nc.sync.dma_start(out=x_last[:], in_=rows(x, LAST))
+        nc.sync.dma_start(out=x_raw[LAST][:], in_=rows(x, LAST))
         for q, n in enumerate(CHUNK_STRIPS):
             nc.sync.dma_start(out=chunk_raw[q][:], in_=rows(xt, LAST)[:, :, strip_cols(chunk_first[q], n)])
 
@@ -149,8 +146,7 @@ def tile_mix_ghost_none_kernel(tc, x, xt, g, gt, out):
             nc.sync.dma_start(out=out.rearrange("(m p) n -> p m n", p=P)[:, tiles, cols], in_=res[:, tiles, cols])
 
         def x_piece(c):
-            raw = x_last[:] if c == LAST else x_early[:, c]
-            return (raw, M // 2, x_codes[:, c, :], x_scales[:, c, :], E4M3X4, [])
+            return (x_raw[c][:], M // 2, x_codes[:, c, :], x_scales[:, c, :], E4M3X4, [])
 
         def xt_pieces(c):
             pieces = []

@@ -32,7 +32,7 @@ FIRST_SPLIT_STRIP = STRIPS - (BANKS - STRIPS)
 
 SHARE_WHOLE_PASS = 288
 SHARE_SECOND_STRIP = 96
-SHARE_LONE_STRIP = 64
+SHARE_LONE_STRIP = 80
 
 
 def tile_mix_ghost_none_kernel(tc, x, xt, g, gt, out):
@@ -79,11 +79,15 @@ def tile_mix_ghost_none_kernel(tc, x, xt, g, gt, out):
         u = keep.tile([P, M_TILES, N], F32, name="u")
         res = keep.tile([P, M_TILES, N], F32, name="res")
 
+        def pool_copy(out, in_):
+            nc.gpsimd.tensor_scalar(out=out, in0=in_, scalar1=1.0, scalar2=0.0, op0=MULT, op1=mybir.AluOpType.add)
+
         def round_piece(piece):
             raw, share = piece[:2]
             width = raw.shape[2]
             grouped = staging.tile([P, BANK, PACK], BF16, align_bytes=256, name="grouped")
-            for copy, lo, hi in ((nc.vector.tensor_copy, 0, share), (nc.scalar.copy, share, width)):
+            helper = pool_copy if share == SHARE_LONE_STRIP else nc.vector.tensor_copy
+            for copy, lo, hi in ((helper, 0, share), (nc.scalar.copy, share, width)):
                 copy(
                     out=grouped[:, lo:hi, :].rearrange("p (c i) t -> p c t i", i=LINE),
                     in_=raw[:, :, lo:hi].rearrange("p t (c i) -> p c t i", i=LINE),
@@ -162,7 +166,7 @@ def tile_mix_ghost_none_kernel(tc, x, xt, g, gt, out):
             cols = strip_cols(s)
             return (chunk_raw[q][:, :, strip_cols(i)], share, xt_codes[:, LAST, cols], xt_scales[:, LAST, cols], E4M3X4, [partial(a_pass, LAST, s)])
 
-        u_pieces = [(g_raw[:], M // 2, g_codes[:], g_scales[:], E5M2X4, [])]
+        u_pieces = [(g_raw[:], SHARE_LONE_STRIP, g_codes[:], g_scales[:], E5M2X4, [])]
         for n0 in range(0, N, BANK):
             cols = slice(n0, n0 + BANK)
             u_pieces.append((gt_raw[:, :, cols], BANK // 2, gt_codes[:, cols], gt_scales[:, cols], E5M2X4, [partial(u_columns, cols)]))

@@ -25,14 +25,15 @@ BANKS = 8
 STRIP = BANK // M_TILES
 STRIPS = N // STRIP
 LINE = 4
-STAGED = 4
+STAGED = 5
 
 CHUNK_STRIPS = (2, 2, 1, 1)
 FIRST_SPLIT_STRIP = STRIPS - (BANKS - STRIPS)
 
 SHARE_WHOLE_PASS = 288
-SHARE_SECOND_STRIP = 96
-SHARE_LONE_STRIP = 80
+SHARE_LAST_X = 160
+SHARE_SECOND_STRIP = 48
+SHARE_LONE_STRIP = 64
 
 
 def tile_mix_ghost_none_kernel(tc, x, xt, g, gt, out):
@@ -150,7 +151,7 @@ def tile_mix_ghost_none_kernel(tc, x, xt, g, gt, out):
             nc.sync.dma_start(out=out.rearrange("(m p) n -> p m n", p=P)[:, tiles, cols], in_=res[:, tiles, cols])
 
         def x_piece(c):
-            return (x_raw[c][:], M // 2, x_codes[:, c, :], x_scales[:, c, :], E4M3X4, [])
+            return (x_raw[c][:], SHARE_LAST_X if c == LAST else M // 2, x_codes[:, c, :], x_scales[:, c, :], E4M3X4, [])
 
         def xt_pieces(c):
             pieces = []
@@ -175,22 +176,21 @@ def tile_mix_ghost_none_kernel(tc, x, xt, g, gt, out):
         for c in range(LAST - 1):
             quantize_piece(run(xt_pieces(c)))
 
-        waiting = [partial(quantize_piece, run(xt_pieces(LAST - 1) + [x_piece(LAST)]))]
+        def finish_strip(s):
+            for bank in range(len(strip_banks[s])):
+                multiply_and_store(s, bank)
+
+        x_last = run(xt_pieces(LAST - 1) + [x_piece(LAST)])
         for q, count in enumerate(CHUNK_STRIPS):
             rounded = []
             for i in range(count):
                 rounded.append(round_piece(chunk_piece(q, i)))
                 if q == 0 and i == 0:
-                    waiting.pop(0)()
+                    quantize_piece(x_last)
             for i in range(count):
-                if count == 1:
-                    waiting.pop(0)()
-                older = len(waiting)
-                quantize_piece(rounded[i])
                 s = chunk_first[q] + i
-                waiting.extend(partial(multiply_and_store, s, bank) for bank in range(len(strip_banks[s])))
-                narrower_next = i == count - 1 and q + 1 < len(CHUNK_STRIPS) and CHUNK_STRIPS[q + 1] < count
-                if older and not narrower_next:
-                    waiting.pop(0)()
-        for step in waiting:
-            step()
+                if s >= 2:
+                    finish_strip(s - 2)
+                quantize_piece(rounded[i])
+        finish_strip(STRIPS - 2)
+        finish_strip(STRIPS - 1)

@@ -25,15 +25,17 @@ BANKS = 8
 STRIP = BANK // M_TILES
 STRIPS = N // STRIP
 LINE = 4
-STAGED = 5
+STAGED = 6
 
 CHUNK_STRIPS = (2, 2, 1, 1)
 FIRST_SPLIT_STRIP = STRIPS - (BANKS - STRIPS)
 
 SHARE_WHOLE_PASS = 288
-SHARE_LAST_X = 160
-SHARE_SECOND_STRIP = 48
-SHARE_LONE_STRIP = 64
+SHARE_X = 112
+SHARE_FIRST_STRIP = 144
+SHARE_SECOND_STRIP = 96
+SHARE_LONE_STRIP = 48
+HELD = 2
 
 
 def tile_mix_ghost_none_kernel(tc, x, xt, g, gt, out):
@@ -61,11 +63,11 @@ def tile_mix_ghost_none_kernel(tc, x, xt, g, gt, out):
 
         nc.sync.dma_start(out=g_raw[:], in_=rows(g, 0))
         nc.sync.dma_start(out=gt_raw[:], in_=rows(gt, 0))
-        for c in range(LAST):
-            nc.sync.dma_start(out=x_raw[c][:], in_=rows(x, c))
+        nc.sync.dma_start(out=x_raw[0][:], in_=rows(x, 0))
         for c in range(LAST):
             nc.sync.dma_start(out=xt_raw[c][:], in_=rows(xt, c))
-        nc.sync.dma_start(out=x_raw[LAST][:], in_=rows(x, LAST))
+        for c in range(1, PASSES):
+            nc.sync.dma_start(out=x_raw[c][:], in_=rows(x, c))
         for q, n in enumerate(CHUNK_STRIPS):
             nc.sync.dma_start(out=chunk_raw[q][:], in_=rows(xt, LAST)[:, :, strip_cols(chunk_first[q], n)])
 
@@ -80,15 +82,11 @@ def tile_mix_ghost_none_kernel(tc, x, xt, g, gt, out):
         u = keep.tile([P, M_TILES, N], F32, name="u")
         res = keep.tile([P, M_TILES, N], F32, name="res")
 
-        def pool_copy(out, in_):
-            nc.gpsimd.tensor_scalar(out=out, in0=in_, scalar1=1.0, scalar2=0.0, op0=MULT, op1=mybir.AluOpType.add)
-
         def round_piece(piece):
             raw, share = piece[:2]
             width = raw.shape[2]
             grouped = staging.tile([P, BANK, PACK], BF16, align_bytes=256, name="grouped")
-            helper = pool_copy if share == SHARE_LONE_STRIP else nc.vector.tensor_copy
-            for copy, lo, hi in ((helper, 0, share), (nc.scalar.copy, share, width)):
+            for copy, lo, hi in ((nc.vector.tensor_copy, 0, share), (nc.scalar.copy, share, width)):
                 copy(
                     out=grouped[:, lo:hi, :].rearrange("p (c i) t -> p c t i", i=LINE),
                     in_=raw[:, :, lo:hi].rearrange("p t (c i) -> p c t i", i=LINE),
@@ -150,29 +148,32 @@ def tile_mix_ghost_none_kernel(tc, x, xt, g, gt, out):
             nc.vector.tensor_tensor(out=res[:, tiles, cols], in0=sums, in1=u[:, tiles, cols], op=MULT)
             nc.sync.dma_start(out=out.rearrange("(m p) n -> p m n", p=P)[:, tiles, cols], in_=res[:, tiles, cols])
 
-        def x_piece(c):
-            return (x_raw[c][:], SHARE_LAST_X if c == LAST else M // 2, x_codes[:, c, :], x_scales[:, c, :], E4M3X4, [])
+        def x_piece(c, strips):
+            return (x_raw[c][:], SHARE_X, x_codes[:, c, :], x_scales[:, c, :], E4M3X4, [partial(a_pass, c, s) for s in strips])
 
         def xt_pieces(c):
             pieces = []
             for s in range(0, STRIPS, M_TILES):
                 cols = strip_cols(s, M_TILES)
-                matmuls = [partial(a_pass, c, s + i) for i in range(M_TILES)]
+                matmuls = [partial(a_pass, c, s + i) for i in range(M_TILES)] if c == 0 else []
                 pieces.append((xt_raw[c][:, :, cols], SHARE_WHOLE_PASS, xt_codes[:, c, cols], xt_scales[:, c, cols], E4M3X4, matmuls))
             return pieces
 
         def chunk_piece(q, i):
             s = chunk_first[q] + i
-            share = SHARE_LONE_STRIP if CHUNK_STRIPS[q] == 1 else (STRIP // 2, SHARE_SECOND_STRIP)[i]
+            if CHUNK_STRIPS[q] > 1:
+                share = (SHARE_FIRST_STRIP, SHARE_SECOND_STRIP)[i]
+            else:
+                share = SHARE_SECOND_STRIP if s == STRIPS - 1 else SHARE_LONE_STRIP
             cols = strip_cols(s)
-            return (chunk_raw[q][:, :, strip_cols(i)], share, xt_codes[:, LAST, cols], xt_scales[:, LAST, cols], E4M3X4, [partial(a_pass, LAST, s)])
+            return (chunk_raw[q][:, :, strip_cols(i)], share, xt_codes[:, LAST, cols], xt_scales[:, LAST, cols], E4M3X4, [partial(a_pass, LAST, s)] + [partial(a_pass, LAST - 1, s + HELD)] * (s + HELD < STRIPS))
 
-        u_pieces = [(g_raw[:], SHARE_LONE_STRIP, g_codes[:], g_scales[:], E5M2X4, [])]
+        u_pieces = [(g_raw[:], SHARE_X, g_codes[:], g_scales[:], E5M2X4, [])]
         for n0 in range(0, N, BANK):
             cols = slice(n0, n0 + BANK)
             u_pieces.append((gt_raw[:, :, cols], BANK // 2, gt_codes[:, cols], gt_scales[:, cols], E5M2X4, [partial(u_columns, cols)]))
         quantize_piece(run(u_pieces))
-        quantize_piece(run([x_piece(c) for c in range(LAST)]))
+        quantize_piece(run([x_piece(0, [])]))
         for c in range(LAST - 1):
             quantize_piece(run(xt_pieces(c)))
 
@@ -180,17 +181,21 @@ def tile_mix_ghost_none_kernel(tc, x, xt, g, gt, out):
             for bank in range(len(strip_banks[s])):
                 multiply_and_store(s, bank)
 
-        x_last = run(xt_pieces(LAST - 1) + [x_piece(LAST)])
+        late_x = [x_piece(1, range(STRIPS)), x_piece(2, range(HELD)), x_piece(LAST, [])]
+        quantize_piece(run([piece for pair in zip(xt_pieces(LAST - 1), late_x) for piece in pair]))
+
+        def round_chunk(q):
+            return [round_piece(chunk_piece(q, i)) for i in range(CHUNK_STRIPS[q])]
+
+        rounded = round_chunk(0)
         for q, count in enumerate(CHUNK_STRIPS):
-            rounded = []
+            narrow_next = q + 1 < len(CHUNK_STRIPS) and CHUNK_STRIPS[q + 1] == 1
             for i in range(count):
-                rounded.append(round_piece(chunk_piece(q, i)))
-                if q == 0 and i == 0:
-                    quantize_piece(x_last)
-            for i in range(count):
-                s = chunk_first[q] + i
-                if s >= 2:
-                    finish_strip(s - 2)
                 quantize_piece(rounded[i])
-        finish_strip(STRIPS - 2)
+                if i == count - 1 and narrow_next:
+                    following = round_chunk(q + 1)
+                if chunk_first[q] + i > 0:
+                    finish_strip(chunk_first[q] + i - 1)
+            if q + 1 < len(CHUNK_STRIPS):
+                rounded = following if narrow_next else round_chunk(q + 1)
         finish_strip(STRIPS - 1)

@@ -55,11 +55,11 @@ def tile_mix_ghost_none_kernel(tc, x, xt, g, gt, out):
 
         chunk_first = [sum(CHUNK_STRIPS[:q]) for q in range(len(CHUNK_STRIPS))]
 
-        g_raw = raws.tile([P, PACK, M], F32, name="g_raw")
-        gt_raw = raws.tile([P, PACK, N], F32, name="gt_raw")
-        x_raw = [raws.tile([P, PACK, M], F32, name="x_raw%d" % c) for c in range(PASSES)]
-        xt_raw = [raws.tile([P, PACK, N], F32, name="xt_raw%d" % c) for c in range(LAST)]
-        chunk_raw = [raws.tile([P, PACK, n * STRIP], F32, name="chunk_raw%d" % q) for q, n in enumerate(CHUNK_STRIPS)]
+        g_raw = raws.tile([P, PACK, M], F32, align_bytes=256, name="g_raw")
+        gt_raw = raws.tile([P, PACK, N], F32, align_bytes=256, name="gt_raw")
+        x_raw = [raws.tile([P, PACK, M], F32, align_bytes=256, name="x_raw%d" % c) for c in range(PASSES)]
+        xt_raw = [raws.tile([P, PACK, N], F32, align_bytes=256, name="xt_raw%d" % c) for c in range(LAST)]
+        chunk_raw = [raws.tile([P, PACK, n * STRIP], F32, align_bytes=256, name="chunk_raw%d" % q) for q, n in enumerate(CHUNK_STRIPS)]
 
         nc.sync.dma_start(out=g_raw[:], in_=rows(g, 0))
         nc.sync.dma_start(out=gt_raw[:], in_=rows(gt, 0))
@@ -79,8 +79,8 @@ def tile_mix_ghost_none_kernel(tc, x, xt, g, gt, out):
         x_scales = keep.tile([P, PASSES, M], U8, align_bytes=256, name="x_scales")
         xt_codes = keep.tile([P, PASSES, N], U32, align_bytes=256, name="xt_codes")
         xt_scales = keep.tile([P, PASSES, N], U8, align_bytes=256, name="xt_scales")
-        u = keep.tile([P, M_TILES, N], F32, name="u")
-        res = keep.tile([P, M_TILES, N], F32, name="res")
+        u = keep.tile([P, M_TILES, N], F32, align_bytes=256, name="u")
+        res = keep.tile([P, M_TILES, N], F32, align_bytes=256, name="res")
 
         def round_piece(piece):
             raw, share = piece[:2]

@@ -25,7 +25,7 @@ BANKS = 8
 STRIP = BANK // M_TILES
 STRIPS = N // STRIP
 LINE = 4
-STAGED = 6
+STAGED = 5
 
 CHUNK_STRIPS = (2, 2, 1, 1)
 FIRST_SPLIT_STRIP = STRIPS - (BANKS - STRIPS)
@@ -55,11 +55,11 @@ def tile_mix_ghost_none_kernel(tc, x, xt, g, gt, out):
 
         chunk_first = [sum(CHUNK_STRIPS[:q]) for q in range(len(CHUNK_STRIPS))]
 
-        g_raw = raws.tile([P, PACK, M], F32, align_bytes=256, name="g_raw")
-        gt_raw = raws.tile([P, PACK, N], F32, align_bytes=256, name="gt_raw")
-        x_raw = [raws.tile([P, PACK, M], F32, align_bytes=256, name="x_raw%d" % c) for c in range(PASSES)]
-        xt_raw = [raws.tile([P, PACK, N], F32, align_bytes=256, name="xt_raw%d" % c) for c in range(LAST)]
-        chunk_raw = [raws.tile([P, PACK, n * STRIP], F32, align_bytes=256, name="chunk_raw%d" % q) for q, n in enumerate(CHUNK_STRIPS)]
+        g_raw = raws.tile([P, PACK, M], F32, align_bytes=512, name="g_raw")
+        gt_raw = raws.tile([P, PACK, N], F32, align_bytes=512, name="gt_raw")
+        x_raw = [raws.tile([P, PACK, M], F32, align_bytes=512, name="x_raw%d" % c) for c in range(PASSES)]
+        xt_raw = [raws.tile([P, PACK, N], F32, align_bytes=512, name="xt_raw%d" % c) for c in range(LAST)]
+        chunk_raw = [raws.tile([P, PACK, n * STRIP], F32, align_bytes=512, name="chunk_raw%d" % q) for q, n in enumerate(CHUNK_STRIPS)]
 
         nc.sync.dma_start(out=g_raw[:], in_=rows(g, 0))
         nc.sync.dma_start(out=gt_raw[:], in_=rows(gt, 0))
@@ -79,8 +79,8 @@ def tile_mix_ghost_none_kernel(tc, x, xt, g, gt, out):
         x_scales = keep.tile([P, PASSES, M], U8, align_bytes=256, name="x_scales")
         xt_codes = keep.tile([P, PASSES, N], U32, align_bytes=256, name="xt_codes")
         xt_scales = keep.tile([P, PASSES, N], U8, align_bytes=256, name="xt_scales")
-        u = keep.tile([P, M_TILES, N], F32, align_bytes=256, name="u")
-        res = keep.tile([P, M_TILES, N], F32, align_bytes=256, name="res")
+        u = keep.tile([P, M_TILES, N], F32, align_bytes=512, name="u")
+        res = keep.tile([P, M_TILES, N], F32, align_bytes=512, name="res")
 
         def round_piece(piece):
             raw, share = piece[:2]

@@ -26,16 +26,17 @@ STRIP = BANK // M_TILES
 STRIPS = N // STRIP
 LINE = 4
 STAGED = 5
+MX_ALIGN = 256
+DMA_ALIGN = 256
 
 CHUNK_STRIPS = (2, 2, 1, 1)
 FIRST_SPLIT_STRIP = STRIPS - (BANKS - STRIPS)
+HELD = 2
 
 SHARE_WHOLE_PASS = 288
-SHARE_X = 112
-SHARE_FIRST_STRIP = 144
-SHARE_SECOND_STRIP = 96
-SHARE_LONE_STRIP = 48
-HELD = 2
+SHARE_NARROW = 112
+SHARE_STRIP = (160, 128, 256, 160, 48, 32)
+HALF = PACK // 2
 
 
 def tile_mix_ghost_none_kernel(tc, x, xt, g, gt, out):
@@ -53,13 +54,21 @@ def tile_mix_ghost_none_kernel(tc, x, xt, g, gt, out):
         def strip_cols(first, count=1):
             return slice(first * STRIP, (first + count) * STRIP)
 
-        chunk_first = [sum(CHUNK_STRIPS[:q]) for q in range(len(CHUNK_STRIPS))]
+        chunks = len(CHUNK_STRIPS)
+        chunk_first = [sum(CHUNK_STRIPS[:q]) for q in range(chunks)]
 
-        g_raw = raws.tile([P, PACK, M], F32, align_bytes=512, name="g_raw")
-        gt_raw = raws.tile([P, PACK, N], F32, align_bytes=512, name="gt_raw")
-        x_raw = [raws.tile([P, PACK, M], F32, align_bytes=512, name="x_raw%d" % c) for c in range(PASSES)]
-        xt_raw = [raws.tile([P, PACK, N], F32, align_bytes=512, name="xt_raw%d" % c) for c in range(LAST)]
-        chunk_raw = [raws.tile([P, PACK, n * STRIP], F32, align_bytes=512, name="chunk_raw%d" % q) for q, n in enumerate(CHUNK_STRIPS)]
+        g_raw = raws.tile([P, PACK, M], F32, align_bytes=DMA_ALIGN, name="g_raw")
+        gt_raw = raws.tile([P, PACK, N], F32, align_bytes=DMA_ALIGN, name="gt_raw")
+        x_raw = [raws.tile([P, PACK, M], F32, align_bytes=DMA_ALIGN, name="x_raw%d" % c) for c in range(PASSES)]
+        xt_raw = [raws.tile([P, PACK, N], F32, align_bytes=DMA_ALIGN, name="xt_raw%d" % c) for c in range(LAST)]
+        chunk_rows = [[slice(0, PACK)]] + [[slice(0, HALF), slice(HALF, PACK)]] * (chunks - 1)
+        chunk_raw = [
+            [
+                raws.tile([P, ts.stop - ts.start, count * STRIP], F32, align_bytes=DMA_ALIGN, name="chunk_raw%d_%d" % (q, ts.start))
+                for ts in chunk_rows[q]
+            ]
+            for q, count in enumerate(CHUNK_STRIPS)
+        ]
 
         nc.sync.dma_start(out=g_raw[:], in_=rows(g, 0))
         nc.sync.dma_start(out=gt_raw[:], in_=rows(gt, 0))
@@ -68,33 +77,38 @@ def tile_mix_ghost_none_kernel(tc, x, xt, g, gt, out):
             nc.sync.dma_start(out=xt_raw[c][:], in_=rows(xt, c))
         for c in range(1, PASSES):
             nc.sync.dma_start(out=x_raw[c][:], in_=rows(x, c))
-        for q, n in enumerate(CHUNK_STRIPS):
-            nc.sync.dma_start(out=chunk_raw[q][:], in_=rows(xt, LAST)[:, :, strip_cols(chunk_first[q], n)])
+        for q, count in enumerate(CHUNK_STRIPS):
+            for ts, raw in zip(chunk_rows[q], chunk_raw[q]):
+                nc.sync.dma_start(out=raw[:], in_=rows(xt, LAST)[:, ts, strip_cols(chunk_first[q], count)])
 
-        g_codes = keep.tile([P, M], U32, align_bytes=256, name="g_codes")
-        g_scales = keep.tile([P, M], U8, align_bytes=256, name="g_scales")
-        gt_codes = keep.tile([P, N], U32, align_bytes=256, name="gt_codes")
-        gt_scales = keep.tile([P, N], U8, align_bytes=256, name="gt_scales")
-        x_codes = keep.tile([P, PASSES, M], U32, align_bytes=256, name="x_codes")
-        x_scales = keep.tile([P, PASSES, M], U8, align_bytes=256, name="x_scales")
-        xt_codes = keep.tile([P, PASSES, N], U32, align_bytes=256, name="xt_codes")
-        xt_scales = keep.tile([P, PASSES, N], U8, align_bytes=256, name="xt_scales")
-        u = keep.tile([P, M_TILES, N], F32, align_bytes=512, name="u")
-        res = keep.tile([P, M_TILES, N], F32, align_bytes=512, name="res")
+        g_codes = keep.tile([P, M], U32, align_bytes=MX_ALIGN, name="g_codes")
+        g_scales = keep.tile([P, M], U8, align_bytes=MX_ALIGN, name="g_scales")
+        gt_codes = keep.tile([P, N], U32, align_bytes=MX_ALIGN, name="gt_codes")
+        gt_scales = keep.tile([P, N], U8, align_bytes=MX_ALIGN, name="gt_scales")
+        x_codes = keep.tile([P, PASSES, M], U32, align_bytes=MX_ALIGN, name="x_codes")
+        x_scales = keep.tile([P, PASSES, M], U8, align_bytes=MX_ALIGN, name="x_scales")
+        xt_codes = keep.tile([P, PASSES, N], U32, align_bytes=MX_ALIGN, name="xt_codes")
+        xt_scales = keep.tile([P, PASSES, N], U8, align_bytes=MX_ALIGN, name="xt_scales")
+        u = keep.tile([P, M_TILES, N], F32, align_bytes=DMA_ALIGN, name="u")
+        res = keep.tile([P, M_TILES, N], F32, align_bytes=DMA_ALIGN, name="res")
+
+        def round_rows(grouped, ts, raw, share):
+            for copy, lo, hi in ((nc.vector.tensor_copy, 0, share), (nc.scalar.copy, share, raw.shape[2])):
+                if hi > lo:
+                    copy(
+                        out=grouped[:, lo:hi, ts].rearrange("p (j i) t -> p j t i", i=LINE),
+                        in_=raw[:, :, lo:hi].rearrange("p t (j i) -> p j t i", i=LINE),
+                    )
 
         def round_piece(piece):
             raw, share = piece[:2]
-            width = raw.shape[2]
-            grouped = staging.tile([P, BANK, PACK], BF16, align_bytes=256, name="grouped")
-            for copy, lo, hi in ((nc.vector.tensor_copy, 0, share), (nc.scalar.copy, share, width)):
-                copy(
-                    out=grouped[:, lo:hi, :].rearrange("p (c i) t -> p c t i", i=LINE),
-                    in_=raw[:, :, lo:hi].rearrange("p t (c i) -> p c t i", i=LINE),
-                )
-            return grouped[:, :width, :].rearrange("p n t -> p (n t)"), piece
+            grouped = staging.tile([P, BANK, PACK], BF16, align_bytes=MX_ALIGN, name="grouped")
+            round_rows(grouped, slice(0, PACK), raw, share)
+            return grouped[:, : raw.shape[2], :].rearrange("p n t -> p (n t)"), piece
 
         def quantize_piece(rounded):
-            grouped, (raw, share, codes, scales, fmt, matmuls) = rounded
+            grouped, piece = rounded
+            codes, scales, fmt, matmuls = piece[2:]
             nc.vector.quantize_mx(out=codes.bitcast(fmt), scales=scales, in_=grouped)
             for matmul in matmuls:
                 matmul()
@@ -105,7 +119,7 @@ def tile_mix_ghost_none_kernel(tc, x, xt, g, gt, out):
                 following = round_piece(piece)
                 quantize_piece(rounded)
                 rounded = following
-            return rounded
+            quantize_piece(rounded)
 
         def u_columns(cols):
             for m in range(M_TILES):
@@ -140,16 +154,18 @@ def tile_mix_ghost_none_kernel(tc, x, xt, g, gt, out):
                     stop=c == LAST and (split or m == M_TILES - 1),
                 )
 
-        def multiply_and_store(s, bank):
-            tiles = slice(bank, bank + 1) if s >= FIRST_SPLIT_STRIP else slice(0, M_TILES)
-            count = tiles.stop - tiles.start
-            sums = strip_banks[s][bank][:, : count * STRIP].rearrange("p (m n) -> p m n", m=count)
+        def finish_strip(s):
             cols = strip_cols(s)
-            nc.vector.tensor_tensor(out=res[:, tiles, cols], in0=sums, in1=u[:, tiles, cols], op=MULT)
-            nc.sync.dma_start(out=out.rearrange("(m p) n -> p m n", p=P)[:, tiles, cols], in_=res[:, tiles, cols])
+            count = M_TILES // len(strip_banks[s])
+            for first, bank in enumerate(strip_banks[s]):
+                tiles = slice(first, first + count)
+                sums = bank[:, : count * STRIP].rearrange("p (m n) -> p m n", m=count)
+                nc.vector.tensor_tensor(out=res[:, tiles, cols], in0=sums, in1=u[:, tiles, cols], op=MULT)
+                nc.sync.dma_start(out=out.rearrange("(m p) n -> p m n", p=P)[:, tiles, cols], in_=res[:, tiles, cols])
 
         def x_piece(c, strips):
-            return (x_raw[c][:], SHARE_X, x_codes[:, c, :], x_scales[:, c, :], E4M3X4, [partial(a_pass, c, s) for s in strips])
+            matmuls = [partial(a_pass, c, s) for s in strips]
+            return (x_raw[c][:], SHARE_NARROW, x_codes[:, c, :], x_scales[:, c, :], E4M3X4, matmuls)
 
         def xt_pieces(c):
             pieces = []
@@ -159,43 +175,45 @@ def tile_mix_ghost_none_kernel(tc, x, xt, g, gt, out):
                 pieces.append((xt_raw[c][:, :, cols], SHARE_WHOLE_PASS, xt_codes[:, c, cols], xt_scales[:, c, cols], E4M3X4, matmuls))
             return pieces
 
-        def chunk_piece(q, i):
-            s = chunk_first[q] + i
-            if CHUNK_STRIPS[q] > 1:
-                share = (SHARE_FIRST_STRIP, SHARE_SECOND_STRIP)[i]
-            else:
-                share = SHARE_SECOND_STRIP if s == STRIPS - 1 else SHARE_LONE_STRIP
-            cols = strip_cols(s)
-            return (chunk_raw[q][:, :, strip_cols(i)], share, xt_codes[:, LAST, cols], xt_scales[:, LAST, cols], E4M3X4, [partial(a_pass, LAST, s)] + [partial(a_pass, LAST - 1, s + HELD)] * (s + HELD < STRIPS))
+        def round_chunk(q):
+            tiles = []
+            for i in range(CHUNK_STRIPS[q]):
+                tiles.append(staging.tile([P, BANK, PACK], BF16, align_bytes=MX_ALIGN, name="grouped"))
+                if len(chunk_rows[q]) > 1:
+                    round_rows(tiles[i], chunk_rows[q][0], chunk_raw[q][0][:, :, strip_cols(i)], 0)
+            rounded = []
+            for i in range(CHUNK_STRIPS[q]):
+                s = chunk_first[q] + i
+                round_rows(tiles[i], chunk_rows[q][-1], chunk_raw[q][-1][:, :, strip_cols(i)], SHARE_STRIP[s])
+                matmuls = [partial(a_pass, LAST, s)]
+                if s + HELD < STRIPS:
+                    matmuls.append(partial(a_pass, LAST - 1, s + HELD))
+                cols = strip_cols(s)
+                piece = (None, None, xt_codes[:, LAST, cols], xt_scales[:, LAST, cols], E4M3X4, matmuls)
+                rounded.append((tiles[i][:, :STRIP, :].rearrange("p n t -> p (n t)"), piece))
+            return rounded
 
-        u_pieces = [(g_raw[:], SHARE_X, g_codes[:], g_scales[:], E5M2X4, [])]
+        u_pieces = [(g_raw[:], SHARE_NARROW, g_codes[:], g_scales[:], E5M2X4, [])]
         for n0 in range(0, N, BANK):
             cols = slice(n0, n0 + BANK)
             u_pieces.append((gt_raw[:, :, cols], BANK // 2, gt_codes[:, cols], gt_scales[:, cols], E5M2X4, [partial(u_columns, cols)]))
-        quantize_piece(run(u_pieces))
-        quantize_piece(run([x_piece(0, [])]))
+        run(u_pieces)
+        run([x_piece(0, [])])
         for c in range(LAST - 1):
-            quantize_piece(run(xt_pieces(c)))
+            run(xt_pieces(c))
 
-        def finish_strip(s):
-            for bank in range(len(strip_banks[s])):
-                multiply_and_store(s, bank)
-
-        late_x = [x_piece(1, range(STRIPS)), x_piece(2, range(HELD)), x_piece(LAST, [])]
-        quantize_piece(run([piece for pair in zip(xt_pieces(LAST - 1), late_x) for piece in pair]))
-
-        def round_chunk(q):
-            return [round_piece(chunk_piece(q, i)) for i in range(CHUNK_STRIPS[q])]
+        late_x = [x_piece(1, range(STRIPS)), x_piece(LAST - 1, range(HELD)), x_piece(LAST, [])]
+        run([piece for pair in zip(xt_pieces(LAST - 1), late_x) for piece in pair])
 
         rounded = round_chunk(0)
         for q, count in enumerate(CHUNK_STRIPS):
-            narrow_next = q + 1 < len(CHUNK_STRIPS) and CHUNK_STRIPS[q + 1] == 1
+            narrow_next = q + 1 < chunks and CHUNK_STRIPS[q + 1] == 1
             for i in range(count):
                 quantize_piece(rounded[i])
                 if i == count - 1 and narrow_next:
                     following = round_chunk(q + 1)
                 if chunk_first[q] + i > 0:
                     finish_strip(chunk_first[q] + i - 1)
-            if q + 1 < len(CHUNK_STRIPS):
+            if q + 1 < chunks:
                 rounded = following if narrow_next else round_chunk(q + 1)
         finish_strip(STRIPS - 1)

@@ -30,13 +30,19 @@ MX_ALIGN = 256
 DMA_ALIGN = 256
 
 CHUNK_STRIPS = (2, 2, 1, 1)
+ALL_ROWS = slice(0, PACK)
+EARLY_ROWS = slice(0, PACK // 2)
+LATE_ROWS = slice(PACK // 2, PACK)
 FIRST_SPLIT_STRIP = STRIPS - (BANKS - STRIPS)
 HELD = 2
 
 SHARE_WHOLE_PASS = 288
 SHARE_NARROW = 112
-SHARE_STRIP = (160, 128, 256, 160, 48, 32)
-HALF = PACK // 2
+SHARE_FIRST_CHUNK = STRIP // 2
+SHARE_WIDE_EARLY = 64
+SHARE_WIDE_LATE = 160
+SHARE_LONE_LATE = 96
+SHARE_LAST_LATE = 48
 
 
 def tile_mix_ghost_none_kernel(tc, x, xt, g, gt, out):
@@ -61,14 +67,12 @@ def tile_mix_ghost_none_kernel(tc, x, xt, g, gt, out):
         gt_raw = raws.tile([P, PACK, N], F32, align_bytes=DMA_ALIGN, name="gt_raw")
         x_raw = [raws.tile([P, PACK, M], F32, align_bytes=DMA_ALIGN, name="x_raw%d" % c) for c in range(PASSES)]
         xt_raw = [raws.tile([P, PACK, N], F32, align_bytes=DMA_ALIGN, name="xt_raw%d" % c) for c in range(LAST)]
-        chunk_rows = [[slice(0, PACK)]] + [[slice(0, HALF), slice(HALF, PACK)]] * (chunks - 1)
-        chunk_raw = [
-            [
-                raws.tile([P, ts.stop - ts.start, count * STRIP], F32, align_bytes=DMA_ALIGN, name="chunk_raw%d_%d" % (q, ts.start))
-                for ts in chunk_rows[q]
-            ]
-            for q, count in enumerate(CHUNK_STRIPS)
-        ]
+        first_raw = raws.tile([P, PACK, CHUNK_STRIPS[0] * STRIP], F32, align_bytes=DMA_ALIGN, name="first_raw")
+        early_raw, late_raw = {}, {}
+        for q in range(1, chunks):
+            shape = [P, PACK // 2, CHUNK_STRIPS[q] * STRIP]
+            early_raw[q] = raws.tile(shape, F32, align_bytes=DMA_ALIGN, name="early_raw%d" % q)
+            late_raw[q] = raws.tile(shape, F32, align_bytes=DMA_ALIGN, name="late_raw%d" % q)
 
         nc.sync.dma_start(out=g_raw[:], in_=rows(g, 0))
         nc.sync.dma_start(out=gt_raw[:], in_=rows(gt, 0))
@@ -77,9 +81,11 @@ def tile_mix_ghost_none_kernel(tc, x, xt, g, gt, out):
             nc.sync.dma_start(out=xt_raw[c][:], in_=rows(xt, c))
         for c in range(1, PASSES):
             nc.sync.dma_start(out=x_raw[c][:], in_=rows(x, c))
-        for q, count in enumerate(CHUNK_STRIPS):
-            for ts, raw in zip(chunk_rows[q], chunk_raw[q]):
-                nc.sync.dma_start(out=raw[:], in_=rows(xt, LAST)[:, ts, strip_cols(chunk_first[q], count)])
+        nc.sync.dma_start(out=first_raw[:], in_=rows(xt, LAST)[:, :, strip_cols(0, CHUNK_STRIPS[0])])
+        for q in range(1, chunks):
+            chunk_cols = strip_cols(chunk_first[q], CHUNK_STRIPS[q])
+            nc.sync.dma_start(out=early_raw[q][:], in_=rows(xt, LAST)[:, EARLY_ROWS, chunk_cols])
+            nc.sync.dma_start(out=late_raw[q][:], in_=rows(xt, LAST)[:, LATE_ROWS, chunk_cols])
 
         g_codes = keep.tile([P, M], U32, align_bytes=MX_ALIGN, name="g_codes")
         g_scales = keep.tile([P, M], U8, align_bytes=MX_ALIGN, name="g_scales")
@@ -92,34 +98,35 @@ def tile_mix_ghost_none_kernel(tc, x, xt, g, gt, out):
         u = keep.tile([P, M_TILES, N], F32, align_bytes=DMA_ALIGN, name="u")
         res = keep.tile([P, M_TILES, N], F32, align_bytes=DMA_ALIGN, name="res")
 
-        def round_rows(grouped, ts, raw, share):
+        def staging_tile():
+            return staging.tile([P, BANK, PACK], BF16, align_bytes=MX_ALIGN, name="grouped")
+
+        def round_rows(grouped, word_rows, raw, share):
             for copy, lo, hi in ((nc.vector.tensor_copy, 0, share), (nc.scalar.copy, share, raw.shape[2])):
                 if hi > lo:
                     copy(
-                        out=grouped[:, lo:hi, ts].rearrange("p (j i) t -> p j t i", i=LINE),
+                        out=grouped[:, lo:hi, word_rows].rearrange("p (j i) t -> p j t i", i=LINE),
                         in_=raw[:, :, lo:hi].rearrange("p t (j i) -> p j t i", i=LINE),
                     )
 
-        def round_piece(piece):
-            raw, share = piece[:2]
-            grouped = staging.tile([P, BANK, PACK], BF16, align_bytes=MX_ALIGN, name="grouped")
-            round_rows(grouped, slice(0, PACK), raw, share)
-            return grouped[:, : raw.shape[2], :].rearrange("p n t -> p (n t)"), piece
-
-        def quantize_piece(rounded):
-            grouped, piece = rounded
-            codes, scales, fmt, matmuls = piece[2:]
-            nc.vector.quantize_mx(out=codes.bitcast(fmt), scales=scales, in_=grouped)
+        def quantize(grouped, codes, scales, fmt, matmuls):
+            width = codes.shape[1]
+            nc.vector.quantize_mx(out=codes.bitcast(fmt), scales=scales, in_=grouped[:, :width, :].rearrange("p n t -> p (n t)"))
             for matmul in matmuls:
                 matmul()
 
+        def round_piece(piece):
+            grouped = staging_tile()
+            round_rows(grouped, ALL_ROWS, *piece[:2])
+            return grouped
+
         def run(pieces):
-            rounded = round_piece(pieces[0])
-            for piece in pieces[1:]:
-                following = round_piece(piece)
-                quantize_piece(rounded)
-                rounded = following
-            quantize_piece(rounded)
+            grouped = round_piece(pieces[0])
+            for piece, following in zip(pieces, pieces[1:]):
+                grouped_next = round_piece(following)
+                quantize(grouped, *piece[2:])
+                grouped = grouped_next
+            quantize(grouped, *pieces[-1][2:])
 
         def u_columns(cols):
             for m in range(M_TILES):
@@ -175,23 +182,21 @@ def tile_mix_ghost_none_kernel(tc, x, xt, g, gt, out):
                 pieces.append((xt_raw[c][:, :, cols], SHARE_WHOLE_PASS, xt_codes[:, c, cols], xt_scales[:, c, cols], E4M3X4, matmuls))
             return pieces
 
-        def round_chunk(q):
-            tiles = []
-            for i in range(CHUNK_STRIPS[q]):
-                tiles.append(staging.tile([P, BANK, PACK], BF16, align_bytes=MX_ALIGN, name="grouped"))
-                if len(chunk_rows[q]) > 1:
-                    round_rows(tiles[i], chunk_rows[q][0], chunk_raw[q][0][:, :, strip_cols(i)], 0)
-            rounded = []
+        strip_staged = []
+
+        def round_chunk(q, word_rows, raw, share):
             for i in range(CHUNK_STRIPS[q]):
                 s = chunk_first[q] + i
-                round_rows(tiles[i], chunk_rows[q][-1], chunk_raw[q][-1][:, :, strip_cols(i)], SHARE_STRIP[s])
-                matmuls = [partial(a_pass, LAST, s)]
-                if s + HELD < STRIPS:
-                    matmuls.append(partial(a_pass, LAST - 1, s + HELD))
-                cols = strip_cols(s)
-                piece = (None, None, xt_codes[:, LAST, cols], xt_scales[:, LAST, cols], E4M3X4, matmuls)
-                rounded.append((tiles[i][:, :STRIP, :].rearrange("p n t -> p (n t)"), piece))
-            return rounded
+                if s == len(strip_staged):
+                    strip_staged.append(staging_tile())
+                round_rows(strip_staged[s], word_rows, raw[:, :, strip_cols(i)], share)
+
+        def quantize_strip(s):
+            matmuls = [partial(a_pass, LAST, s)]
+            if s + HELD < STRIPS:
+                matmuls.append(partial(a_pass, LAST - 1, s + HELD))
+            cols = strip_cols(s)
+            quantize(strip_staged[s], xt_codes[:, LAST, cols], xt_scales[:, LAST, cols], E4M3X4, matmuls)
 
         u_pieces = [(g_raw[:], SHARE_NARROW, g_codes[:], g_scales[:], E5M2X4, [])]
         for n0 in range(0, N, BANK):
@@ -205,15 +210,22 @@ def tile_mix_ghost_none_kernel(tc, x, xt, g, gt, out):
         late_x = [x_piece(1, range(STRIPS)), x_piece(LAST - 1, range(HELD)), x_piece(LAST, [])]
         run([piece for pair in zip(xt_pieces(LAST - 1), late_x) for piece in pair])
 
-        rounded = round_chunk(0)
+        round_chunk(0, ALL_ROWS, first_raw, SHARE_FIRST_CHUNK)
         for q, count in enumerate(CHUNK_STRIPS):
-            narrow_next = q + 1 < chunks and CHUNK_STRIPS[q + 1] == 1
-            for i in range(count):
-                quantize_piece(rounded[i])
-                if i == count - 1 and narrow_next:
-                    following = round_chunk(q + 1)
-                if chunk_first[q] + i > 0:
-                    finish_strip(chunk_first[q] + i - 1)
-            if q + 1 < chunks:
-                rounded = following if narrow_next else round_chunk(q + 1)
+            last_strip = chunk_first[q] + count - 1
+            for s in range(chunk_first[q], last_strip):
+                quantize_strip(s)
+                if s > 0:
+                    finish_strip(s - 1)
+            quantize_strip(last_strip)
+            if q + 1 == chunks:
+                finish_strip(last_strip - 1)
+            elif CHUNK_STRIPS[q + 1] > 1:
+                round_chunk(q + 1, EARLY_ROWS, early_raw[q + 1], SHARE_WIDE_EARLY)
+                finish_strip(last_strip - 1)
+                round_chunk(q + 1, LATE_ROWS, late_raw[q + 1], SHARE_WIDE_LATE)
+            else:
+                round_chunk(q + 1, EARLY_ROWS, early_raw[q + 1], 0)
+                round_chunk(q + 1, LATE_ROWS, late_raw[q + 1], SHARE_LAST_LATE if q + 2 == chunks else SHARE_LONE_LATE)
+                finish_strip(last_strip - 1)
         finish_strip(STRIPS - 1)

@@ -102,11 +102,12 @@ def tile_mix_ghost_none_kernel(tc, x, xt, g, gt, out):
             return staging.tile([P, BANK, PACK], BF16, align_bytes=MX_ALIGN, name="grouped")
 
         def round_rows(grouped, word_rows, raw, share):
-            for copy, lo, hi in ((nc.vector.tensor_copy, 0, share), (nc.scalar.copy, share, raw.shape[2])):
+            scalar_run = LINE if word_rows == ALL_ROWS else 1
+            for copy, lo, hi, run_length in ((nc.vector.tensor_copy, 0, share, LINE), (nc.scalar.copy, share, raw.shape[2], scalar_run)):
                 if hi > lo:
                     copy(
-                        out=grouped[:, lo:hi, word_rows].rearrange("p (j i) t -> p j t i", i=LINE),
-                        in_=raw[:, :, lo:hi].rearrange("p t (j i) -> p j t i", i=LINE),
+                        out=grouped[:, lo:hi, word_rows].rearrange("p (j i) t -> p j t i", i=run_length),
+                        in_=raw[:, :, lo:hi].rearrange("p t (j i) -> p j t i", i=run_length),
                     )
 
         def quantize(grouped, codes, scales, fmt, matmuls):

@@ -34,15 +34,30 @@ ALL_ROWS = slice(0, PACK)
 EARLY_ROWS = slice(0, PACK // 2)
 LATE_ROWS = slice(PACK // 2, PACK)
 FIRST_SPLIT_STRIP = STRIPS - (BANKS - STRIPS)
-HELD = 2
+HELD = 1
+X_EARLY = 0
+HALVED = 0
+SHARE_H_EARLY = 288
+SHARE_H_LATE = 288
+SHARE_LONE_EARLY = 0
+SHARE_LAST_EARLY = 0
+SHARE_X_LATE = 112
+X_AFTER = 1
+SHARE_X_LAST = 160
+BUF = 0
+ORDER = 'Q2 T1 Q3 e4 l4 T2 Q4 e5 l5 T3 Q5 T4 T5'
+HEAD = 'f0 f1 x Q0 X Q1 e2 e3 T0 l2 l3'
+SHARE_F1 = 144
+SHARE_E3 = 128
+SHARE_L3 = 160
 
 SHARE_WHOLE_PASS = 288
 SHARE_NARROW = 112
-SHARE_FIRST_CHUNK = STRIP // 2
-SHARE_WIDE_EARLY = 64
+SHARE_FIRST_CHUNK = 144
+SHARE_WIDE_EARLY = 128
 SHARE_WIDE_LATE = 160
-SHARE_LONE_LATE = 96
-SHARE_LAST_LATE = 48
+SHARE_LONE_LATE = 112
+SHARE_LAST_LATE = 80
 
 
 def tile_mix_ghost_none_kernel(tc, x, xt, g, gt, out):
@@ -66,7 +81,8 @@ def tile_mix_ghost_none_kernel(tc, x, xt, g, gt, out):
         g_raw = raws.tile([P, PACK, M], F32, align_bytes=DMA_ALIGN, name="g_raw")
         gt_raw = raws.tile([P, PACK, N], F32, align_bytes=DMA_ALIGN, name="gt_raw")
         x_raw = [raws.tile([P, PACK, M], F32, align_bytes=DMA_ALIGN, name="x_raw%d" % c) for c in range(PASSES)]
-        xt_raw = [raws.tile([P, PACK, N], F32, align_bytes=DMA_ALIGN, name="xt_raw%d" % c) for c in range(LAST)]
+        xt_raw = [raws.tile([P, PACK, N], F32, align_bytes=DMA_ALIGN, name="xt_raw%d" % c) for c in range(LAST - HALVED)]
+        halved_raw = [raws.tile([P, PACK // 2, N], F32, align_bytes=DMA_ALIGN, name="halved_raw%d" % h) for h in range(2 * HALVED)]
         first_raw = raws.tile([P, PACK, CHUNK_STRIPS[0] * STRIP], F32, align_bytes=DMA_ALIGN, name="first_raw")
         early_raw, late_raw = {}, {}
         for q in range(1, chunks):
@@ -76,12 +92,17 @@ def tile_mix_ghost_none_kernel(tc, x, xt, g, gt, out):
 
         nc.sync.dma_start(out=g_raw[:], in_=rows(g, 0))
         nc.sync.dma_start(out=gt_raw[:], in_=rows(gt, 0))
-        nc.sync.dma_start(out=x_raw[0][:], in_=rows(x, 0))
-        for c in range(LAST):
+        for c in range(X_EARLY):
+            nc.sync.dma_start(out=x_raw[c][:], in_=rows(x, c))
+        for c in range(LAST - HALVED):
             nc.sync.dma_start(out=xt_raw[c][:], in_=rows(xt, c))
-        for c in range(1, PASSES):
+        for raw, word_rows in zip(halved_raw, (EARLY_ROWS, LATE_ROWS)):
+            nc.sync.dma_start(out=raw[:], in_=rows(xt, LAST - 1)[:, word_rows, :])
+        for c in range(X_EARLY, PASSES - X_AFTER):
             nc.sync.dma_start(out=x_raw[c][:], in_=rows(x, c))
         nc.sync.dma_start(out=first_raw[:], in_=rows(xt, LAST)[:, :, strip_cols(0, CHUNK_STRIPS[0])])
+        for c in range(PASSES - X_AFTER, PASSES):
+            nc.sync.dma_start(out=x_raw[c][:], in_=rows(x, c))
         for q in range(1, chunks):
             chunk_cols = strip_cols(chunk_first[q], CHUNK_STRIPS[q])
             nc.sync.dma_start(out=early_raw[q][:], in_=rows(xt, LAST)[:, EARLY_ROWS, chunk_cols])
@@ -173,13 +194,13 @@ def tile_mix_ghost_none_kernel(tc, x, xt, g, gt, out):
 
         def x_piece(c, strips):
             matmuls = [partial(a_pass, c, s) for s in strips]
-            return (x_raw[c][:], SHARE_NARROW, x_codes[:, c, :], x_scales[:, c, :], E4M3X4, matmuls)
+            return (x_raw[c][:], SHARE_NARROW if c < X_EARLY else SHARE_X_LATE, x_codes[:, c, :], x_scales[:, c, :], E4M3X4, matmuls)
 
         def xt_pieces(c):
             pieces = []
             for s in range(0, STRIPS, M_TILES):
                 cols = strip_cols(s, M_TILES)
-                matmuls = [partial(a_pass, c, s + i) for i in range(M_TILES)] if c == 0 else []
+                matmuls = [partial(a_pass, c, s + i) for i in range(M_TILES)] if c < X_EARLY else []
                 pieces.append((xt_raw[c][:, :, cols], SHARE_WHOLE_PASS, xt_codes[:, c, cols], xt_scales[:, c, cols], E4M3X4, matmuls))
             return pieces
 
@@ -204,29 +225,65 @@ def tile_mix_ghost_none_kernel(tc, x, xt, g, gt, out):
             cols = slice(n0, n0 + BANK)
             u_pieces.append((gt_raw[:, :, cols], BANK // 2, gt_codes[:, cols], gt_scales[:, cols], E5M2X4, [partial(u_columns, cols)]))
         run(u_pieces)
-        run([x_piece(0, [])])
+        for c in range(X_EARLY):
+            run([x_piece(c, [])])
         for c in range(LAST - 1):
             run(xt_pieces(c))
 
-        late_x = [x_piece(1, range(STRIPS)), x_piece(LAST - 1, range(HELD)), x_piece(LAST, [])]
-        run([piece for pair in zip(xt_pieces(LAST - 1), late_x) for piece in pair])
+        late_x = [x_piece(c, range(STRIPS) if c < LAST - 1 else range(HELD) if c == LAST - 1 else []) for c in range(X_EARLY, LAST)]
+        if HALVED:
+            staged = [staging_tile() for i in range(3)]
+            for i in range(3):
+                round_rows(staged[i], EARLY_ROWS, halved_raw[0][:, :, strip_cols(2 * i, 2)], SHARE_H_EARLY)
+            prev = None
+            xs = late_x[:]
+            for i in range(3):
+                round_rows(staged[i], LATE_ROWS, halved_raw[1][:, :, strip_cols(2 * i, 2)], SHARE_H_LATE)
+                if i > 0:
+                    quantize(staged[i - 1], xt_codes[:, LAST - 1, strip_cols(2 * i - 2, 2)], xt_scales[:, LAST - 1, strip_cols(2 * i - 2, 2)], E4M3X4, [])
+            grouped = round_piece(xs[0])
+            quantize(staged[2], xt_codes[:, LAST - 1, strip_cols(4, 2)], xt_scales[:, LAST - 1, strip_cols(4, 2)], E4M3X4, [])
+            for piece, following in zip(xs, xs[1:]):
+                grouped_next = round_piece(following)
+                quantize(grouped, *piece[2:])
+                grouped = grouped_next
+            quantize(grouped, *xs[-1][2:])
+        else:
+            whole = xt_pieces(LAST - 1)
+            order = whole[:BUF]
+            for i in range(len(whole)):
+                order.extend(whole[BUF + i : BUF + i + 1] + late_x[i : i + 1])
+            run(order)
 
-        round_chunk(0, ALL_ROWS, first_raw, SHARE_FIRST_CHUNK)
-        for q, count in enumerate(CHUNK_STRIPS):
-            last_strip = chunk_first[q] + count - 1
-            for s in range(chunk_first[q], last_strip):
-                quantize_strip(s)
-                if s > 0:
-                    finish_strip(s - 1)
-            quantize_strip(last_strip)
-            if q + 1 == chunks:
-                finish_strip(last_strip - 1)
-            elif CHUNK_STRIPS[q + 1] > 1:
-                round_chunk(q + 1, EARLY_ROWS, early_raw[q + 1], SHARE_WIDE_EARLY)
-                finish_strip(last_strip - 1)
-                round_chunk(q + 1, LATE_ROWS, late_raw[q + 1], SHARE_WIDE_LATE)
+        staged = {}
+        src = {"f0": (first_raw, 0, ALL_ROWS, SHARE_FIRST_CHUNK), "f1": (first_raw, 1, ALL_ROWS, SHARE_F1),
+               "e2": (early_raw[1], 0, EARLY_ROWS, SHARE_WIDE_EARLY), "e3": (early_raw[1], 1, EARLY_ROWS, SHARE_E3),
+               "l2": (late_raw[1], 0, LATE_ROWS, SHARE_WIDE_LATE), "l3": (late_raw[1], 1, LATE_ROWS, SHARE_L3),
+               "e4": (early_raw[2], 0, EARLY_ROWS, SHARE_LONE_EARLY), "l4": (late_raw[2], 0, LATE_ROWS, SHARE_LONE_LATE),
+               "e5": (early_raw[3], 0, EARLY_ROWS, SHARE_LAST_EARLY), "l5": (late_raw[3], 0, LATE_ROWS, SHARE_LAST_LATE)}
+        done = set()
+        pend = []
+        for tok in (HEAD + " " + ORDER).split():
+            if tok in src:
+                raw, i, word_rows, share = src[tok]
+                s = int(tok[1])
+                if s not in staged:
+                    staged[s] = staging_tile()
+                round_rows(staged[s], word_rows, raw[:, :, strip_cols(i)], share)
+            elif tok == "x":
+                xg = staging_tile()
+                round_rows(xg, ALL_ROWS, x_raw[LAST][:], SHARE_X_LAST)
+            elif tok == "X":
+                quantize(xg, x_codes[:, LAST, :], x_scales[:, LAST, :], E4M3X4, pend)
+                done.add("X")
+            elif tok[0] == "Q":
+                s = int(tok[1])
+                matmuls = [partial(a_pass, LAST, s)]
+                if s + HELD < STRIPS:
+                    matmuls.append(partial(a_pass, LAST - 1, s + HELD))
+                if "X" not in done:
+                    pend.extend(matmuls)
+                    matmuls = []
+                quantize(staged[s], xt_codes[:, LAST, strip_cols(s)], xt_scales[:, LAST, strip_cols(s)], E4M3X4, matmuls)
             else:
-                round_chunk(q + 1, EARLY_ROWS, early_raw[q + 1], 0)
-                round_chunk(q + 1, LATE_ROWS, late_raw[q + 1], SHARE_LAST_LATE if q + 2 == chunks else SHARE_LONE_LATE)
-                finish_strip(last_strip - 1)
-        finish_strip(STRIPS - 1)
+                finish_strip(int(tok[1]))

@@ -29,35 +29,36 @@ STAGED = 5
 MX_ALIGN = 256
 DMA_ALIGN = 256
 
-CHUNK_STRIPS = (2, 2, 1, 1)
+HEAD = 2
+JOINT = 2
 ALL_ROWS = slice(0, PACK)
 EARLY_ROWS = slice(0, PACK // 2)
 LATE_ROWS = slice(PACK // 2, PACK)
 FIRST_SPLIT_STRIP = STRIPS - (BANKS - STRIPS)
 HELD = 1
+JOINED = 2
+HF0 = 6
+HF1 = 3
+HF2 = 2
 X_EARLY = 0
-HALVED = 0
-SHARE_H_EARLY = 288
-SHARE_H_LATE = 288
-SHARE_LONE_EARLY = 0
-SHARE_LAST_EARLY = 0
-SHARE_X_LATE = 112
 X_AFTER = 1
-SHARE_X_LAST = 160
 BUF = 0
-ORDER = 'Q2 T1 Q3 e4 l4 T2 Q4 e5 l5 T3 Q5 T4 T5'
-HEAD = 'f0 f1 x Q0 X Q1 e2 e3 T0 l2 l3'
-SHARE_F1 = 144
-SHARE_E3 = 128
-SHARE_L3 = 160
+HORD = 'f0 x Q0 f1 X e3 Q1'
 
 SHARE_WHOLE_PASS = 288
 SHARE_NARROW = 112
-SHARE_FIRST_CHUNK = 144
-SHARE_WIDE_EARLY = 128
-SHARE_WIDE_LATE = 160
-SHARE_LONE_LATE = 112
-SHARE_LAST_LATE = 80
+SHARE_F0 = 96
+SHARE_F1 = 0
+SHARE_X_LATE = 112
+SHARE_X_LAST = 256
+SHARE_E2 = 0
+SHARE_E3 = 144
+SHARE_L2 = 256
+SHARE_L3 = 0
+SHARE_E4 = 0
+SHARE_L4 = 176
+SHARE_E5 = 0
+SHARE_L5 = 160
 
 
 def tile_mix_ghost_none_kernel(tc, x, xt, g, gt, out):
@@ -75,38 +76,32 @@ def tile_mix_ghost_none_kernel(tc, x, xt, g, gt, out):
         def strip_cols(first, count=1):
             return slice(first * STRIP, (first + count) * STRIP)
 
-        chunks = len(CHUNK_STRIPS)
-        chunk_first = [sum(CHUNK_STRIPS[:q]) for q in range(chunks)]
-
         g_raw = raws.tile([P, PACK, M], F32, align_bytes=DMA_ALIGN, name="g_raw")
         gt_raw = raws.tile([P, PACK, N], F32, align_bytes=DMA_ALIGN, name="gt_raw")
         x_raw = [raws.tile([P, PACK, M], F32, align_bytes=DMA_ALIGN, name="x_raw%d" % c) for c in range(PASSES)]
-        xt_raw = [raws.tile([P, PACK, N], F32, align_bytes=DMA_ALIGN, name="xt_raw%d" % c) for c in range(LAST - HALVED)]
-        halved_raw = [raws.tile([P, PACK // 2, N], F32, align_bytes=DMA_ALIGN, name="halved_raw%d" % h) for h in range(2 * HALVED)]
-        first_raw = raws.tile([P, PACK, CHUNK_STRIPS[0] * STRIP], F32, align_bytes=DMA_ALIGN, name="first_raw")
-        early_raw, late_raw = {}, {}
-        for q in range(1, chunks):
-            shape = [P, PACK // 2, CHUNK_STRIPS[q] * STRIP]
-            early_raw[q] = raws.tile(shape, F32, align_bytes=DMA_ALIGN, name="early_raw%d" % q)
-            late_raw[q] = raws.tile(shape, F32, align_bytes=DMA_ALIGN, name="late_raw%d" % q)
-
+        xt_raw = [raws.tile([P, PACK, N], F32, align_bytes=DMA_ALIGN, name="xt_raw%d" % c) for c in range(LAST)]
+        pieces = [(ALL_ROWS, 0, HEAD), (EARLY_ROWS, HEAD, JOINT)]
+        for s in range(HEAD, STRIPS):
+            if s >= HEAD + JOINT:
+                pieces.append((EARLY_ROWS, s, 1))
+            pieces.append((LATE_ROWS, s, 1))
+        part_raw = [
+            raws.tile([P, word_rows.stop - word_rows.start, count * STRIP], F32, align_bytes=DMA_ALIGN, name="part_raw%d" % h)
+            for h, (word_rows, first, count) in enumerate(pieces)
+        ]
         nc.sync.dma_start(out=g_raw[:], in_=rows(g, 0))
         nc.sync.dma_start(out=gt_raw[:], in_=rows(gt, 0))
         for c in range(X_EARLY):
             nc.sync.dma_start(out=x_raw[c][:], in_=rows(x, c))
-        for c in range(LAST - HALVED):
+        for c in range(LAST):
             nc.sync.dma_start(out=xt_raw[c][:], in_=rows(xt, c))
-        for raw, word_rows in zip(halved_raw, (EARLY_ROWS, LATE_ROWS)):
-            nc.sync.dma_start(out=raw[:], in_=rows(xt, LAST - 1)[:, word_rows, :])
         for c in range(X_EARLY, PASSES - X_AFTER):
             nc.sync.dma_start(out=x_raw[c][:], in_=rows(x, c))
-        nc.sync.dma_start(out=first_raw[:], in_=rows(xt, LAST)[:, :, strip_cols(0, CHUNK_STRIPS[0])])
-        for c in range(PASSES - X_AFTER, PASSES):
-            nc.sync.dma_start(out=x_raw[c][:], in_=rows(x, c))
-        for q in range(1, chunks):
-            chunk_cols = strip_cols(chunk_first[q], CHUNK_STRIPS[q])
-            nc.sync.dma_start(out=early_raw[q][:], in_=rows(xt, LAST)[:, EARLY_ROWS, chunk_cols])
-            nc.sync.dma_start(out=late_raw[q][:], in_=rows(xt, LAST)[:, LATE_ROWS, chunk_cols])
+        for h, (word_rows, first, count) in enumerate(pieces):
+            nc.sync.dma_start(out=part_raw[h][:], in_=rows(xt, LAST)[:, word_rows, strip_cols(first, count)])
+            if h == 0:
+                for c in range(PASSES - X_AFTER, PASSES):
+                    nc.sync.dma_start(out=x_raw[c][:], in_=rows(x, c))
 
         g_codes = keep.tile([P, M], U32, align_bytes=MX_ALIGN, name="g_codes")
         g_scales = keep.tile([P, M], U8, align_bytes=MX_ALIGN, name="g_scales")
@@ -165,12 +160,12 @@ def tile_mix_ghost_none_kernel(tc, x, xt, g, gt, out):
                 )
                 nc.scalar.copy(out=u[:, m, cols], in_=bank[:])
 
-        strip_banks = []
+        strip_banks = {}
 
         def a_pass(c, s):
             split = s >= FIRST_SPLIT_STRIP
             if c == 0:
-                strip_banks.append([psum.tile([P, BANK], F32, name="bank") for m in range(M_TILES if split else 1)])
+                strip_banks[s] = [psum.tile([P, BANK], F32, name="bank") for m in range(M_TILES if split else 1)]
             for m in range(M_TILES):
                 tile_m = slice(m * P, (m + 1) * P)
                 nc.tensor.matmul_mx(
@@ -190,7 +185,9 @@ def tile_mix_ghost_none_kernel(tc, x, xt, g, gt, out):
                 tiles = slice(first, first + count)
                 sums = bank[:, : count * STRIP].rearrange("p (m n) -> p m n", m=count)
                 nc.vector.tensor_tensor(out=res[:, tiles, cols], in0=sums, in1=u[:, tiles, cols], op=MULT)
-                nc.sync.dma_start(out=out.rearrange("(m p) n -> p m n", p=P)[:, tiles, cols], in_=res[:, tiles, cols])
+                stored = cols if s >= JOINED else strip_cols(0, JOINED)
+                if s >= JOINED - 1:
+                    nc.sync.dma_start(out=out.rearrange("(m p) n -> p m n", p=P)[:, tiles, stored], in_=res[:, tiles, stored])
 
         def x_piece(c, strips):
             matmuls = [partial(a_pass, c, s) for s in strips]
@@ -204,19 +201,23 @@ def tile_mix_ghost_none_kernel(tc, x, xt, g, gt, out):
                 pieces.append((xt_raw[c][:, :, cols], SHARE_WHOLE_PASS, xt_codes[:, c, cols], xt_scales[:, c, cols], E4M3X4, matmuls))
             return pieces
 
-        strip_staged = []
+        strip_staged = {}
+        prompt = [STRIPS if c < X_EARLY else (HF0, HF1, HF2)[c] for c in range(LAST)]
 
-        def round_chunk(q, word_rows, raw, share):
-            for i in range(CHUNK_STRIPS[q]):
-                s = chunk_first[q] + i
-                if s == len(strip_staged):
-                    strip_staged.append(staging_tile())
-                round_rows(strip_staged[s], word_rows, raw[:, :, strip_cols(i)], share)
+        def round_part(word_rows, s, share):
+            if s not in strip_staged:
+                strip_staged[s] = staging_tile()
+            for raw, (loaded_rows, first, count) in zip(part_raw, pieces):
+                if loaded_rows == word_rows and first <= s < first + count:
+                    round_rows(strip_staged[s], word_rows, raw[:, :, strip_cols(s - first)], share)
 
-        def quantize_strip(s):
+        def strip_matmuls(s):
             matmuls = [partial(a_pass, LAST, s)]
             if s + HELD < STRIPS:
-                matmuls.append(partial(a_pass, LAST - 1, s + HELD))
+                matmuls.extend(partial(a_pass, c, s + HELD) for c in range(LAST) if s + HELD >= max(prompt[c], HELD))
+            return matmuls
+
+        def quantize_strip(s, matmuls):
             cols = strip_cols(s)
             quantize(strip_staged[s], xt_codes[:, LAST, cols], xt_scales[:, LAST, cols], E4M3X4, matmuls)
 
@@ -230,60 +231,41 @@ def tile_mix_ghost_none_kernel(tc, x, xt, g, gt, out):
         for c in range(LAST - 1):
             run(xt_pieces(c))
 
-        late_x = [x_piece(c, range(STRIPS) if c < LAST - 1 else range(HELD) if c == LAST - 1 else []) for c in range(X_EARLY, LAST)]
-        if HALVED:
-            staged = [staging_tile() for i in range(3)]
-            for i in range(3):
-                round_rows(staged[i], EARLY_ROWS, halved_raw[0][:, :, strip_cols(2 * i, 2)], SHARE_H_EARLY)
-            prev = None
-            xs = late_x[:]
-            for i in range(3):
-                round_rows(staged[i], LATE_ROWS, halved_raw[1][:, :, strip_cols(2 * i, 2)], SHARE_H_LATE)
-                if i > 0:
-                    quantize(staged[i - 1], xt_codes[:, LAST - 1, strip_cols(2 * i - 2, 2)], xt_scales[:, LAST - 1, strip_cols(2 * i - 2, 2)], E4M3X4, [])
-            grouped = round_piece(xs[0])
-            quantize(staged[2], xt_codes[:, LAST - 1, strip_cols(4, 2)], xt_scales[:, LAST - 1, strip_cols(4, 2)], E4M3X4, [])
-            for piece, following in zip(xs, xs[1:]):
-                grouped_next = round_piece(following)
-                quantize(grouped, *piece[2:])
-                grouped = grouped_next
-            quantize(grouped, *xs[-1][2:])
-        else:
-            whole = xt_pieces(LAST - 1)
-            order = whole[:BUF]
-            for i in range(len(whole)):
-                order.extend(whole[BUF + i : BUF + i + 1] + late_x[i : i + 1])
-            run(order)
+        late_x = [x_piece(c, range(max(prompt[c], HELD))) for c in range(X_EARLY, LAST)]
+        whole = xt_pieces(LAST - 1)
+        order = whole[:BUF]
+        for i in range(len(whole)):
+            order.extend(whole[BUF + i : BUF + i + 1] + late_x[i : i + 1])
+        run(order)
 
-        staged = {}
-        src = {"f0": (first_raw, 0, ALL_ROWS, SHARE_FIRST_CHUNK), "f1": (first_raw, 1, ALL_ROWS, SHARE_F1),
-               "e2": (early_raw[1], 0, EARLY_ROWS, SHARE_WIDE_EARLY), "e3": (early_raw[1], 1, EARLY_ROWS, SHARE_E3),
-               "l2": (late_raw[1], 0, LATE_ROWS, SHARE_WIDE_LATE), "l3": (late_raw[1], 1, LATE_ROWS, SHARE_L3),
-               "e4": (early_raw[2], 0, EARLY_ROWS, SHARE_LONE_EARLY), "l4": (late_raw[2], 0, LATE_ROWS, SHARE_LONE_LATE),
-               "e5": (early_raw[3], 0, EARLY_ROWS, SHARE_LAST_EARLY), "l5": (late_raw[3], 0, LATE_ROWS, SHARE_LAST_LATE)}
-        done = set()
         pend = []
-        for tok in (HEAD + " " + ORDER).split():
-            if tok in src:
-                raw, i, word_rows, share = src[tok]
-                s = int(tok[1])
-                if s not in staged:
-                    staged[s] = staging_tile()
-                round_rows(staged[s], word_rows, raw[:, :, strip_cols(i)], share)
+        waiting = True
+        early = {2: SHARE_E2, 3: SHARE_E3, 4: SHARE_E4, 5: SHARE_E5}
+        late = {2: SHARE_L2, 3: SHARE_L3, 4: SHARE_L4, 5: SHARE_L5}
+        seen = set()
+        for tok in HORD.split():
+            if tok[0] == "f":
+                round_part(ALL_ROWS, int(tok[1]), SHARE_F0 if tok == "f0" else SHARE_F1)
             elif tok == "x":
                 xg = staging_tile()
                 round_rows(xg, ALL_ROWS, x_raw[LAST][:], SHARE_X_LAST)
             elif tok == "X":
                 quantize(xg, x_codes[:, LAST, :], x_scales[:, LAST, :], E4M3X4, pend)
-                done.add("X")
-            elif tok[0] == "Q":
-                s = int(tok[1])
-                matmuls = [partial(a_pass, LAST, s)]
-                if s + HELD < STRIPS:
-                    matmuls.append(partial(a_pass, LAST - 1, s + HELD))
-                if "X" not in done:
-                    pend.extend(matmuls)
-                    matmuls = []
-                quantize(staged[s], xt_codes[:, LAST, strip_cols(s)], xt_scales[:, LAST, strip_cols(s)], E4M3X4, matmuls)
+                waiting = False
+            elif tok[0] == "e":
+                for s in range(2, int(tok[1]) + 1):
+                    round_part(EARLY_ROWS, s, early[s])
+                    seen.add(s)
             else:
-                finish_strip(int(tok[1]))
+                s = int(tok[1])
+                if waiting:
+                    pend.extend(strip_matmuls(s))
+                quantize_strip(s, [] if waiting else strip_matmuls(s))
+        for s in range(HEAD, STRIPS):
+            if s not in seen:
+                round_part(EARLY_ROWS, s, early[s])
+            round_part(LATE_ROWS, s, late[s])
+            finish_strip(s - 2)
+            quantize_strip(s, strip_matmuls(s))
+        finish_strip(STRIPS - 2)
+        finish_strip(STRIPS - 1)

@@ -49,7 +49,7 @@ SHARE_WHOLE_PASS = 288
 SHARE_NARROW = 112
 SHARE_F0 = 96
 SHARE_F1 = 0
-SHARE_X_LATE = 112
+SHARE_X_LATE = 160
 SHARE_X_LAST = 256
 SHARE_E2 = 0
 SHARE_E3 = 144

@@ -29,36 +29,18 @@ STAGED = 5
 MX_ALIGN = 256
 DMA_ALIGN = 256
 
-HEAD = 2
-JOINT = 2
 ALL_ROWS = slice(0, PACK)
 EARLY_ROWS = slice(0, PACK // 2)
 LATE_ROWS = slice(PACK // 2, PACK)
+HEAD = range(0, 2)
+PAIR = range(2, 4)
+LONE = range(4, STRIPS)
 FIRST_SPLIT_STRIP = STRIPS - (BANKS - STRIPS)
-HELD = 1
-JOINED = 2
-HF0 = 6
-HF1 = 3
-HF2 = 2
-X_EARLY = 0
-X_AFTER = 1
-BUF = 0
-HORD = 'f0 x Q0 f1 X e3 Q1'
 
 SHARE_WHOLE_PASS = 288
-SHARE_NARROW = 112
-SHARE_F0 = 96
-SHARE_F1 = 0
-SHARE_X_LATE = 160
-SHARE_X_LAST = 256
-SHARE_E2 = 0
-SHARE_E3 = 144
-SHARE_L2 = 256
-SHARE_L3 = 0
-SHARE_E4 = 0
-SHARE_L4 = 176
-SHARE_E5 = 0
-SHARE_L5 = 160
+SHARE_NARROW = 160
+SHARE_FIRST_STRIP = 96
+SHARE_HALF = 176
 
 
 def tile_mix_ghost_none_kernel(tc, x, xt, g, gt, out):
@@ -76,32 +58,33 @@ def tile_mix_ghost_none_kernel(tc, x, xt, g, gt, out):
         def strip_cols(first, count=1):
             return slice(first * STRIP, (first + count) * STRIP)
 
+        parts = [(ALL_ROWS, HEAD), (EARLY_ROWS, PAIR)]
+        parts.extend((LATE_ROWS, range(s, s + 1)) for s in PAIR)
+        parts.extend((word_rows, range(s, s + 1)) for s in LONE for word_rows in (EARLY_ROWS, LATE_ROWS))
+
         g_raw = raws.tile([P, PACK, M], F32, align_bytes=DMA_ALIGN, name="g_raw")
         gt_raw = raws.tile([P, PACK, N], F32, align_bytes=DMA_ALIGN, name="gt_raw")
         x_raw = [raws.tile([P, PACK, M], F32, align_bytes=DMA_ALIGN, name="x_raw%d" % c) for c in range(PASSES)]
         xt_raw = [raws.tile([P, PACK, N], F32, align_bytes=DMA_ALIGN, name="xt_raw%d" % c) for c in range(LAST)]
-        pieces = [(ALL_ROWS, 0, HEAD), (EARLY_ROWS, HEAD, JOINT)]
-        for s in range(HEAD, STRIPS):
-            if s >= HEAD + JOINT:
-                pieces.append((EARLY_ROWS, s, 1))
-            pieces.append((LATE_ROWS, s, 1))
         part_raw = [
-            raws.tile([P, word_rows.stop - word_rows.start, count * STRIP], F32, align_bytes=DMA_ALIGN, name="part_raw%d" % h)
-            for h, (word_rows, first, count) in enumerate(pieces)
+            raws.tile([P, word_rows.stop - word_rows.start, len(strips) * STRIP], F32, align_bytes=DMA_ALIGN, name="part_raw%d" % q)
+            for q, (word_rows, strips) in enumerate(parts)
         ]
+
+        def load_part(q):
+            word_rows, strips = parts[q]
+            nc.sync.dma_start(out=part_raw[q][:], in_=rows(xt, LAST)[:, word_rows, strip_cols(strips.start, len(strips))])
+
         nc.sync.dma_start(out=g_raw[:], in_=rows(g, 0))
         nc.sync.dma_start(out=gt_raw[:], in_=rows(gt, 0))
-        for c in range(X_EARLY):
-            nc.sync.dma_start(out=x_raw[c][:], in_=rows(x, c))
         for c in range(LAST):
             nc.sync.dma_start(out=xt_raw[c][:], in_=rows(xt, c))
-        for c in range(X_EARLY, PASSES - X_AFTER):
+        for c in range(LAST):
             nc.sync.dma_start(out=x_raw[c][:], in_=rows(x, c))
-        for h, (word_rows, first, count) in enumerate(pieces):
-            nc.sync.dma_start(out=part_raw[h][:], in_=rows(xt, LAST)[:, word_rows, strip_cols(first, count)])
-            if h == 0:
-                for c in range(PASSES - X_AFTER, PASSES):
-                    nc.sync.dma_start(out=x_raw[c][:], in_=rows(x, c))
+        load_part(0)
+        nc.sync.dma_start(out=x_raw[LAST][:], in_=rows(x, LAST))
+        for q in range(1, len(parts)):
+            load_part(q)
 
         g_codes = keep.tile([P, M], U32, align_bytes=MX_ALIGN, name="g_codes")
         g_scales = keep.tile([P, M], U8, align_bytes=MX_ALIGN, name="g_scales")
@@ -160,12 +143,12 @@ def tile_mix_ghost_none_kernel(tc, x, xt, g, gt, out):
                 )
                 nc.scalar.copy(out=u[:, m, cols], in_=bank[:])
 
-        strip_banks = {}
+        strip_banks = []
 
         def a_pass(c, s):
             split = s >= FIRST_SPLIT_STRIP
             if c == 0:
-                strip_banks[s] = [psum.tile([P, BANK], F32, name="bank") for m in range(M_TILES if split else 1)]
+                strip_banks.append([psum.tile([P, BANK], F32, name="bank") for m in range(M_TILES if split else 1)])
             for m in range(M_TILES):
                 tile_m = slice(m * P, (m + 1) * P)
                 nc.tensor.matmul_mx(
@@ -178,44 +161,38 @@ def tile_mix_ghost_none_kernel(tc, x, xt, g, gt, out):
                     stop=c == LAST and (split or m == M_TILES - 1),
                 )
 
+        def closing_matmuls(s):
+            matmuls = [partial(a_pass, LAST, s)]
+            if s + 1 in PAIR or s + 1 in LONE:
+                matmuls.extend(partial(a_pass, c, s + 1) for c in range(1, LAST))
+            return matmuls
+
         def finish_strip(s):
             cols = strip_cols(s)
+            stored = strip_cols(HEAD.start, len(HEAD)) if s in HEAD else cols
             count = M_TILES // len(strip_banks[s])
             for first, bank in enumerate(strip_banks[s]):
                 tiles = slice(first, first + count)
                 sums = bank[:, : count * STRIP].rearrange("p (m n) -> p m n", m=count)
                 nc.vector.tensor_tensor(out=res[:, tiles, cols], in0=sums, in1=u[:, tiles, cols], op=MULT)
-                stored = cols if s >= JOINED else strip_cols(0, JOINED)
-                if s >= JOINED - 1:
+                if stored.stop == cols.stop:
                     nc.sync.dma_start(out=out.rearrange("(m p) n -> p m n", p=P)[:, tiles, stored], in_=res[:, tiles, stored])
 
-        def x_piece(c, strips):
-            matmuls = [partial(a_pass, c, s) for s in strips]
-            return (x_raw[c][:], SHARE_NARROW if c < X_EARLY else SHARE_X_LATE, x_codes[:, c, :], x_scales[:, c, :], E4M3X4, matmuls)
+        def x_piece(c, share, matmuls):
+            return (x_raw[c][:], share, x_codes[:, c, :], x_scales[:, c, :], E4M3X4, matmuls)
 
         def xt_pieces(c):
-            pieces = []
-            for s in range(0, STRIPS, M_TILES):
-                cols = strip_cols(s, M_TILES)
-                matmuls = [partial(a_pass, c, s + i) for i in range(M_TILES)] if c < X_EARLY else []
-                pieces.append((xt_raw[c][:, :, cols], SHARE_WHOLE_PASS, xt_codes[:, c, cols], xt_scales[:, c, cols], E4M3X4, matmuls))
-            return pieces
+            columns = [slice(n0, n0 + BANK) for n0 in range(0, N, BANK)]
+            return [(xt_raw[c][:, :, cols], SHARE_WHOLE_PASS, xt_codes[:, c, cols], xt_scales[:, c, cols], E4M3X4, []) for cols in columns]
 
-        strip_staged = {}
-        prompt = [STRIPS if c < X_EARLY else (HF0, HF1, HF2)[c] for c in range(LAST)]
+        strip_staged = []
 
         def round_part(word_rows, s, share):
-            if s not in strip_staged:
-                strip_staged[s] = staging_tile()
-            for raw, (loaded_rows, first, count) in zip(part_raw, pieces):
-                if loaded_rows == word_rows and first <= s < first + count:
-                    round_rows(strip_staged[s], word_rows, raw[:, :, strip_cols(s - first)], share)
-
-        def strip_matmuls(s):
-            matmuls = [partial(a_pass, LAST, s)]
-            if s + HELD < STRIPS:
-                matmuls.extend(partial(a_pass, c, s + HELD) for c in range(LAST) if s + HELD >= max(prompt[c], HELD))
-            return matmuls
+            if s == len(strip_staged):
+                strip_staged.append(staging_tile())
+            for raw, (part_rows, strips) in zip(part_raw, parts):
+                if part_rows == word_rows and s in strips:
+                    round_rows(strip_staged[s], word_rows, raw[:, :, strip_cols(s - strips.start)], share)
 
         def quantize_strip(s, matmuls):
             cols = strip_cols(s)
@@ -226,46 +203,28 @@ def tile_mix_ghost_none_kernel(tc, x, xt, g, gt, out):
             cols = slice(n0, n0 + BANK)
             u_pieces.append((gt_raw[:, :, cols], BANK // 2, gt_codes[:, cols], gt_scales[:, cols], E5M2X4, [partial(u_columns, cols)]))
         run(u_pieces)
-        for c in range(X_EARLY):
-            run([x_piece(c, [])])
         for c in range(LAST - 1):
             run(xt_pieces(c))
 
-        late_x = [x_piece(c, range(max(prompt[c], HELD))) for c in range(X_EARLY, LAST)]
-        whole = xt_pieces(LAST - 1)
-        order = whole[:BUF]
-        for i in range(len(whole)):
-            order.extend(whole[BUF + i : BUF + i + 1] + late_x[i : i + 1])
-        run(order)
+        x_pieces = [x_piece(c, SHARE_NARROW, [partial(a_pass, c, s) for s in (range(STRIPS) if c == 0 else HEAD)]) for c in range(LAST)]
+        run([piece for pair in zip(xt_pieces(LAST - 1), x_pieces) for piece in pair])
 
-        pend = []
-        waiting = True
-        early = {2: SHARE_E2, 3: SHARE_E3, 4: SHARE_E4, 5: SHARE_E5}
-        late = {2: SHARE_L2, 3: SHARE_L3, 4: SHARE_L4, 5: SHARE_L5}
-        seen = set()
-        for tok in HORD.split():
-            if tok[0] == "f":
-                round_part(ALL_ROWS, int(tok[1]), SHARE_F0 if tok == "f0" else SHARE_F1)
-            elif tok == "x":
-                xg = staging_tile()
-                round_rows(xg, ALL_ROWS, x_raw[LAST][:], SHARE_X_LAST)
-            elif tok == "X":
-                quantize(xg, x_codes[:, LAST, :], x_scales[:, LAST, :], E4M3X4, pend)
-                waiting = False
-            elif tok[0] == "e":
-                for s in range(2, int(tok[1]) + 1):
-                    round_part(EARLY_ROWS, s, early[s])
-                    seen.add(s)
-            else:
-                s = int(tok[1])
-                if waiting:
-                    pend.extend(strip_matmuls(s))
-                quantize_strip(s, [] if waiting else strip_matmuls(s))
-        for s in range(HEAD, STRIPS):
-            if s not in seen:
-                round_part(EARLY_ROWS, s, early[s])
-            round_part(LATE_ROWS, s, late[s])
+        last_x = x_piece(LAST, M, closing_matmuls(0))
+        round_part(ALL_ROWS, 0, SHARE_FIRST_STRIP)
+        last_x_staged = round_piece(last_x)
+        quantize_strip(0, [])
+        round_part(ALL_ROWS, 1, 0)
+        quantize(last_x_staged, *last_x[2:])
+        round_part(EARLY_ROWS, PAIR[0], 0)
+        round_part(EARLY_ROWS, PAIR[1], SHARE_HALF)
+        quantize_strip(1, closing_matmuls(1))
+
+        late_share = {PAIR[0]: STRIP, PAIR[1]: 0}
+        for s in range(HEAD.stop, STRIPS):
+            if s in LONE:
+                round_part(EARLY_ROWS, s, 0)
+            round_part(LATE_ROWS, s, late_share.get(s, SHARE_HALF))
             finish_strip(s - 2)
-            quantize_strip(s, strip_matmuls(s))
+            quantize_strip(s, closing_matmuls(s))
         finish_strip(STRIPS - 2)
         finish_strip(STRIPS - 1)

@@ -41,10 +41,15 @@ SHARE_WHOLE_PASS = 288
 SHARE_NARROW = 160
 SHARE_FIRST_STRIP = 96
 SHARE_HALF = 176
+H0 = 96
+X3 = 256
+E3 = 144
+L4 = 160
 
 
 def tile_mix_ghost_none_kernel(tc, x, xt, g, gt, out):
     nc = tc.nc
+    vector_copy, scalar_copy = nc.vector.tensor_copy, nc.scalar.copy
     with ExitStack() as ctx:
         ctx.enter_context(tc.manual_schedule())
         raws = ctx.enter_context(tc.tile_pool(name="raws", bufs=1))
@@ -63,17 +68,20 @@ def tile_mix_ghost_none_kernel(tc, x, xt, g, gt, out):
         parts.extend((word_rows, range(s, s + 1)) for s in LONE for word_rows in (EARLY_ROWS, LATE_ROWS))
 
         g_raw = raws.tile([P, PACK, M], F32, align_bytes=DMA_ALIGN, name="g_raw")
-        gt_raw = raws.tile([P, PACK, N], F32, align_bytes=DMA_ALIGN, name="gt_raw")
+        gt_raw = raws.tile([P, PACK, N], F32, align_bytes=DMA_ALIGN, name="gt_raw", tag="gt_then_res")
         x_raw = [raws.tile([P, PACK, M], F32, align_bytes=DMA_ALIGN, name="x_raw%d" % c) for c in range(PASSES)]
         xt_raw = [raws.tile([P, PACK, N], F32, align_bytes=DMA_ALIGN, name="xt_raw%d" % c) for c in range(LAST)]
+        lone_raw = {s: raws.tile([P, PACK, STRIP], F32, align_bytes=DMA_ALIGN, name="lone_raw%d" % s) for s in LONE}
         part_raw = [
-            raws.tile([P, word_rows.stop - word_rows.start, len(strips) * STRIP], F32, align_bytes=DMA_ALIGN, name="part_raw%d" % q)
+            lone_raw[strips.start][:, word_rows, :]
+            if strips.start in LONE
+            else raws.tile([P, word_rows.stop - word_rows.start, len(strips) * STRIP], F32, align_bytes=DMA_ALIGN, name="part_raw%d" % q)[:]
             for q, (word_rows, strips) in enumerate(parts)
         ]
 
         def load_part(q):
             word_rows, strips = parts[q]
-            nc.sync.dma_start(out=part_raw[q][:], in_=rows(xt, LAST)[:, word_rows, strip_cols(strips.start, len(strips))])
+            nc.sync.dma_start(out=part_raw[q], in_=rows(xt, LAST)[:, word_rows, strip_cols(strips.start, len(strips))])
 
         nc.sync.dma_start(out=g_raw[:], in_=rows(g, 0))
         nc.sync.dma_start(out=gt_raw[:], in_=rows(gt, 0))
@@ -95,19 +103,21 @@ def tile_mix_ghost_none_kernel(tc, x, xt, g, gt, out):
         xt_codes = keep.tile([P, PASSES, N], U32, align_bytes=MX_ALIGN, name="xt_codes")
         xt_scales = keep.tile([P, PASSES, N], U8, align_bytes=MX_ALIGN, name="xt_scales")
         u = keep.tile([P, M_TILES, N], F32, align_bytes=DMA_ALIGN, name="u")
-        res = keep.tile([P, M_TILES, N], F32, align_bytes=DMA_ALIGN, name="res")
 
         def staging_tile():
             return staging.tile([P, BANK, PACK], BF16, align_bytes=MX_ALIGN, name="grouped")
 
+        def round_columns(copy, grouped, word_rows, raw, lo, hi):
+            run_length = LINE if word_rows == ALL_ROWS or copy is vector_copy else 1
+            if hi > lo:
+                copy(
+                    out=grouped[:, lo:hi, word_rows].rearrange("p (j i) t -> p j t i", i=run_length),
+                    in_=raw[:, :, lo:hi].rearrange("p t (j i) -> p j t i", i=run_length),
+                )
+
         def round_rows(grouped, word_rows, raw, share):
-            scalar_run = LINE if word_rows == ALL_ROWS else 1
-            for copy, lo, hi, run_length in ((nc.vector.tensor_copy, 0, share, LINE), (nc.scalar.copy, share, raw.shape[2], scalar_run)):
-                if hi > lo:
-                    copy(
-                        out=grouped[:, lo:hi, word_rows].rearrange("p (j i) t -> p j t i", i=run_length),
-                        in_=raw[:, :, lo:hi].rearrange("p t (j i) -> p j t i", i=run_length),
-                    )
+            round_columns(vector_copy, grouped, word_rows, raw, 0, share)
+            round_columns(scalar_copy, grouped, word_rows, raw, share, raw.shape[2])
 
         def quantize(grouped, codes, scales, fmt, matmuls):
             width = codes.shape[1]
@@ -117,7 +127,7 @@ def tile_mix_ghost_none_kernel(tc, x, xt, g, gt, out):
 
         def round_piece(piece):
             grouped = staging_tile()
-            round_rows(grouped, ALL_ROWS, *piece[:2])
+            round_rows(grouped, ALL_ROWS, piece[0], *piece[1])
             return grouped
 
         def run(pieces):
@@ -145,10 +155,30 @@ def tile_mix_ghost_none_kernel(tc, x, xt, g, gt, out):
 
         strip_banks = []
 
+        def half_cols(h):
+            return slice(N - STRIP + h * P, N - STRIP + (h + 1) * P)
+
+        def half_pass(c, h):
+            for m in range(M_TILES):
+                tile_m = slice(m * P, (m + 1) * P)
+                nc.tensor.matmul_mx(
+                    out=strip_banks[STRIPS - 1][h][:, tile_m],
+                    lhsT=x_codes[:, c, tile_m].bitcast(E4M3X4),
+                    lhsT_scale=x_scales[:, c, tile_m],
+                    rhs=xt_codes[:, c, half_cols(h)].bitcast(E4M3X4),
+                    rhs_scale=xt_scales[:, c, half_cols(h)],
+                    start=c == 0 and m == 0,
+                    stop=c == LAST and m == M_TILES - 1,
+                )
+
         def a_pass(c, s):
             split = s >= FIRST_SPLIT_STRIP
             if c == 0:
                 strip_banks.append([psum.tile([P, BANK], F32, name="bank") for m in range(M_TILES if split else 1)])
+            if s == STRIPS - 1:
+                for h in range(2):
+                    half_pass(c, h)
+                return
             for m in range(M_TILES):
                 tile_m = slice(m * P, (m + 1) * P)
                 nc.tensor.matmul_mx(
@@ -163,33 +193,32 @@ def tile_mix_ghost_none_kernel(tc, x, xt, g, gt, out):
 
         def closing_matmuls(s):
             matmuls = [partial(a_pass, LAST, s)]
-            if s + 1 in PAIR or s + 1 in LONE:
-                matmuls.extend(partial(a_pass, c, s + 1) for c in range(1, LAST))
+            if 0 < s < STRIPS - 2:
+                matmuls.extend(partial(a_pass, c, s + 2) for c in range(1, LAST))
             return matmuls
 
-        def finish_strip(s):
+        def multiply(s, tiles):
             cols = strip_cols(s)
-            stored = strip_cols(HEAD.start, len(HEAD)) if s in HEAD else cols
-            count = M_TILES // len(strip_banks[s])
-            for first, bank in enumerate(strip_banks[s]):
-                tiles = slice(first, first + count)
-                sums = bank[:, : count * STRIP].rearrange("p (m n) -> p m n", m=count)
-                nc.vector.tensor_tensor(out=res[:, tiles, cols], in0=sums, in1=u[:, tiles, cols], op=MULT)
-                if stored.stop == cols.stop:
-                    nc.sync.dma_start(out=out.rearrange("(m p) n -> p m n", p=P)[:, tiles, stored], in_=res[:, tiles, stored])
+            count = tiles.stop - tiles.start
+            if len(strip_banks[s]) > 1:
+                sums = strip_banks[s][tiles.start][:, :STRIP].rearrange("p (m n) -> p m n", m=1)
+            else:
+                sums = strip_banks[s][0][:, tiles.start * STRIP : tiles.stop * STRIP].rearrange("p (m n) -> p m n", m=count)
+            nc.vector.tensor_tensor(out=res[:, tiles, cols], in0=sums, in1=u[:, tiles, cols], op=MULT)
+
+        def store(cols, tiles):
+            nc.sync.dma_start(out=out.rearrange("(m p) n -> p m n", p=P)[:, tiles, cols], in_=res[:, tiles, cols])
 
         def x_piece(c, share, matmuls):
-            return (x_raw[c][:], share, x_codes[:, c, :], x_scales[:, c, :], E4M3X4, matmuls)
+            return (x_raw[c][:], (share,), x_codes[:, c, :], x_scales[:, c, :], E4M3X4, matmuls)
 
         def xt_pieces(c):
             columns = [slice(n0, n0 + BANK) for n0 in range(0, N, BANK)]
-            return [(xt_raw[c][:, :, cols], SHARE_WHOLE_PASS, xt_codes[:, c, cols], xt_scales[:, c, cols], E4M3X4, []) for cols in columns]
+            return [(xt_raw[c][:, :, cols], (SHARE_WHOLE_PASS,), xt_codes[:, c, cols], xt_scales[:, c, cols], E4M3X4, []) for cols in columns]
 
-        strip_staged = []
+        strip_staged = [keep.tile([P, STRIP, PACK], BF16, align_bytes=MX_ALIGN, name="strip_staged%d" % s) for s in range(STRIPS)]
 
         def round_part(word_rows, s, share):
-            if s == len(strip_staged):
-                strip_staged.append(staging_tile())
             for raw, (part_rows, strips) in zip(part_raw, parts):
                 if part_rows == word_rows and s in strips:
                     round_rows(strip_staged[s], word_rows, raw[:, :, strip_cols(s - strips.start)], share)
@@ -198,33 +227,65 @@ def tile_mix_ghost_none_kernel(tc, x, xt, g, gt, out):
             cols = strip_cols(s)
             quantize(strip_staged[s], xt_codes[:, LAST, cols], xt_scales[:, LAST, cols], E4M3X4, matmuls)
 
-        u_pieces = [(g_raw[:], SHARE_NARROW, g_codes[:], g_scales[:], E5M2X4, [])]
+        u_pieces = [(g_raw[:], (SHARE_NARROW,), g_codes[:], g_scales[:], E5M2X4, [])]
         for n0 in range(0, N, BANK):
             cols = slice(n0, n0 + BANK)
-            u_pieces.append((gt_raw[:, :, cols], BANK // 2, gt_codes[:, cols], gt_scales[:, cols], E5M2X4, [partial(u_columns, cols)]))
+            u_pieces.append((gt_raw[:, :, cols], (BANK // 2,), gt_codes[:, cols], gt_scales[:, cols], E5M2X4, [partial(u_columns, cols)]))
         run(u_pieces)
+        res = raws.tile([P, M_TILES, N], F32, align_bytes=DMA_ALIGN, name="res", tag="gt_then_res")
         for c in range(LAST - 1):
             run(xt_pieces(c))
 
-        x_pieces = [x_piece(c, SHARE_NARROW, [partial(a_pass, c, s) for s in (range(STRIPS) if c == 0 else HEAD)]) for c in range(LAST)]
+        x_pieces = [x_piece(c, SHARE_NARROW, [partial(a_pass, c, s) for s in (range(STRIPS) if c == 0 else range(PAIR.start + 1))]) for c in range(LAST)]
         run([piece for pair in zip(xt_pieces(LAST - 1), x_pieces) for piece in pair])
 
-        last_x = x_piece(LAST, M, closing_matmuls(0))
-        round_part(ALL_ROWS, 0, SHARE_FIRST_STRIP)
+        both, top, bottom = slice(0, 2), slice(0, 1), slice(1, 2)
+
+        def quantize_half(h):
+            cols = half_cols(h)
+            quantize(strip_staged[-1][:, h * P :, :], xt_codes[:, LAST, cols], xt_scales[:, LAST, cols], E4M3X4, [partial(half_pass, LAST, h)])
+
+        def finish_half(h):
+            cols = half_cols(h)
+            sums = strip_banks[-1][h][:, :STRIP].rearrange("p (m n) -> p m n", m=M_TILES)
+            nc.vector.tensor_tensor(out=res[:, :, cols], in0=sums, in1=u[:, :, cols], op=MULT)
+            store(cols, both)
+
+        def round_lone(s, early, late):
+            raw = lone_raw[s]
+            round_columns(scalar_copy, strip_staged[s], EARLY_ROWS, raw[:, EARLY_ROWS, :], 0, early)
+            round_columns(vector_copy, strip_staged[s], LATE_ROWS, raw[:, LATE_ROWS, :], 0, late)
+            round_columns(scalar_copy, strip_staged[s], LATE_ROWS, raw[:, LATE_ROWS, :], late, early)
+            round_columns(scalar_copy, strip_staged[s], ALL_ROWS, raw[:], early, STRIP)
+
+        last_x = x_piece(LAST, X3, closing_matmuls(0))
+        round_part(ALL_ROWS, 0, H0)
         last_x_staged = round_piece(last_x)
         quantize_strip(0, [])
         round_part(ALL_ROWS, 1, 0)
         quantize(last_x_staged, *last_x[2:])
-        round_part(EARLY_ROWS, PAIR[0], 0)
-        round_part(EARLY_ROWS, PAIR[1], SHARE_HALF)
+        round_part(EARLY_ROWS, 2, 0)
+        round_part(EARLY_ROWS, 3, E3)
         quantize_strip(1, closing_matmuls(1))
-
-        late_share = {PAIR[0]: STRIP, PAIR[1]: 0}
-        for s in range(HEAD.stop, STRIPS):
-            if s in LONE:
-                round_part(EARLY_ROWS, s, 0)
-            round_part(LATE_ROWS, s, late_share.get(s, SHARE_HALF))
-            finish_strip(s - 2)
-            quantize_strip(s, closing_matmuls(s))
-        finish_strip(STRIPS - 2)
-        finish_strip(STRIPS - 1)
+        round_part(LATE_ROWS, 2, STRIP)
+        multiply(0, both)
+        quantize_strip(2, closing_matmuls(2))
+        round_part(LATE_ROWS, 3, 0)
+        multiply(1, both)
+        store(strip_cols(0, 2), both)
+        quantize_strip(3, closing_matmuls(3))
+        round_lone(4, L4, L4)
+        multiply(2, both)
+        store(strip_cols(2), both)
+        quantize_strip(4, closing_matmuls(4))
+        multiply(3, top)
+        round_lone(5, STRIP, P)
+        multiply(3, bottom)
+        store(strip_cols(3), both)
+        quantize_half(0)
+        quantize_half(1)
+        for tiles in (top, bottom):
+            multiply(4, tiles)
+            store(strip_cols(4), tiles)
+        finish_half(0)
+        finish_half(1)

@@ -38,13 +38,13 @@ LONE = range(4, STRIPS)
 FIRST_SPLIT_STRIP = STRIPS - (BANKS - STRIPS)
 
 SHARE_WHOLE_PASS = 288
-SHARE_NARROW = 160
+SHARE_NARROW = 128
 SHARE_FIRST_STRIP = 96
 SHARE_HALF = 176
-H0 = 96
+H0 = 112
 X3 = 256
 E3 = 144
-L4 = 160
+L4 = 128
 
 
 def tile_mix_ghost_none_kernel(tc, x, xt, g, gt, out):
@@ -153,7 +153,7 @@ def tile_mix_ghost_none_kernel(tc, x, xt, g, gt, out):
                 )
                 nc.scalar.copy(out=u[:, m, cols], in_=bank[:])
 
-        strip_banks = []
+        strip_banks = {}
 
         def half_cols(h):
             return slice(N - STRIP + h * P, N - STRIP + (h + 1) * P)
@@ -171,10 +171,31 @@ def tile_mix_ghost_none_kernel(tc, x, xt, g, gt, out):
                     stop=c == LAST and m == M_TILES - 1,
                 )
 
+        def head_pass(c):
+            cols = strip_cols(HEAD.start, len(HEAD))
+            for m in range(M_TILES):
+                tile_m = slice(m * P, (m + 1) * P)
+                nc.tensor.matmul_mx(
+                    out=strip_banks[HEAD.start][m][:],
+                    lhsT=x_codes[:, c, tile_m].bitcast(E4M3X4),
+                    lhsT_scale=x_scales[:, c, tile_m],
+                    rhs=xt_codes[:, c, cols].bitcast(E4M3X4),
+                    rhs_scale=xt_scales[:, c, cols],
+                    start=c == 0,
+                    stop=c == LAST,
+                )
+
+        def multiply_head(m):
+            cols = strip_cols(HEAD.start, len(HEAD))
+            nc.vector.tensor_tensor(out=res[:, m, cols], in0=strip_banks[HEAD.start][m][:], in1=u[:, m, cols], op=MULT)
+
         def a_pass(c, s):
-            split = s >= FIRST_SPLIT_STRIP
+            split = s >= FIRST_SPLIT_STRIP or s in HEAD
             if c == 0:
-                strip_banks.append([psum.tile([P, BANK], F32, name="bank") for m in range(M_TILES if split else 1)])
+                strip_banks[s] = ([psum.tile([P, BANK], F32, name="bank") for m in range(M_TILES if split else 1)])
+            if s in HEAD:
+                head_pass(c)
+                return
             if s == STRIPS - 1:
                 for h in range(2):
                     half_pass(c, h)
@@ -192,9 +213,9 @@ def tile_mix_ghost_none_kernel(tc, x, xt, g, gt, out):
                 )
 
         def closing_matmuls(s):
-            matmuls = [partial(a_pass, LAST, s)]
-            if 0 < s < STRIPS - 2:
-                matmuls.extend(partial(a_pass, c, s + 2) for c in range(1, LAST))
+            matmuls = [partial(a_pass, LAST, HEAD.start if s in HEAD else s)]
+            if 0 < s < STRIPS - 1:
+                matmuls.extend(partial(a_pass, c, s + 1) for c in range(1, LAST))
             return matmuls
 
         def multiply(s, tiles):
@@ -236,7 +257,7 @@ def tile_mix_ghost_none_kernel(tc, x, xt, g, gt, out):
         for c in range(LAST - 1):
             run(xt_pieces(c))
 
-        x_pieces = [x_piece(c, SHARE_NARROW, [partial(a_pass, c, s) for s in (range(STRIPS) if c == 0 else range(PAIR.start + 1))]) for c in range(LAST)]
+        x_pieces = [x_piece(c, SHARE_NARROW, [partial(a_pass, c, s) for s in (range(STRIPS) if c == 0 else HEAD) if s != 1]) for c in range(LAST)]
         run([piece for pair in zip(xt_pieces(LAST - 1), x_pieces) for piece in pair])
 
         both, top, bottom = slice(0, 2), slice(0, 1), slice(1, 2)
@@ -247,7 +268,7 @@ def tile_mix_ghost_none_kernel(tc, x, xt, g, gt, out):
 
         def finish_half(h):
             cols = half_cols(h)
-            sums = strip_banks[-1][h][:, :STRIP].rearrange("p (m n) -> p m n", m=M_TILES)
+            sums = strip_banks[STRIPS - 1][h][:, :STRIP].rearrange("p (m n) -> p m n", m=M_TILES)
             nc.vector.tensor_tensor(out=res[:, :, cols], in0=sums, in1=u[:, :, cols], op=MULT)
             store(cols, both)
 
@@ -258,20 +279,20 @@ def tile_mix_ghost_none_kernel(tc, x, xt, g, gt, out):
             round_columns(scalar_copy, strip_staged[s], LATE_ROWS, raw[:, LATE_ROWS, :], late, early)
             round_columns(scalar_copy, strip_staged[s], ALL_ROWS, raw[:], early, STRIP)
 
-        last_x = x_piece(LAST, X3, closing_matmuls(0))
+        last_x = x_piece(LAST, X3, [])
         round_part(ALL_ROWS, 0, H0)
         last_x_staged = round_piece(last_x)
         quantize_strip(0, [])
         round_part(ALL_ROWS, 1, 0)
         quantize(last_x_staged, *last_x[2:])
+        quantize_strip(1, closing_matmuls(1))
         round_part(EARLY_ROWS, 2, 0)
         round_part(EARLY_ROWS, 3, E3)
-        quantize_strip(1, closing_matmuls(1))
         round_part(LATE_ROWS, 2, STRIP)
-        multiply(0, both)
+        multiply_head(0)
         quantize_strip(2, closing_matmuls(2))
         round_part(LATE_ROWS, 3, 0)
-        multiply(1, both)
+        multiply_head(1)
         store(strip_cols(0, 2), both)
         quantize_strip(3, closing_matmuls(3))
         round_lone(4, L4, L4)

@@ -23,7 +23,6 @@ M_TILES = M // P
 BANK = 512
 BANKS = 8
 STRIP = BANK // M_TILES
-STRIPS = N // STRIP
 LINE = 4
 STAGED = 5
 MX_ALIGN = 256
@@ -32,24 +31,39 @@ DMA_ALIGN = 256
 ALL_ROWS = slice(0, PACK)
 EARLY_ROWS = slice(0, PACK // 2)
 LATE_ROWS = slice(PACK // 2, PACK)
-HEAD = range(0, 2)
-PAIR = range(2, 4)
-LONE = range(4, STRIPS)
-FIRST_SPLIT_STRIP = STRIPS - (BANKS - STRIPS)
+BOTH_TILES = slice(0, M_TILES)
+TOP, BOTTOM = slice(0, 1), slice(1, 2)
+
+HEAD = slice(0, BANK)
+FIRST = slice(BANK, BANK + STRIP)
+SECOND = slice(BANK + STRIP, BANK + 2 * STRIP)
+THIRD = slice(BANK + 2 * STRIP, BANK + 3 * STRIP)
+LAST_STRIP = slice(N - STRIP, N)
+HALVES = [slice(N - STRIP, N - P), slice(N - P, N)]
+RANGES = [HEAD, FIRST, SECOND, THIRD] + HALVES
+BANK_PER_TILE = [HEAD, THIRD]
+
+PARTS = [
+    (ALL_ROWS, HEAD),
+    (EARLY_ROWS, slice(BANK, BANK + 2 * STRIP)),
+    (LATE_ROWS, FIRST),
+    (LATE_ROWS, SECOND),
+    (EARLY_ROWS, THIRD),
+    (LATE_ROWS, THIRD),
+    (EARLY_ROWS, LAST_STRIP),
+    (LATE_ROWS, LAST_STRIP),
+]
 
 SHARE_WHOLE_PASS = 288
 SHARE_NARROW = 128
-SHARE_FIRST_STRIP = 96
-SHARE_HALF = 176
-H0 = 112
-X3 = 256
-E3 = 144
-L4 = 128
+SHARE_LAST_X = 144
+SHARE_FIRST_EARLY = 64
+SHARE_FIRST_LATE = 112
+SHARE_THIRD = 144
 
 
 def tile_mix_ghost_none_kernel(tc, x, xt, g, gt, out):
     nc = tc.nc
-    vector_copy, scalar_copy = nc.vector.tensor_copy, nc.scalar.copy
     with ExitStack() as ctx:
         ctx.enter_context(tc.manual_schedule())
         raws = ctx.enter_context(tc.tile_pool(name="raws", bufs=1))
@@ -60,28 +74,24 @@ def tile_mix_ghost_none_kernel(tc, x, xt, g, gt, out):
         def rows(ap, c):
             return ap[c * K_PASS : (c + 1) * K_PASS, :].rearrange("(p t) n -> p t n", t=PACK)
 
-        def strip_cols(first, count=1):
-            return slice(first * STRIP, (first + count) * STRIP)
-
-        parts = [(ALL_ROWS, HEAD), (EARLY_ROWS, PAIR)]
-        parts.extend((LATE_ROWS, range(s, s + 1)) for s in PAIR)
-        parts.extend((word_rows, range(s, s + 1)) for s in LONE for word_rows in (EARLY_ROWS, LATE_ROWS))
+        def width(cols):
+            return cols.stop - cols.start
 
         g_raw = raws.tile([P, PACK, M], F32, align_bytes=DMA_ALIGN, name="g_raw")
         gt_raw = raws.tile([P, PACK, N], F32, align_bytes=DMA_ALIGN, name="gt_raw", tag="gt_then_res")
         x_raw = [raws.tile([P, PACK, M], F32, align_bytes=DMA_ALIGN, name="x_raw%d" % c) for c in range(PASSES)]
         xt_raw = [raws.tile([P, PACK, N], F32, align_bytes=DMA_ALIGN, name="xt_raw%d" % c) for c in range(LAST)]
-        lone_raw = {s: raws.tile([P, PACK, STRIP], F32, align_bytes=DMA_ALIGN, name="lone_raw%d" % s) for s in LONE}
+        third_raw = raws.tile([P, PACK, STRIP], F32, align_bytes=DMA_ALIGN, name="third_raw")
         part_raw = [
-            lone_raw[strips.start][:, word_rows, :]
-            if strips.start in LONE
-            else raws.tile([P, word_rows.stop - word_rows.start, len(strips) * STRIP], F32, align_bytes=DMA_ALIGN, name="part_raw%d" % q)[:]
-            for q, (word_rows, strips) in enumerate(parts)
+            third_raw[:, word_rows, :]
+            if cols == THIRD
+            else raws.tile([P, width(word_rows), width(cols)], F32, align_bytes=DMA_ALIGN, name="part_raw%d" % q)[:]
+            for q, (word_rows, cols) in enumerate(PARTS)
         ]
 
         def load_part(q):
-            word_rows, strips = parts[q]
-            nc.sync.dma_start(out=part_raw[q], in_=rows(xt, LAST)[:, word_rows, strip_cols(strips.start, len(strips))])
+            word_rows, cols = PARTS[q]
+            nc.sync.dma_start(out=part_raw[q], in_=rows(xt, LAST)[:, word_rows, cols])
 
         nc.sync.dma_start(out=g_raw[:], in_=rows(g, 0))
         nc.sync.dma_start(out=gt_raw[:], in_=rows(gt, 0))
@@ -91,7 +101,7 @@ def tile_mix_ghost_none_kernel(tc, x, xt, g, gt, out):
             nc.sync.dma_start(out=x_raw[c][:], in_=rows(x, c))
         load_part(0)
         nc.sync.dma_start(out=x_raw[LAST][:], in_=rows(x, LAST))
-        for q in range(1, len(parts)):
+        for q in range(1, len(PARTS)):
             load_part(q)
 
         g_codes = keep.tile([P, M], U32, align_bytes=MX_ALIGN, name="g_codes")
@@ -103,31 +113,41 @@ def tile_mix_ghost_none_kernel(tc, x, xt, g, gt, out):
         xt_codes = keep.tile([P, PASSES, N], U32, align_bytes=MX_ALIGN, name="xt_codes")
         xt_scales = keep.tile([P, PASSES, N], U8, align_bytes=MX_ALIGN, name="xt_scales")
         u = keep.tile([P, M_TILES, N], F32, align_bytes=DMA_ALIGN, name="u")
+        last_tiles = [
+            (cols, keep.tile([P, width(cols), PACK], BF16, align_bytes=MX_ALIGN, name="last_grouped%d" % cols.start))
+            for cols in (HEAD, FIRST, SECOND, THIRD, LAST_STRIP)
+        ]
 
-        def staging_tile():
-            return staging.tile([P, BANK, PACK], BF16, align_bytes=MX_ALIGN, name="grouped")
+        def last_grouped(cols):
+            for tile_cols, tile in last_tiles:
+                if tile_cols.start <= cols.start < tile_cols.stop:
+                    return tile[:, cols.start - tile_cols.start : cols.stop - tile_cols.start, :]
 
-        def round_columns(copy, grouped, word_rows, raw, lo, hi):
-            run_length = LINE if word_rows == ALL_ROWS or copy is vector_copy else 1
-            if hi > lo:
+        def round_columns(copy, run_length, grouped, word_rows, raw, cols):
+            if width(cols):
                 copy(
-                    out=grouped[:, lo:hi, word_rows].rearrange("p (j i) t -> p j t i", i=run_length),
-                    in_=raw[:, :, lo:hi].rearrange("p t (j i) -> p j t i", i=run_length),
+                    out=grouped[:, cols, word_rows].rearrange("p (j i) t -> p j t i", i=run_length),
+                    in_=raw[:, :, cols].rearrange("p t (j i) -> p j t i", i=run_length),
                 )
 
-        def round_rows(grouped, word_rows, raw, share):
-            round_columns(vector_copy, grouped, word_rows, raw, 0, share)
-            round_columns(scalar_copy, grouped, word_rows, raw, share, raw.shape[2])
+        def vector_rounds(grouped, word_rows, raw, cols):
+            round_columns(nc.vector.tensor_copy, LINE, grouped, word_rows, raw, cols)
+
+        def scalar_rounds(grouped, word_rows, raw, cols):
+            round_columns(nc.scalar.copy, LINE if word_rows == ALL_ROWS else 1, grouped, word_rows, raw, cols)
+
+        def round_shared(grouped, word_rows, raw, share):
+            vector_rounds(grouped, word_rows, raw, slice(0, share))
+            scalar_rounds(grouped, word_rows, raw, slice(share, raw.shape[2]))
 
         def quantize(grouped, codes, scales, fmt, matmuls):
-            width = codes.shape[1]
-            nc.vector.quantize_mx(out=codes.bitcast(fmt), scales=scales, in_=grouped[:, :width, :].rearrange("p n t -> p (n t)"))
+            nc.vector.quantize_mx(out=codes.bitcast(fmt), scales=scales, in_=grouped[:, : codes.shape[1], :].rearrange("p n t -> p (n t)"))
             for matmul in matmuls:
                 matmul()
 
         def round_piece(piece):
-            grouped = staging_tile()
-            round_rows(grouped, ALL_ROWS, piece[0], *piece[1])
+            grouped = staging.tile([P, BANK, PACK], BF16, align_bytes=MX_ALIGN, name="grouped")
+            round_shared(grouped, ALL_ROWS, *piece[:2])
             return grouped
 
         def run(pieces):
@@ -153,160 +173,101 @@ def tile_mix_ghost_none_kernel(tc, x, xt, g, gt, out):
                 )
                 nc.scalar.copy(out=u[:, m, cols], in_=bank[:])
 
-        strip_banks = {}
+        range_banks = {}
 
-        def half_cols(h):
-            return slice(N - STRIP + h * P, N - STRIP + (h + 1) * P)
+        def sums(cols, tiles):
+            banks = range_banks[cols.start]
+            if cols in BANK_PER_TILE:
+                return banks[tiles.start][:, : width(cols)]
+            return banks[0][:, tiles.start * width(cols) : tiles.stop * width(cols)]
 
-        def half_pass(c, h):
+        def a_pass(c, cols):
+            own_bank = cols in BANK_PER_TILE
+            if c == 0:
+                range_banks[cols.start] = [psum.tile([P, BANK], F32, name="bank") for m in range(M_TILES if own_bank else 1)]
             for m in range(M_TILES):
                 tile_m = slice(m * P, (m + 1) * P)
                 nc.tensor.matmul_mx(
-                    out=strip_banks[STRIPS - 1][h][:, tile_m],
-                    lhsT=x_codes[:, c, tile_m].bitcast(E4M3X4),
-                    lhsT_scale=x_scales[:, c, tile_m],
-                    rhs=xt_codes[:, c, half_cols(h)].bitcast(E4M3X4),
-                    rhs_scale=xt_scales[:, c, half_cols(h)],
-                    start=c == 0 and m == 0,
-                    stop=c == LAST and m == M_TILES - 1,
-                )
-
-        def head_pass(c):
-            cols = strip_cols(HEAD.start, len(HEAD))
-            for m in range(M_TILES):
-                tile_m = slice(m * P, (m + 1) * P)
-                nc.tensor.matmul_mx(
-                    out=strip_banks[HEAD.start][m][:],
+                    out=sums(cols, slice(m, m + 1)),
                     lhsT=x_codes[:, c, tile_m].bitcast(E4M3X4),
                     lhsT_scale=x_scales[:, c, tile_m],
                     rhs=xt_codes[:, c, cols].bitcast(E4M3X4),
                     rhs_scale=xt_scales[:, c, cols],
-                    start=c == 0,
-                    stop=c == LAST,
+                    start=c == 0 and (own_bank or m == 0),
+                    stop=c == LAST and (own_bank or m == M_TILES - 1),
                 )
 
-        def multiply_head(m):
-            cols = strip_cols(HEAD.start, len(HEAD))
-            nc.vector.tensor_tensor(out=res[:, m, cols], in0=strip_banks[HEAD.start][m][:], in1=u[:, m, cols], op=MULT)
+        def closing_matmuls(cols, *later):
+            return [partial(a_pass, LAST, cols)] + [partial(a_pass, c, held) for c in range(1, LAST) for held in later]
 
-        def a_pass(c, s):
-            split = s >= FIRST_SPLIT_STRIP or s in HEAD
-            if c == 0:
-                strip_banks[s] = ([psum.tile([P, BANK], F32, name="bank") for m in range(M_TILES if split else 1)])
-            if s in HEAD:
-                head_pass(c)
-                return
-            if s == STRIPS - 1:
-                for h in range(2):
-                    half_pass(c, h)
-                return
-            for m in range(M_TILES):
-                tile_m = slice(m * P, (m + 1) * P)
-                nc.tensor.matmul_mx(
-                    out=strip_banks[s][m][:, :STRIP] if split else strip_banks[s][0][:, strip_cols(m)],
-                    lhsT=x_codes[:, c, tile_m].bitcast(E4M3X4),
-                    lhsT_scale=x_scales[:, c, tile_m],
-                    rhs=xt_codes[:, c, strip_cols(s)].bitcast(E4M3X4),
-                    rhs_scale=xt_scales[:, c, strip_cols(s)],
-                    start=c == 0 and (split or m == 0),
-                    stop=c == LAST and (split or m == M_TILES - 1),
-                )
-
-        def closing_matmuls(s):
-            matmuls = [partial(a_pass, LAST, HEAD.start if s in HEAD else s)]
-            if 0 < s < STRIPS - 1:
-                matmuls.extend(partial(a_pass, c, s + 1) for c in range(1, LAST))
-            return matmuls
-
-        def multiply(s, tiles):
-            cols = strip_cols(s)
-            count = tiles.stop - tiles.start
-            if len(strip_banks[s]) > 1:
-                sums = strip_banks[s][tiles.start][:, :STRIP].rearrange("p (m n) -> p m n", m=1)
-            else:
-                sums = strip_banks[s][0][:, tiles.start * STRIP : tiles.stop * STRIP].rearrange("p (m n) -> p m n", m=count)
-            nc.vector.tensor_tensor(out=res[:, tiles, cols], in0=sums, in1=u[:, tiles, cols], op=MULT)
+        def multiply(cols, tiles):
+            in_psum = sums(cols, tiles).rearrange("p (m n) -> p m n", n=width(cols))
+            nc.vector.tensor_tensor(out=res[:, tiles, cols], in0=in_psum, in1=u[:, tiles, cols], op=MULT)
 
         def store(cols, tiles):
             nc.sync.dma_start(out=out.rearrange("(m p) n -> p m n", p=P)[:, tiles, cols], in_=res[:, tiles, cols])
 
         def x_piece(c, share, matmuls):
-            return (x_raw[c][:], (share,), x_codes[:, c, :], x_scales[:, c, :], E4M3X4, matmuls)
+            return (x_raw[c][:], share, x_codes[:, c, :], x_scales[:, c, :], E4M3X4, matmuls)
 
         def xt_pieces(c):
             columns = [slice(n0, n0 + BANK) for n0 in range(0, N, BANK)]
-            return [(xt_raw[c][:, :, cols], (SHARE_WHOLE_PASS,), xt_codes[:, c, cols], xt_scales[:, c, cols], E4M3X4, []) for cols in columns]
+            return [(xt_raw[c][:, :, cols], SHARE_WHOLE_PASS, xt_codes[:, c, cols], xt_scales[:, c, cols], E4M3X4, []) for cols in columns]
 
-        strip_staged = [keep.tile([P, STRIP, PACK], BF16, align_bytes=MX_ALIGN, name="strip_staged%d" % s) for s in range(STRIPS)]
+        def part(word_rows, cols):
+            for raw, (part_rows, part_cols) in zip(part_raw, PARTS):
+                if part_rows == word_rows and part_cols.start <= cols.start < part_cols.stop:
+                    first = cols.start - part_cols.start
+                    return last_grouped(cols), word_rows, raw[:, :, first : first + width(cols)]
 
-        def round_part(word_rows, s, share):
-            for raw, (part_rows, strips) in zip(part_raw, parts):
-                if part_rows == word_rows and s in strips:
-                    round_rows(strip_staged[s], word_rows, raw[:, :, strip_cols(s - strips.start)], share)
+        def quantize_range(cols, matmuls):
+            quantize(last_grouped(cols), xt_codes[:, LAST, cols], xt_scales[:, LAST, cols], E4M3X4, matmuls)
 
-        def quantize_strip(s, matmuls):
-            cols = strip_cols(s)
-            quantize(strip_staged[s], xt_codes[:, LAST, cols], xt_scales[:, LAST, cols], E4M3X4, matmuls)
-
-        u_pieces = [(g_raw[:], (SHARE_NARROW,), g_codes[:], g_scales[:], E5M2X4, [])]
+        u_pieces = [(g_raw[:], SHARE_NARROW, g_codes[:], g_scales[:], E5M2X4, [])]
         for n0 in range(0, N, BANK):
             cols = slice(n0, n0 + BANK)
-            u_pieces.append((gt_raw[:, :, cols], (BANK // 2,), gt_codes[:, cols], gt_scales[:, cols], E5M2X4, [partial(u_columns, cols)]))
+            u_pieces.append((gt_raw[:, :, cols], BANK // 2, gt_codes[:, cols], gt_scales[:, cols], E5M2X4, [partial(u_columns, cols)]))
         run(u_pieces)
         res = raws.tile([P, M_TILES, N], F32, align_bytes=DMA_ALIGN, name="res", tag="gt_then_res")
         for c in range(LAST - 1):
             run(xt_pieces(c))
 
-        x_pieces = [x_piece(c, SHARE_NARROW, [partial(a_pass, c, s) for s in (range(STRIPS) if c == 0 else HEAD) if s != 1]) for c in range(LAST)]
+        x_pieces = [x_piece(c, SHARE_NARROW, [partial(a_pass, c, cols) for cols in (RANGES if c == 0 else (HEAD, FIRST))]) for c in range(LAST)]
         run([piece for pair in zip(xt_pieces(LAST - 1), x_pieces) for piece in pair])
 
-        both, top, bottom = slice(0, 2), slice(0, 1), slice(1, 2)
+        last_x = x_piece(LAST, SHARE_LAST_X, closing_matmuls(HEAD, SECOND))
+        round_shared(*part(ALL_ROWS, HEAD), BANK // 2)
+        last_x_grouped = round_piece(last_x)
+        quantize_range(slice(HEAD.start, BANK // 2), [])
+        quantize_range(slice(BANK // 2, HEAD.stop), [])
+        quantize(last_x_grouped, *last_x[2:])
 
-        def quantize_half(h):
-            cols = half_cols(h)
-            quantize(strip_staged[-1][:, h * P :, :], xt_codes[:, LAST, cols], xt_scales[:, LAST, cols], E4M3X4, [partial(half_pass, LAST, h)])
+        round_shared(*part(EARLY_ROWS, FIRST), SHARE_FIRST_EARLY)
+        round_shared(*part(EARLY_ROWS, SECOND), STRIP)
+        round_shared(*part(LATE_ROWS, FIRST), SHARE_FIRST_LATE)
+        multiply(HEAD, TOP)
+        quantize_range(FIRST, closing_matmuls(FIRST, THIRD))
+        round_shared(*part(LATE_ROWS, SECOND), 0)
+        multiply(HEAD, BOTTOM)
+        store(HEAD, BOTH_TILES)
+        quantize_range(SECOND, closing_matmuls(SECOND, *HALVES))
 
-        def finish_half(h):
-            cols = half_cols(h)
-            sums = strip_banks[STRIPS - 1][h][:, :STRIP].rearrange("p (m n) -> p m n", m=M_TILES)
-            nc.vector.tensor_tensor(out=res[:, :, cols], in0=sums, in1=u[:, :, cols], op=MULT)
-            store(cols, both)
+        scalar_rounds(*part(EARLY_ROWS, THIRD), slice(0, SHARE_THIRD))
+        vector_rounds(*part(LATE_ROWS, THIRD), slice(0, SHARE_THIRD))
+        scalar_rounds(last_grouped(THIRD), ALL_ROWS, third_raw[:], slice(SHARE_THIRD, STRIP))
+        multiply(FIRST, BOTH_TILES)
+        store(FIRST, BOTH_TILES)
+        quantize_range(THIRD, closing_matmuls(THIRD))
 
-        def round_lone(s, early, late):
-            raw = lone_raw[s]
-            round_columns(scalar_copy, strip_staged[s], EARLY_ROWS, raw[:, EARLY_ROWS, :], 0, early)
-            round_columns(vector_copy, strip_staged[s], LATE_ROWS, raw[:, LATE_ROWS, :], 0, late)
-            round_columns(scalar_copy, strip_staged[s], LATE_ROWS, raw[:, LATE_ROWS, :], late, early)
-            round_columns(scalar_copy, strip_staged[s], ALL_ROWS, raw[:], early, STRIP)
-
-        last_x = x_piece(LAST, X3, [])
-        round_part(ALL_ROWS, 0, H0)
-        last_x_staged = round_piece(last_x)
-        quantize_strip(0, [])
-        round_part(ALL_ROWS, 1, 0)
-        quantize(last_x_staged, *last_x[2:])
-        quantize_strip(1, closing_matmuls(1))
-        round_part(EARLY_ROWS, 2, 0)
-        round_part(EARLY_ROWS, 3, E3)
-        round_part(LATE_ROWS, 2, STRIP)
-        multiply_head(0)
-        quantize_strip(2, closing_matmuls(2))
-        round_part(LATE_ROWS, 3, 0)
-        multiply_head(1)
-        store(strip_cols(0, 2), both)
-        quantize_strip(3, closing_matmuls(3))
-        round_lone(4, L4, L4)
-        multiply(2, both)
-        store(strip_cols(2), both)
-        quantize_strip(4, closing_matmuls(4))
-        multiply(3, top)
-        round_lone(5, STRIP, P)
-        multiply(3, bottom)
-        store(strip_cols(3), both)
-        quantize_half(0)
-        quantize_half(1)
-        for tiles in (top, bottom):
-            multiply(4, tiles)
-            store(strip_cols(4), tiles)
-        finish_half(0)
-        finish_half(1)
+        multiply(SECOND, TOP)
+        round_shared(*part(EARLY_ROWS, LAST_STRIP), 0)
+        round_shared(*part(LATE_ROWS, LAST_STRIP), P)
+        multiply(SECOND, BOTTOM)
+        store(SECOND, BOTH_TILES)
+        for half, tiles in zip(HALVES, (TOP, BOTTOM)):
+            quantize_range(half, closing_matmuls(half))
+            multiply(THIRD, tiles)
+            store(THIRD, tiles)
+        for half in HALVES:
+            multiply(half, BOTH_TILES)
+            store(half, BOTH_TILES)

@@ -28,9 +28,6 @@ STAGED = 5
 MX_ALIGN = 256
 DMA_ALIGN = 256
 
-ALL_ROWS = slice(0, PACK)
-EARLY_ROWS = slice(0, PACK // 2)
-LATE_ROWS = slice(PACK // 2, PACK)
 BOTH_TILES = slice(0, M_TILES)
 TOP, BOTTOM = slice(0, 1), slice(1, 2)
 
@@ -38,28 +35,19 @@ HEAD = slice(0, BANK)
 FIRST = slice(BANK, BANK + STRIP)
 SECOND = slice(BANK + STRIP, BANK + 2 * STRIP)
 THIRD = slice(BANK + 2 * STRIP, BANK + 3 * STRIP)
-LAST_STRIP = slice(N - STRIP, N)
 HALVES = [slice(N - STRIP, N - P), slice(N - P, N)]
 RANGES = [HEAD, FIRST, SECOND, THIRD] + HALVES
 BANK_PER_TILE = [HEAD, THIRD]
 
-PARTS = [
-    (ALL_ROWS, HEAD),
-    (EARLY_ROWS, slice(BANK, BANK + 2 * STRIP)),
-    (LATE_ROWS, FIRST),
-    (LATE_ROWS, SECOND),
-    (EARLY_ROWS, THIRD),
-    (LATE_ROWS, THIRD),
-    (EARLY_ROWS, LAST_STRIP),
-    (LATE_ROWS, LAST_STRIP),
-]
+STRIPS = [slice(n0, n0 + STRIP) for n0 in range(0, THIRD.start, STRIP)]
+NARROW = [slice(n0, n0 + P) for n0 in range(THIRD.start, N, P)]
+PARTS = STRIPS + NARROW
+AHEAD_OF_LAST_X = BANK // STRIP
 
 SHARE_WHOLE_PASS = 288
 SHARE_NARROW = 128
-SHARE_LAST_X = 144
-SHARE_FIRST_EARLY = 64
-SHARE_FIRST_LATE = 112
-SHARE_THIRD = 144
+SHARE_HEAD = 64
+SHARE_STRIP = 96
 
 
 def tile_mix_ghost_none_kernel(tc, x, xt, g, gt, out):
@@ -81,17 +69,10 @@ def tile_mix_ghost_none_kernel(tc, x, xt, g, gt, out):
         gt_raw = raws.tile([P, PACK, N], F32, align_bytes=DMA_ALIGN, name="gt_raw", tag="gt_then_res")
         x_raw = [raws.tile([P, PACK, M], F32, align_bytes=DMA_ALIGN, name="x_raw%d" % c) for c in range(PASSES)]
         xt_raw = [raws.tile([P, PACK, N], F32, align_bytes=DMA_ALIGN, name="xt_raw%d" % c) for c in range(LAST)]
-        third_raw = raws.tile([P, PACK, STRIP], F32, align_bytes=DMA_ALIGN, name="third_raw")
-        part_raw = [
-            third_raw[:, word_rows, :]
-            if cols == THIRD
-            else raws.tile([P, width(word_rows), width(cols)], F32, align_bytes=DMA_ALIGN, name="part_raw%d" % q)[:]
-            for q, (word_rows, cols) in enumerate(PARTS)
-        ]
+        part_raw = [raws.tile([P, PACK, width(cols)], F32, align_bytes=DMA_ALIGN, name="part_raw%d" % cols.start) for cols in PARTS]
 
         def load_part(q):
-            word_rows, cols = PARTS[q]
-            nc.sync.dma_start(out=part_raw[q], in_=rows(xt, LAST)[:, word_rows, cols])
+            nc.sync.dma_start(out=part_raw[q][:], in_=rows(xt, LAST)[:, :, PARTS[q]])
 
         nc.sync.dma_start(out=g_raw[:], in_=rows(g, 0))
         nc.sync.dma_start(out=gt_raw[:], in_=rows(gt, 0))
@@ -99,9 +80,9 @@ def tile_mix_ghost_none_kernel(tc, x, xt, g, gt, out):
             nc.sync.dma_start(out=xt_raw[c][:], in_=rows(xt, c))
         for c in range(LAST):
             nc.sync.dma_start(out=x_raw[c][:], in_=rows(x, c))
-        load_part(0)
-        nc.sync.dma_start(out=x_raw[LAST][:], in_=rows(x, LAST))
-        for q in range(1, len(PARTS)):
+        for q in range(len(PARTS)):
+            if q == AHEAD_OF_LAST_X:
+                nc.sync.dma_start(out=x_raw[LAST][:], in_=rows(x, LAST))
             load_part(q)
 
         g_codes = keep.tile([P, M], U32, align_bytes=MX_ALIGN, name="g_codes")
@@ -113,32 +94,19 @@ def tile_mix_ghost_none_kernel(tc, x, xt, g, gt, out):
         xt_codes = keep.tile([P, PASSES, N], U32, align_bytes=MX_ALIGN, name="xt_codes")
         xt_scales = keep.tile([P, PASSES, N], U8, align_bytes=MX_ALIGN, name="xt_scales")
         u = keep.tile([P, M_TILES, N], F32, align_bytes=DMA_ALIGN, name="u")
-        last_tiles = [
-            (cols, keep.tile([P, width(cols), PACK], BF16, align_bytes=MX_ALIGN, name="last_grouped%d" % cols.start))
-            for cols in (HEAD, FIRST, SECOND, THIRD, LAST_STRIP)
-        ]
+        last_grouped = keep.tile([P, N, PACK], BF16, align_bytes=MX_ALIGN, name="last_grouped")
+        last_x_grouped = keep.tile([P, M, PACK], BF16, align_bytes=MX_ALIGN, name="last_x_grouped")
 
-        def last_grouped(cols):
-            for tile_cols, tile in last_tiles:
-                if tile_cols.start <= cols.start < tile_cols.stop:
-                    return tile[:, cols.start - tile_cols.start : cols.stop - tile_cols.start, :]
-
-        def round_columns(copy, run_length, grouped, word_rows, raw, cols):
+        def round_columns(copy, grouped, raw, cols):
             if width(cols):
                 copy(
-                    out=grouped[:, cols, word_rows].rearrange("p (j i) t -> p j t i", i=run_length),
-                    in_=raw[:, :, cols].rearrange("p t (j i) -> p j t i", i=run_length),
+                    out=grouped[:, cols, :].rearrange("p (j i) t -> p j t i", i=LINE),
+                    in_=raw[:, :, cols].rearrange("p t (j i) -> p j t i", i=LINE),
                 )
 
-        def vector_rounds(grouped, word_rows, raw, cols):
-            round_columns(nc.vector.tensor_copy, LINE, grouped, word_rows, raw, cols)
-
-        def scalar_rounds(grouped, word_rows, raw, cols):
-            round_columns(nc.scalar.copy, LINE if word_rows == ALL_ROWS else 1, grouped, word_rows, raw, cols)
-
-        def round_shared(grouped, word_rows, raw, share):
-            vector_rounds(grouped, word_rows, raw, slice(0, share))
-            scalar_rounds(grouped, word_rows, raw, slice(share, raw.shape[2]))
+        def round_shared(grouped, raw, share):
+            round_columns(nc.vector.tensor_copy, grouped, raw, slice(0, share))
+            round_columns(nc.scalar.copy, grouped, raw, slice(share, raw.shape[2]))
 
         def quantize(grouped, codes, scales, fmt, matmuls):
             nc.vector.quantize_mx(out=codes.bitcast(fmt), scales=scales, in_=grouped[:, : codes.shape[1], :].rearrange("p n t -> p (n t)"))
@@ -147,7 +115,7 @@ def tile_mix_ghost_none_kernel(tc, x, xt, g, gt, out):
 
         def round_piece(piece):
             grouped = staging.tile([P, BANK, PACK], BF16, align_bytes=MX_ALIGN, name="grouped")
-            round_shared(grouped, ALL_ROWS, *piece[:2])
+            round_shared(grouped, *piece[:2])
             return grouped
 
         def run(pieces):
@@ -181,11 +149,11 @@ def tile_mix_ghost_none_kernel(tc, x, xt, g, gt, out):
                 return banks[tiles.start][:, : width(cols)]
             return banks[0][:, tiles.start * width(cols) : tiles.stop * width(cols)]
 
-        def a_pass(c, cols):
+        def a_pass(c, cols, tiles=BOTH_TILES):
             own_bank = cols in BANK_PER_TILE
             if c == 0:
                 range_banks[cols.start] = [psum.tile([P, BANK], F32, name="bank") for m in range(M_TILES if own_bank else 1)]
-            for m in range(M_TILES):
+            for m in range(tiles.start, tiles.stop):
                 tile_m = slice(m * P, (m + 1) * P)
                 nc.tensor.matmul_mx(
                     out=sums(cols, slice(m, m + 1)),
@@ -197,8 +165,8 @@ def tile_mix_ghost_none_kernel(tc, x, xt, g, gt, out):
                     stop=c == LAST and (own_bank or m == M_TILES - 1),
                 )
 
-        def closing_matmuls(cols, *later):
-            return [partial(a_pass, LAST, cols)] + [partial(a_pass, c, held) for c in range(1, LAST) for held in later]
+        def closing_matmuls(cols, *later, tiles=BOTH_TILES):
+            return [partial(a_pass, LAST, cols, tiles)] + [partial(a_pass, c, held) for c in range(1, LAST) for held in later]
 
         def multiply(cols, tiles):
             in_psum = sums(cols, tiles).rearrange("p (m n) -> p m n", n=width(cols))
@@ -214,14 +182,15 @@ def tile_mix_ghost_none_kernel(tc, x, xt, g, gt, out):
             columns = [slice(n0, n0 + BANK) for n0 in range(0, N, BANK)]
             return [(xt_raw[c][:, :, cols], SHARE_WHOLE_PASS, xt_codes[:, c, cols], xt_scales[:, c, cols], E4M3X4, []) for cols in columns]
 
-        def part(word_rows, cols):
-            for raw, (part_rows, part_cols) in zip(part_raw, PARTS):
-                if part_rows == word_rows and part_cols.start <= cols.start < part_cols.stop:
-                    first = cols.start - part_cols.start
-                    return last_grouped(cols), word_rows, raw[:, :, first : first + width(cols)]
+        def round_part(cols, share):
+            round_shared(last_grouped[:, cols, :], part_raw[PARTS.index(cols)][:], share)
 
         def quantize_range(cols, matmuls):
-            quantize(last_grouped(cols), xt_codes[:, LAST, cols], xt_scales[:, LAST, cols], E4M3X4, matmuls)
+            quantize(last_grouped[:, cols, :], xt_codes[:, LAST, cols], xt_scales[:, LAST, cols], E4M3X4, matmuls)
+
+        def quantize_last_x(tiles, matmuls):
+            cols = slice(tiles.start * P, tiles.stop * P)
+            quantize(last_x_grouped[:, cols, :], x_codes[:, LAST, cols], x_scales[:, LAST, cols], E4M3X4, matmuls)
 
         u_pieces = [(g_raw[:], SHARE_NARROW, g_codes[:], g_scales[:], E5M2X4, [])]
         for n0 in range(0, N, BANK):
@@ -235,34 +204,27 @@ def tile_mix_ghost_none_kernel(tc, x, xt, g, gt, out):
         x_pieces = [x_piece(c, SHARE_NARROW, [partial(a_pass, c, cols) for cols in (RANGES if c == 0 else (HEAD, FIRST))]) for c in range(LAST)]
         run([piece for pair in zip(xt_pieces(LAST - 1), x_pieces) for piece in pair])
 
-        last_x = x_piece(LAST, SHARE_LAST_X, closing_matmuls(HEAD, SECOND))
-        round_shared(*part(ALL_ROWS, HEAD), BANK // 2)
-        last_x_grouped = round_piece(last_x)
-        quantize_range(slice(HEAD.start, BANK // 2), [])
-        quantize_range(slice(BANK // 2, HEAD.stop), [])
-        quantize(last_x_grouped, *last_x[2:])
+        round_part(STRIPS[0], SHARE_HEAD)
+        round_part(STRIPS[1], SHARE_HEAD)
+        quantize_range(STRIPS[0], [])
+        round_shared(last_x_grouped[:], x_raw[LAST][:], P)
+        quantize_range(STRIPS[1], [])
+        quantize_last_x(TOP, closing_matmuls(HEAD, tiles=TOP))
+        quantize_last_x(BOTTOM, closing_matmuls(HEAD, SECOND, tiles=BOTTOM))
 
-        round_shared(*part(EARLY_ROWS, FIRST), SHARE_FIRST_EARLY)
-        round_shared(*part(EARLY_ROWS, SECOND), STRIP)
-        round_shared(*part(LATE_ROWS, FIRST), SHARE_FIRST_LATE)
+        round_part(FIRST, SHARE_STRIP)
         multiply(HEAD, TOP)
         quantize_range(FIRST, closing_matmuls(FIRST, THIRD))
-        round_shared(*part(LATE_ROWS, SECOND), 0)
+        round_part(SECOND, SHARE_STRIP)
         multiply(HEAD, BOTTOM)
         store(HEAD, BOTH_TILES)
         quantize_range(SECOND, closing_matmuls(SECOND, *HALVES))
-
-        scalar_rounds(*part(EARLY_ROWS, THIRD), slice(0, SHARE_THIRD))
-        vector_rounds(*part(LATE_ROWS, THIRD), slice(0, SHARE_THIRD))
-        scalar_rounds(last_grouped(THIRD), ALL_ROWS, third_raw[:], slice(SHARE_THIRD, STRIP))
+        for cols in NARROW:
+            round_part(cols, 0)
         multiply(FIRST, BOTH_TILES)
         store(FIRST, BOTH_TILES)
         quantize_range(THIRD, closing_matmuls(THIRD))
-
-        multiply(SECOND, TOP)
-        round_shared(*part(EARLY_ROWS, LAST_STRIP), 0)
-        round_shared(*part(LATE_ROWS, LAST_STRIP), P)
-        multiply(SECOND, BOTTOM)
+        multiply(SECOND, BOTH_TILES)
         store(SECOND, BOTH_TILES)
         for half, tiles in zip(HALVES, (TOP, BOTTOM)):
             quantize_range(half, closing_matmuls(half))

@@ -44,10 +44,11 @@ NARROW = [slice(n0, n0 + P) for n0 in range(THIRD.start, N, P)]
 PARTS = STRIPS + NARROW
 AHEAD_OF_LAST_X = BANK // STRIP
 
-SHARE_WHOLE_PASS = 288
+SHARE_WHOLE_PASS = 304
 SHARE_NARROW = 128
-SHARE_HEAD = 64
-SHARE_STRIP = 96
+SHARE_HEAD = (176, 112)
+SHARE_FIRST = 48
+SHARE_SECOND = 128
 
 
 def tile_mix_ghost_none_kernel(tc, x, xt, g, gt, out):
@@ -104,17 +105,26 @@ def tile_mix_ghost_none_kernel(tc, x, xt, g, gt, out):
                     in_=raw[:, :, cols].rearrange("p t (j i) -> p j t i", i=LINE),
                 )
 
-        def round_shared(grouped, raw, share):
+        def vector_rounds(grouped, raw, share):
             round_columns(nc.vector.tensor_copy, grouped, raw, slice(0, share))
+
+        def scalar_rounds(grouped, raw, share):
             round_columns(nc.scalar.copy, grouped, raw, slice(share, raw.shape[2]))
+
+        def round_shared(grouped, raw, share):
+            vector_rounds(grouped, raw, share)
+            scalar_rounds(grouped, raw, share)
 
         def quantize(grouped, codes, scales, fmt, matmuls):
             nc.vector.quantize_mx(out=codes.bitcast(fmt), scales=scales, in_=grouped[:, : codes.shape[1], :].rearrange("p n t -> p (n t)"))
             for matmul in matmuls:
                 matmul()
 
+        def staging_tile():
+            return staging.tile([P, BANK, PACK], BF16, align_bytes=MX_ALIGN, name="grouped")
+
         def round_piece(piece):
-            grouped = staging.tile([P, BANK, PACK], BF16, align_bytes=MX_ALIGN, name="grouped")
+            grouped = staging_tile()
             round_shared(grouped, *piece[:2])
             return grouped
 
@@ -201,21 +211,35 @@ def tile_mix_ghost_none_kernel(tc, x, xt, g, gt, out):
         for c in range(LAST - 1):
             run(xt_pieces(c))
 
+        thirds = xt_pieces(LAST - 1)
         x_pieces = [x_piece(c, SHARE_NARROW, [partial(a_pass, c, cols) for cols in (RANGES if c == 0 else (HEAD, FIRST))]) for c in range(LAST)]
-        run([piece for pair in zip(xt_pieces(LAST - 1), x_pieces) for piece in pair])
+        first_third = round_piece(thirds[0])
+        second_third = staging_tile()
+        vector_rounds(second_third, *thirds[1][:2])
+        x_first = round_piece(x_pieces[0])
+        scalar_rounds(second_third, *thirds[1][:2])
+        quantize(first_third, *thirds[0][2:])
+        quantize(x_first, *x_pieces[0][2:])
+        x_second = round_piece(x_pieces[1])
+        quantize(second_third, *thirds[1][2:])
+        last_third = round_piece(thirds[2])
+        quantize(x_second, *x_pieces[1][2:])
+        x_third = round_piece(x_pieces[2])
 
-        round_part(STRIPS[0], SHARE_HEAD)
-        round_part(STRIPS[1], SHARE_HEAD)
+        round_part(STRIPS[0], SHARE_HEAD[0])
+        quantize(x_third, *x_pieces[2][2:])
+        round_part(STRIPS[1], SHARE_HEAD[1])
         quantize_range(STRIPS[0], [])
         round_shared(last_x_grouped[:], x_raw[LAST][:], P)
         quantize_range(STRIPS[1], [])
         quantize_last_x(TOP, closing_matmuls(HEAD, tiles=TOP))
         quantize_last_x(BOTTOM, closing_matmuls(HEAD, SECOND, tiles=BOTTOM))
+        quantize(last_third, *thirds[2][2:])
 
-        round_part(FIRST, SHARE_STRIP)
+        round_part(FIRST, SHARE_FIRST)
         multiply(HEAD, TOP)
         quantize_range(FIRST, closing_matmuls(FIRST, THIRD))
-        round_part(SECOND, SHARE_STRIP)
+        round_part(SECOND, SHARE_SECOND)
         multiply(HEAD, BOTTOM)
         store(HEAD, BOTH_TILES)
         quantize_range(SECOND, closing_matmuls(SECOND, *HALVES))

@@ -39,16 +39,12 @@ HALVES = [slice(N - STRIP, N - P), slice(N - P, N)]
 RANGES = [HEAD, FIRST, SECOND, THIRD] + HALVES
 BANK_PER_TILE = [HEAD, THIRD]
 
-STRIPS = [slice(n0, n0 + STRIP) for n0 in range(0, THIRD.start, STRIP)]
-NARROW = [slice(n0, n0 + P) for n0 in range(THIRD.start, N, P)]
-PARTS = STRIPS + NARROW
-AHEAD_OF_LAST_X = BANK // STRIP
 
 SHARE_WHOLE_PASS = 304
 SHARE_NARROW = 128
-SHARE_HEAD = (176, 112)
 SHARE_FIRST = 48
-SHARE_SECOND = 128
+SHARE_SECOND = 64
+SHARE_THIRD = 96
 
 
 def tile_mix_ghost_none_kernel(tc, x, xt, g, gt, out):
@@ -70,10 +66,7 @@ def tile_mix_ghost_none_kernel(tc, x, xt, g, gt, out):
         gt_raw = raws.tile([P, PACK, N], F32, align_bytes=DMA_ALIGN, name="gt_raw", tag="gt_then_res")
         x_raw = [raws.tile([P, PACK, M], F32, align_bytes=DMA_ALIGN, name="x_raw%d" % c) for c in range(PASSES)]
         xt_raw = [raws.tile([P, PACK, N], F32, align_bytes=DMA_ALIGN, name="xt_raw%d" % c) for c in range(LAST)]
-        part_raw = [raws.tile([P, PACK, width(cols)], F32, align_bytes=DMA_ALIGN, name="part_raw%d" % cols.start) for cols in PARTS]
-
-        def load_part(q):
-            nc.sync.dma_start(out=part_raw[q][:], in_=rows(xt, LAST)[:, :, PARTS[q]])
+        part_raw = [raws.tile([P, PACK, width(cols)], F32, align_bytes=DMA_ALIGN, name="part_raw%d" % cols.start) for cols in RANGES]
 
         nc.sync.dma_start(out=g_raw[:], in_=rows(g, 0))
         nc.sync.dma_start(out=gt_raw[:], in_=rows(gt, 0))
@@ -81,10 +74,10 @@ def tile_mix_ghost_none_kernel(tc, x, xt, g, gt, out):
             nc.sync.dma_start(out=xt_raw[c][:], in_=rows(xt, c))
         for c in range(LAST):
             nc.sync.dma_start(out=x_raw[c][:], in_=rows(x, c))
-        for q in range(len(PARTS)):
-            if q == AHEAD_OF_LAST_X:
+        for raw, cols in zip(part_raw, RANGES):
+            nc.sync.dma_start(out=raw[:], in_=rows(xt, LAST)[:, :, cols])
+            if cols == HEAD:
                 nc.sync.dma_start(out=x_raw[LAST][:], in_=rows(x, LAST))
-            load_part(q)
 
         g_codes = keep.tile([P, M], U32, align_bytes=MX_ALIGN, name="g_codes")
         g_scales = keep.tile([P, M], U8, align_bytes=MX_ALIGN, name="g_scales")
@@ -178,12 +171,16 @@ def tile_mix_ghost_none_kernel(tc, x, xt, g, gt, out):
         def closing_matmuls(cols, *later, tiles=BOTH_TILES):
             return [partial(a_pass, LAST, cols, tiles)] + [partial(a_pass, c, held) for c in range(1, LAST) for held in later]
 
+        def products(cols, tiles):
+            of_range = res[:, M_TILES * cols.start : M_TILES * cols.stop].rearrange("p (m n) -> p m n", m=M_TILES)
+            return of_range[:, tiles, :]
+
         def multiply(cols, tiles):
             in_psum = sums(cols, tiles).rearrange("p (m n) -> p m n", n=width(cols))
-            nc.vector.tensor_tensor(out=res[:, tiles, cols], in0=in_psum, in1=u[:, tiles, cols], op=MULT)
+            nc.vector.tensor_tensor(out=products(cols, tiles), in0=in_psum, in1=u[:, tiles, cols], op=MULT)
 
         def store(cols, tiles):
-            nc.sync.dma_start(out=out.rearrange("(m p) n -> p m n", p=P)[:, tiles, cols], in_=res[:, tiles, cols])
+            nc.sync.dma_start(out=out.rearrange("(m p) n -> p m n", p=P)[:, tiles, cols], in_=products(cols, tiles))
 
         def x_piece(c, share, matmuls):
             return (x_raw[c][:], share, x_codes[:, c, :], x_scales[:, c, :], E4M3X4, matmuls)
@@ -193,7 +190,7 @@ def tile_mix_ghost_none_kernel(tc, x, xt, g, gt, out):
             return [(xt_raw[c][:, :, cols], SHARE_WHOLE_PASS, xt_codes[:, c, cols], xt_scales[:, c, cols], E4M3X4, []) for cols in columns]
 
         def round_part(cols, share):
-            round_shared(last_grouped[:, cols, :], part_raw[PARTS.index(cols)][:], share)
+            round_shared(last_grouped[:, cols, :], part_raw[RANGES.index(cols)][:], share)
 
         def quantize_range(cols, matmuls):
             quantize(last_grouped[:, cols, :], xt_codes[:, LAST, cols], xt_scales[:, LAST, cols], E4M3X4, matmuls)
@@ -207,7 +204,7 @@ def tile_mix_ghost_none_kernel(tc, x, xt, g, gt, out):
             cols = slice(n0, n0 + BANK)
             u_pieces.append((gt_raw[:, :, cols], BANK // 2, gt_codes[:, cols], gt_scales[:, cols], E5M2X4, [partial(u_columns, cols)]))
         run(u_pieces)
-        res = raws.tile([P, M_TILES, N], F32, align_bytes=DMA_ALIGN, name="res", tag="gt_then_res")
+        res = raws.tile([P, M_TILES * N], F32, align_bytes=DMA_ALIGN, name="res", tag="gt_then_res")
         for c in range(LAST - 1):
             run(xt_pieces(c))
 
@@ -226,12 +223,11 @@ def tile_mix_ghost_none_kernel(tc, x, xt, g, gt, out):
         quantize(x_second, *x_pieces[1][2:])
         x_third = round_piece(x_pieces[2])
 
-        round_part(STRIPS[0], SHARE_HEAD[0])
+        round_part(HEAD, STRIP)
         quantize(x_third, *x_pieces[2][2:])
-        round_part(STRIPS[1], SHARE_HEAD[1])
-        quantize_range(STRIPS[0], [])
+        quantize_range(slice(0, STRIP), [])
         round_shared(last_x_grouped[:], x_raw[LAST][:], P)
-        quantize_range(STRIPS[1], [])
+        quantize_range(slice(STRIP, BANK), [])
         quantize_last_x(TOP, closing_matmuls(HEAD, tiles=TOP))
         quantize_last_x(BOTTOM, closing_matmuls(HEAD, SECOND, tiles=BOTTOM))
         quantize(last_third, *thirds[2][2:])
@@ -243,11 +239,12 @@ def tile_mix_ghost_none_kernel(tc, x, xt, g, gt, out):
         multiply(HEAD, BOTTOM)
         store(HEAD, BOTH_TILES)
         quantize_range(SECOND, closing_matmuls(SECOND, *HALVES))
-        for cols in NARROW:
-            round_part(cols, 0)
+        round_part(THIRD, SHARE_THIRD)
         multiply(FIRST, BOTH_TILES)
         store(FIRST, BOTH_TILES)
         quantize_range(THIRD, closing_matmuls(THIRD))
+        for half in HALVES:
+            round_part(half, 0)
         multiply(SECOND, BOTH_TILES)
         store(SECOND, BOTH_TILES)
         for half, tiles in zip(HALVES, (TOP, BOTTOM)):

@@ -234,14 +234,16 @@ def tile_mix_ghost_none_kernel(tc, x, xt, g, gt, out):
 
         round_part(FIRST, SHARE_FIRST)
         multiply(HEAD, TOP)
+        store(HEAD, TOP)
         quantize_range(FIRST, closing_matmuls(FIRST, THIRD))
         round_part(SECOND, SHARE_SECOND)
         multiply(HEAD, BOTTOM)
-        store(HEAD, BOTH_TILES)
+        store(HEAD, BOTTOM)
         quantize_range(SECOND, closing_matmuls(SECOND, *HALVES))
         round_part(THIRD, SHARE_THIRD)
         multiply(FIRST, BOTH_TILES)
-        store(FIRST, BOTH_TILES)
+        store(FIRST, TOP)
+        store(FIRST, BOTTOM)
         quantize_range(THIRD, closing_matmuls(THIRD))
         for half in HALVES:
             round_part(half, 0)

@@ -40,11 +40,11 @@ RANGES = [HEAD, FIRST, SECOND, THIRD] + HALVES
 BANK_PER_TILE = [HEAD, THIRD]
 
 
-SHARE_WHOLE_PASS = 304
+SHARE_WHOLE_PASS = 288
 SHARE_NARROW = 128
-SHARE_FIRST = 48
-SHARE_SECOND = 64
-SHARE_THIRD = 96
+SHARE_FIRST = 112
+SHARE_SECOND = 48
+SHARE_THIRD = 80
 
 
 def tile_mix_ghost_none_kernel(tc, x, xt, g, gt, out):
@@ -175,11 +175,9 @@ def tile_mix_ghost_none_kernel(tc, x, xt, g, gt, out):
             of_range = res[:, M_TILES * cols.start : M_TILES * cols.stop].rearrange("p (m n) -> p m n", m=M_TILES)
             return of_range[:, tiles, :]
 
-        def multiply(cols, tiles):
+        def multiply_and_store(cols, tiles):
             in_psum = sums(cols, tiles).rearrange("p (m n) -> p m n", n=width(cols))
             nc.vector.tensor_tensor(out=products(cols, tiles), in0=in_psum, in1=u[:, tiles, cols], op=MULT)
-
-        def store(cols, tiles):
             nc.sync.dma_start(out=out.rearrange("(m p) n -> p m n", p=P)[:, tiles, cols], in_=products(cols, tiles))
 
         def x_piece(c, share, matmuls):
@@ -230,29 +228,23 @@ def tile_mix_ghost_none_kernel(tc, x, xt, g, gt, out):
         quantize_range(slice(STRIP, BANK), [])
         quantize_last_x(TOP, closing_matmuls(HEAD, tiles=TOP))
         quantize_last_x(BOTTOM, closing_matmuls(HEAD, SECOND, tiles=BOTTOM))
+        round_part(FIRST, SHARE_FIRST)
         quantize(last_third, *thirds[2][2:])
 
-        round_part(FIRST, SHARE_FIRST)
-        multiply(HEAD, TOP)
-        store(HEAD, TOP)
         quantize_range(FIRST, closing_matmuls(FIRST, THIRD))
+        multiply_and_store(HEAD, TOP)
         round_part(SECOND, SHARE_SECOND)
-        multiply(HEAD, BOTTOM)
-        store(HEAD, BOTTOM)
+        multiply_and_store(HEAD, BOTTOM)
         quantize_range(SECOND, closing_matmuls(SECOND, *HALVES))
         round_part(THIRD, SHARE_THIRD)
-        multiply(FIRST, BOTH_TILES)
-        store(FIRST, TOP)
-        store(FIRST, BOTTOM)
+        multiply_and_store(FIRST, BOTH_TILES)
         quantize_range(THIRD, closing_matmuls(THIRD))
         for half in HALVES:
             round_part(half, 0)
-        multiply(SECOND, BOTH_TILES)
-        store(SECOND, BOTH_TILES)
         for half, tiles in zip(HALVES, (TOP, BOTTOM)):
+            multiply_and_store(SECOND, tiles)
             quantize_range(half, closing_matmuls(half))
-            multiply(THIRD, tiles)
-            store(THIRD, tiles)
+        for tiles in (TOP, BOTTOM):
+            multiply_and_store(THIRD, tiles)
         for half in HALVES:
-            multiply(half, BOTH_TILES)
-            store(half, BOTH_TILES)
+            multiply_and_store(half, BOTH_TILES)

@@ -35,6 +35,7 @@ HEAD = slice(0, BANK)
 FIRST = slice(BANK, BANK + STRIP)
 SECOND = slice(BANK + STRIP, BANK + 2 * STRIP)
 THIRD = slice(BANK + 2 * STRIP, BANK + 3 * STRIP)
+LAST_STRIP = slice(N - STRIP, N)
 HALVES = [slice(N - STRIP, N - P), slice(N - P, N)]
 RANGES = [HEAD, FIRST, SECOND, THIRD] + HALVES
 BANK_PER_TILE = [HEAD, THIRD]
@@ -172,13 +173,20 @@ def tile_mix_ghost_none_kernel(tc, x, xt, g, gt, out):
             return [partial(a_pass, LAST, cols, tiles)] + [partial(a_pass, c, held) for c in range(1, LAST) for held in later]
 
         def products(cols, tiles):
-            of_range = res[:, M_TILES * cols.start : M_TILES * cols.stop].rearrange("p (m n) -> p m n", m=M_TILES)
-            return of_range[:, tiles, :]
+            stored = LAST_STRIP if cols in HALVES else cols
+            of_range = res[:, M_TILES * stored.start : M_TILES * stored.stop].rearrange("p (m n) -> p m n", m=M_TILES)
+            return of_range[:, tiles, cols.start - stored.start : cols.stop - stored.start]
 
-        def multiply_and_store(cols, tiles):
+        def multiply(cols, tiles):
             in_psum = sums(cols, tiles).rearrange("p (m n) -> p m n", n=width(cols))
             nc.vector.tensor_tensor(out=products(cols, tiles), in0=in_psum, in1=u[:, tiles, cols], op=MULT)
+
+        def store(cols, tiles):
             nc.sync.dma_start(out=out.rearrange("(m p) n -> p m n", p=P)[:, tiles, cols], in_=products(cols, tiles))
+
+        def multiply_and_store(cols, tiles):
+            multiply(cols, tiles)
+            store(cols, tiles)
 
         def x_piece(c, share, matmuls):
             return (x_raw[c][:], share, x_codes[:, c, :], x_scales[:, c, :], E4M3X4, matmuls)
@@ -246,5 +254,7 @@ def tile_mix_ghost_none_kernel(tc, x, xt, g, gt, out):
             quantize_range(half, closing_matmuls(half))
         for tiles in (TOP, BOTTOM):
             multiply_and_store(THIRD, tiles)
-        for half in HALVES:
-            multiply_and_store(half, BOTH_TILES)
+        multiply(HALVES[0], BOTH_TILES)
+        for tiles in (TOP, BOTTOM):
+            multiply(HALVES[1], tiles)
+            store(LAST_STRIP, tiles)

@@ -35,17 +35,19 @@ HEAD = slice(0, BANK)
 FIRST = slice(BANK, BANK + STRIP)
 SECOND = slice(BANK + STRIP, BANK + 2 * STRIP)
 THIRD = slice(BANK + 2 * STRIP, BANK + 3 * STRIP)
-LAST_STRIP = slice(N - STRIP, N)
+FOURTH = slice(N - STRIP, N)
+RANGES = [HEAD, FIRST, SECOND, THIRD, FOURTH]
+BANK_PER_TILE = [HEAD, THIRD, FOURTH]
 HALVES = [slice(N - STRIP, N - P), slice(N - P, N)]
-RANGES = [HEAD, FIRST, SECOND, THIRD] + HALVES
-BANK_PER_TILE = [HEAD, THIRD]
+PARTS = RANGES[:-1] + HALVES
 
 
 SHARE_WHOLE_PASS = 288
 SHARE_NARROW = 128
-SHARE_FIRST = 112
-SHARE_SECOND = 48
-SHARE_THIRD = 80
+SHARE_FIRST = 128
+SHARE_SECOND = 0
+SHARE_THIRD = 96
+SHARE_LAST = 48
 
 
 def tile_mix_ghost_none_kernel(tc, x, xt, g, gt, out):
@@ -67,7 +69,7 @@ def tile_mix_ghost_none_kernel(tc, x, xt, g, gt, out):
         gt_raw = raws.tile([P, PACK, N], F32, align_bytes=DMA_ALIGN, name="gt_raw", tag="gt_then_res")
         x_raw = [raws.tile([P, PACK, M], F32, align_bytes=DMA_ALIGN, name="x_raw%d" % c) for c in range(PASSES)]
         xt_raw = [raws.tile([P, PACK, N], F32, align_bytes=DMA_ALIGN, name="xt_raw%d" % c) for c in range(LAST)]
-        part_raw = [raws.tile([P, PACK, width(cols)], F32, align_bytes=DMA_ALIGN, name="part_raw%d" % cols.start) for cols in RANGES]
+        part_raw = [raws.tile([P, PACK, width(cols)], F32, align_bytes=DMA_ALIGN, name="part_raw%d" % cols.start) for cols in PARTS]
 
         nc.sync.dma_start(out=g_raw[:], in_=rows(g, 0))
         nc.sync.dma_start(out=gt_raw[:], in_=rows(gt, 0))
@@ -75,7 +77,7 @@ def tile_mix_ghost_none_kernel(tc, x, xt, g, gt, out):
             nc.sync.dma_start(out=xt_raw[c][:], in_=rows(xt, c))
         for c in range(LAST):
             nc.sync.dma_start(out=x_raw[c][:], in_=rows(x, c))
-        for raw, cols in zip(part_raw, RANGES):
+        for raw, cols in zip(part_raw, PARTS):
             nc.sync.dma_start(out=raw[:], in_=rows(xt, LAST)[:, :, cols])
             if cols == HEAD:
                 nc.sync.dma_start(out=x_raw[LAST][:], in_=rows(x, LAST))
@@ -173,20 +175,13 @@ def tile_mix_ghost_none_kernel(tc, x, xt, g, gt, out):
             return [partial(a_pass, LAST, cols, tiles)] + [partial(a_pass, c, held) for c in range(1, LAST) for held in later]
 
         def products(cols, tiles):
-            stored = LAST_STRIP if cols in HALVES else cols
-            of_range = res[:, M_TILES * stored.start : M_TILES * stored.stop].rearrange("p (m n) -> p m n", m=M_TILES)
-            return of_range[:, tiles, cols.start - stored.start : cols.stop - stored.start]
-
-        def multiply(cols, tiles):
-            in_psum = sums(cols, tiles).rearrange("p (m n) -> p m n", n=width(cols))
-            nc.vector.tensor_tensor(out=products(cols, tiles), in0=in_psum, in1=u[:, tiles, cols], op=MULT)
-
-        def store(cols, tiles):
-            nc.sync.dma_start(out=out.rearrange("(m p) n -> p m n", p=P)[:, tiles, cols], in_=products(cols, tiles))
+            of_range = res[:, M_TILES * cols.start : M_TILES * cols.stop].rearrange("p (m n) -> p m n", m=M_TILES)
+            return of_range[:, tiles, :]
 
         def multiply_and_store(cols, tiles):
-            multiply(cols, tiles)
-            store(cols, tiles)
+            in_psum = sums(cols, tiles).rearrange("p (m n) -> p m n", n=width(cols))
+            nc.vector.tensor_tensor(out=products(cols, tiles), in0=in_psum, in1=u[:, tiles, cols], op=MULT)
+            nc.sync.dma_start(out=out.rearrange("(m p) n -> p m n", p=P)[:, tiles, cols], in_=products(cols, tiles))
 
         def x_piece(c, share, matmuls):
             return (x_raw[c][:], share, x_codes[:, c, :], x_scales[:, c, :], E4M3X4, matmuls)
@@ -196,7 +191,7 @@ def tile_mix_ghost_none_kernel(tc, x, xt, g, gt, out):
             return [(xt_raw[c][:, :, cols], SHARE_WHOLE_PASS, xt_codes[:, c, cols], xt_scales[:, c, cols], E4M3X4, []) for cols in columns]
 
         def round_part(cols, share):
-            round_shared(last_grouped[:, cols, :], part_raw[RANGES.index(cols)][:], share)
+            round_shared(last_grouped[:, cols, :], part_raw[PARTS.index(cols)][:], share)
 
         def quantize_range(cols, matmuls):
             quantize(last_grouped[:, cols, :], xt_codes[:, LAST, cols], xt_scales[:, LAST, cols], E4M3X4, matmuls)
@@ -240,21 +235,19 @@ def tile_mix_ghost_none_kernel(tc, x, xt, g, gt, out):
         quantize(last_third, *thirds[2][2:])
 
         quantize_range(FIRST, closing_matmuls(FIRST, THIRD))
-        multiply_and_store(HEAD, TOP)
         round_part(SECOND, SHARE_SECOND)
+        multiply_and_store(HEAD, TOP)
         multiply_and_store(HEAD, BOTTOM)
-        quantize_range(SECOND, closing_matmuls(SECOND, *HALVES))
         round_part(THIRD, SHARE_THIRD)
+        quantize_range(SECOND, closing_matmuls(SECOND, FOURTH))
         multiply_and_store(FIRST, BOTH_TILES)
         quantize_range(THIRD, closing_matmuls(THIRD))
-        for half in HALVES:
-            round_part(half, 0)
-        for half, tiles in zip(HALVES, (TOP, BOTTOM)):
-            multiply_and_store(SECOND, tiles)
-            quantize_range(half, closing_matmuls(half))
-        for tiles in (TOP, BOTTOM):
-            multiply_and_store(THIRD, tiles)
-        multiply(HALVES[0], BOTH_TILES)
-        for tiles in (TOP, BOTTOM):
-            multiply(HALVES[1], tiles)
-            store(LAST_STRIP, tiles)
+        round_part(HALVES[0], 0)
+        round_part(HALVES[1], SHARE_LAST)
+        quantize_range(HALVES[0], [])
+        multiply_and_store(SECOND, TOP)
+        quantize_range(HALVES[1], closing_matmuls(FOURTH))
+        multiply_and_store(SECOND, BOTTOM)
+        for cols in (THIRD, FOURTH):
+            for tiles in (TOP, BOTTOM):
+                multiply_and_store(cols, tiles)

@@ -32,22 +32,24 @@ BOTH_TILES = slice(0, M_TILES)
 TOP, BOTTOM = slice(0, 1), slice(1, 2)
 
 HEAD = slice(0, BANK)
-FIRST = slice(BANK, BANK + STRIP)
-SECOND = slice(BANK + STRIP, BANK + 2 * STRIP)
-THIRD = slice(BANK + 2 * STRIP, BANK + 3 * STRIP)
-FOURTH = slice(N - STRIP, N)
+FIRST, SECOND, THIRD, FOURTH = [slice(n0, n0 + STRIP) for n0 in range(BANK, N, STRIP)]
 RANGES = [HEAD, FIRST, SECOND, THIRD, FOURTH]
 BANK_PER_TILE = [HEAD, THIRD, FOURTH]
-HALVES = [slice(N - STRIP, N - P), slice(N - P, N)]
-PARTS = RANGES[:-1] + HALVES
 
+
+def halves(cols):
+    middle = (cols.start + cols.stop) // 2
+    return [slice(cols.start, middle), slice(middle, cols.stop)]
+
+
+PARTS = halves(HEAD) + [FIRST] + halves(SECOND) + halves(THIRD) + halves(FOURTH)
 
 SHARE_WHOLE_PASS = 288
-SHARE_NARROW = 128
-SHARE_FIRST = 128
-SHARE_SECOND = 0
-SHARE_THIRD = 96
-SHARE_LAST = 48
+SHARE_FIRST_THIRD = 384
+SHARE_LAST_THIRD = 192
+SHARE_FIRST = 160
+SHARE_THIRD = 48
+SHARE_FOURTH = 32
 
 
 def tile_mix_ghost_none_kernel(tc, x, xt, g, gt, out):
@@ -67,7 +69,10 @@ def tile_mix_ghost_none_kernel(tc, x, xt, g, gt, out):
 
         g_raw = raws.tile([P, PACK, M], F32, align_bytes=DMA_ALIGN, name="g_raw")
         gt_raw = raws.tile([P, PACK, N], F32, align_bytes=DMA_ALIGN, name="gt_raw", tag="gt_then_res")
-        x_raw = [raws.tile([P, PACK, M], F32, align_bytes=DMA_ALIGN, name="x_raw%d" % c) for c in range(PASSES)]
+        middle_x_raw = raws.tile([P, LAST - 1, PACK * M], F32, align_bytes=DMA_ALIGN, name="middle_x_raw")
+        first_x_raw = raws.tile([P, PACK, M], F32, align_bytes=DMA_ALIGN, name="first_x_raw")
+        last_x_raw = raws.tile([P, PACK, M], F32, align_bytes=DMA_ALIGN, name="last_x_raw")
+        x_raw = [first_x_raw[:]] + [middle_x_raw[:, c - 1, :].rearrange("p (t n) -> p t n", t=PACK) for c in range(1, LAST)]
         xt_raw = [raws.tile([P, PACK, N], F32, align_bytes=DMA_ALIGN, name="xt_raw%d" % c) for c in range(LAST)]
         part_raw = [raws.tile([P, PACK, width(cols)], F32, align_bytes=DMA_ALIGN, name="part_raw%d" % cols.start) for cols in PARTS]
 
@@ -75,12 +80,12 @@ def tile_mix_ghost_none_kernel(tc, x, xt, g, gt, out):
         nc.sync.dma_start(out=gt_raw[:], in_=rows(gt, 0))
         for c in range(LAST):
             nc.sync.dma_start(out=xt_raw[c][:], in_=rows(xt, c))
-        for c in range(LAST):
-            nc.sync.dma_start(out=x_raw[c][:], in_=rows(x, c))
+        nc.sync.dma_start(out=first_x_raw[:], in_=rows(x, 0))
+        nc.sync.dma_start(out=middle_x_raw[:], in_=x[K_PASS : LAST * K_PASS, :].rearrange("(c p t) n -> p c (t n)", p=P, t=PACK))
         for raw, cols in zip(part_raw, PARTS):
             nc.sync.dma_start(out=raw[:], in_=rows(xt, LAST)[:, :, cols])
-            if cols == HEAD:
-                nc.sync.dma_start(out=x_raw[LAST][:], in_=rows(x, LAST))
+            if cols.stop == HEAD.stop:
+                nc.sync.dma_start(out=last_x_raw[:], in_=rows(x, LAST))
 
         g_codes = keep.tile([P, M], U32, align_bytes=MX_ALIGN, name="g_codes")
         g_scales = keep.tile([P, M], U8, align_bytes=MX_ALIGN, name="g_scales")
@@ -178,20 +183,27 @@ def tile_mix_ghost_none_kernel(tc, x, xt, g, gt, out):
             of_range = res[:, M_TILES * cols.start : M_TILES * cols.stop].rearrange("p (m n) -> p m n", m=M_TILES)
             return of_range[:, tiles, :]
 
-        def multiply_and_store(cols, tiles):
+        def multiply(cols, tiles):
             in_psum = sums(cols, tiles).rearrange("p (m n) -> p m n", n=width(cols))
             nc.vector.tensor_tensor(out=products(cols, tiles), in0=in_psum, in1=u[:, tiles, cols], op=MULT)
+
+        def store(cols, tiles):
             nc.sync.dma_start(out=out.rearrange("(m p) n -> p m n", p=P)[:, tiles, cols], in_=products(cols, tiles))
 
-        def x_piece(c, share, matmuls):
-            return (x_raw[c][:], share, x_codes[:, c, :], x_scales[:, c, :], E4M3X4, matmuls)
+        def x_piece(c, ranges):
+            return (x_raw[c], M, x_codes[:, c, :], x_scales[:, c, :], E4M3X4, [partial(a_pass, c, cols) for cols in ranges])
 
-        def xt_pieces(c):
+        def xt_pieces(c, shares):
             columns = [slice(n0, n0 + BANK) for n0 in range(0, N, BANK)]
-            return [(xt_raw[c][:, :, cols], SHARE_WHOLE_PASS, xt_codes[:, c, cols], xt_scales[:, c, cols], E4M3X4, []) for cols in columns]
+            return [(xt_raw[c][:, :, cols], share, xt_codes[:, c, cols], xt_scales[:, c, cols], E4M3X4, []) for cols, share in zip(columns, shares)]
 
         def round_part(cols, share):
             round_shared(last_grouped[:, cols, :], part_raw[PARTS.index(cols)][:], share)
+
+        def round_halves(cols, share):
+            first_half, second_half = halves(cols)
+            round_part(first_half, 0)
+            round_part(second_half, share)
 
         def quantize_range(cols, matmuls):
             quantize(last_grouped[:, cols, :], xt_codes[:, LAST, cols], xt_scales[:, LAST, cols], E4M3X4, matmuls)
@@ -200,54 +212,55 @@ def tile_mix_ghost_none_kernel(tc, x, xt, g, gt, out):
             cols = slice(tiles.start * P, tiles.stop * P)
             quantize(last_x_grouped[:, cols, :], x_codes[:, LAST, cols], x_scales[:, LAST, cols], E4M3X4, matmuls)
 
-        u_pieces = [(g_raw[:], SHARE_NARROW, g_codes[:], g_scales[:], E5M2X4, [])]
+        u_pieces = [(g_raw[:], M // 2, g_codes[:], g_scales[:], E5M2X4, [])]
         for n0 in range(0, N, BANK):
             cols = slice(n0, n0 + BANK)
             u_pieces.append((gt_raw[:, :, cols], BANK // 2, gt_codes[:, cols], gt_scales[:, cols], E5M2X4, [partial(u_columns, cols)]))
         run(u_pieces)
         res = raws.tile([P, M_TILES * N], F32, align_bytes=DMA_ALIGN, name="res", tag="gt_then_res")
         for c in range(LAST - 1):
-            run(xt_pieces(c))
+            run(xt_pieces(c, [SHARE_WHOLE_PASS] * (N // BANK)))
 
-        thirds = xt_pieces(LAST - 1)
-        x_pieces = [x_piece(c, SHARE_NARROW, [partial(a_pass, c, cols) for cols in (RANGES if c == 0 else (HEAD, FIRST))]) for c in range(LAST)]
+        thirds = xt_pieces(LAST - 1, [SHARE_FIRST_THIRD, 0, SHARE_LAST_THIRD])
+        x_pieces = [x_piece(c, RANGES if c == 0 else (HEAD, FIRST)) for c in range(LAST)]
         first_third = round_piece(thirds[0])
-        second_third = staging_tile()
-        vector_rounds(second_third, *thirds[1][:2])
+        second_third = round_piece(thirds[1])
         x_first = round_piece(x_pieces[0])
-        scalar_rounds(second_third, *thirds[1][:2])
         quantize(first_third, *thirds[0][2:])
         quantize(x_first, *x_pieces[0][2:])
-        x_second = round_piece(x_pieces[1])
-        quantize(second_third, *thirds[1][2:])
         last_third = round_piece(thirds[2])
-        quantize(x_second, *x_pieces[1][2:])
+        quantize(second_third, *thirds[1][2:])
+        x_second = round_piece(x_pieces[1])
         x_third = round_piece(x_pieces[2])
-
-        round_part(HEAD, STRIP)
-        quantize(x_third, *x_pieces[2][2:])
-        quantize_range(slice(0, STRIP), [])
-        round_shared(last_x_grouped[:], x_raw[LAST][:], P)
-        quantize_range(slice(STRIP, BANK), [])
-        quantize_last_x(TOP, closing_matmuls(HEAD, tiles=TOP))
-        quantize_last_x(BOTTOM, closing_matmuls(HEAD, SECOND, tiles=BOTTOM))
-        round_part(FIRST, SHARE_FIRST)
+        quantize(x_second, *x_pieces[1][2:])
         quantize(last_third, *thirds[2][2:])
+        quantize(x_third, *x_pieces[2][2:])
+
+        round_halves(HEAD, 0)
+        quantize_range(halves(HEAD)[0], [])
+        round_shared(last_x_grouped[:], last_x_raw[:], P)
+        quantize_range(halves(HEAD)[1], [])
+        quantize_last_x(TOP, closing_matmuls(HEAD, tiles=TOP))
+        round_part(FIRST, SHARE_FIRST)
+        quantize_last_x(BOTTOM, closing_matmuls(HEAD, SECOND, tiles=BOTTOM))
 
         quantize_range(FIRST, closing_matmuls(FIRST, THIRD))
-        round_part(SECOND, SHARE_SECOND)
-        multiply_and_store(HEAD, TOP)
-        multiply_and_store(HEAD, BOTTOM)
-        round_part(THIRD, SHARE_THIRD)
+        multiply(HEAD, TOP)
+        round_halves(SECOND, 0)
+        multiply(HEAD, BOTTOM)
+        store(HEAD, BOTH_TILES)
         quantize_range(SECOND, closing_matmuls(SECOND, FOURTH))
-        multiply_and_store(FIRST, BOTH_TILES)
+        round_halves(THIRD, SHARE_THIRD)
+        multiply(FIRST, BOTH_TILES)
+        store(FIRST, BOTH_TILES)
         quantize_range(THIRD, closing_matmuls(THIRD))
-        round_part(HALVES[0], 0)
-        round_part(HALVES[1], SHARE_LAST)
-        quantize_range(HALVES[0], [])
-        multiply_and_store(SECOND, TOP)
-        quantize_range(HALVES[1], closing_matmuls(FOURTH))
-        multiply_and_store(SECOND, BOTTOM)
+        round_halves(FOURTH, SHARE_FOURTH)
+        multiply(SECOND, TOP)
+        quantize_range(halves(FOURTH)[0], [])
+        multiply(SECOND, BOTTOM)
+        store(SECOND, BOTH_TILES)
+        quantize_range(halves(FOURTH)[1], closing_matmuls(FOURTH))
         for cols in (THIRD, FOURTH):
             for tiles in (TOP, BOTTOM):
-                multiply_and_store(cols, tiles)
+                multiply(cols, tiles)
+                store(cols, tiles)

@@ -31,16 +31,17 @@ DMA_ALIGN = 256
 BOTH_TILES = slice(0, M_TILES)
 TOP, BOTTOM = slice(0, 1), slice(1, 2)
 
-HEAD = slice(0, BANK)
-FIRST, SECOND, THIRD, FOURTH = [slice(n0, n0 + STRIP) for n0 in range(BANK, N, STRIP)]
-RANGES = [HEAD, FIRST, SECOND, THIRD, FOURTH]
-BANK_PER_TILE = [HEAD, THIRD, FOURTH]
-
 
 def halves(cols):
     middle = (cols.start + cols.stop) // 2
     return [slice(cols.start, middle), slice(middle, cols.stop)]
 
+
+HEAD = slice(0, BANK)
+FIRST, SECOND, THIRD, FOURTH = [slice(n0, n0 + STRIP) for n0 in range(BANK, N, STRIP)]
+HALF_A, HALF_B = halves(FOURTH)
+RANGES = [HEAD, FIRST, SECOND, THIRD, HALF_A, HALF_B]
+BANK_PER_TILE = [HEAD, THIRD]
 
 PARTS = halves(HEAD) + [FIRST] + halves(SECOND) + halves(THIRD) + halves(FOURTH)
 
@@ -48,8 +49,7 @@ SHARE_WHOLE_PASS = 288
 SHARE_FIRST_THIRD = 384
 SHARE_LAST_THIRD = 192
 SHARE_FIRST = 160
-SHARE_THIRD = 48
-SHARE_FOURTH = 32
+SHARE_THIRD = 64
 
 
 def tile_mix_ghost_none_kernel(tc, x, xt, g, gt, out):
@@ -249,18 +249,20 @@ def tile_mix_ghost_none_kernel(tc, x, xt, g, gt, out):
         round_halves(SECOND, 0)
         multiply(HEAD, BOTTOM)
         store(HEAD, BOTH_TILES)
-        quantize_range(SECOND, closing_matmuls(SECOND, FOURTH))
+        quantize_range(SECOND, closing_matmuls(SECOND, HALF_A))
         round_halves(THIRD, SHARE_THIRD)
         multiply(FIRST, BOTH_TILES)
         store(FIRST, BOTH_TILES)
-        quantize_range(THIRD, closing_matmuls(THIRD))
-        round_halves(FOURTH, SHARE_FOURTH)
-        multiply(SECOND, TOP)
-        quantize_range(halves(FOURTH)[0], [])
-        multiply(SECOND, BOTTOM)
+        quantize_range(THIRD, closing_matmuls(THIRD, HALF_B))
+        round_halves(FOURTH, 0)
+        multiply(SECOND, BOTH_TILES)
         store(SECOND, BOTH_TILES)
-        quantize_range(halves(FOURTH)[1], closing_matmuls(FOURTH))
-        for cols in (THIRD, FOURTH):
-            for tiles in (TOP, BOTTOM):
-                multiply(cols, tiles)
-                store(cols, tiles)
+        quantize_range(HALF_A, closing_matmuls(HALF_A))
+        multiply(THIRD, TOP)
+        store(THIRD, TOP)
+        quantize_range(HALF_B, closing_matmuls(HALF_B))
+        multiply(THIRD, BOTTOM)
+        store(THIRD, BOTTOM)
+        for half in (HALF_A, HALF_B):
+            multiply(half, BOTH_TILES)
+            store(half, BOTH_TILES)

@@ -46,10 +46,11 @@ BANK_PER_TILE = [HEAD, THIRD]
 PARTS = halves(HEAD) + [FIRST] + halves(SECOND) + halves(THIRD) + halves(FOURTH)
 
 SHARE_WHOLE_PASS = 288
-SHARE_FIRST_THIRD = 384
+SHARE_FIRST_THIRD = 368
 SHARE_LAST_THIRD = 192
 SHARE_FIRST = 160
-SHARE_THIRD = 64
+SHARE_THIRD = 80
+SHARE_FOURTH = 16
 
 
 def tile_mix_ghost_none_kernel(tc, x, xt, g, gt, out):
@@ -254,15 +255,14 @@ def tile_mix_ghost_none_kernel(tc, x, xt, g, gt, out):
         multiply(FIRST, BOTH_TILES)
         store(FIRST, BOTH_TILES)
         quantize_range(THIRD, closing_matmuls(THIRD, HALF_B))
-        round_halves(FOURTH, 0)
+        round_halves(FOURTH, SHARE_FOURTH)
         multiply(SECOND, BOTH_TILES)
         store(SECOND, BOTH_TILES)
         quantize_range(HALF_A, closing_matmuls(HALF_A))
-        multiply(THIRD, TOP)
-        store(THIRD, TOP)
         quantize_range(HALF_B, closing_matmuls(HALF_B))
-        multiply(THIRD, BOTTOM)
-        store(THIRD, BOTTOM)
+        for tiles in (TOP, BOTTOM):
+            multiply(THIRD, tiles)
+            store(THIRD, tiles)
         for half in (HALF_A, HALF_B):
             multiply(half, BOTH_TILES)
             store(half, BOTH_TILES)

from contextlib import ExitStack
from functools import partial

import concourse.mybir as mybir

K, L, M, N = 2048, 512, 256, 1536
FLOPS = 2 * M * N * (K + L)

F32 = mybir.dt.float32
BF16 = mybir.dt.bfloat16
U32 = mybir.dt.uint32
U8 = mybir.dt.uint8
E4M3X4 = mybir.dt.float8_e4m3fn_x4
E5M2X4 = mybir.dt.float8_e5m2_x4
MULT = mybir.AluOpType.mult

P = 128
PACK = 4
K_PASS = P * PACK
PASSES = K // K_PASS
LAST = PASSES - 1
M_TILES = M // P
BANK = 512
BANKS = 8
STRIP = BANK // M_TILES
LINE = 4
STAGED = 5
MX_ALIGN = 256
DMA_ALIGN = 256

BOTH_TILES = slice(0, M_TILES)
TOP, BOTTOM = slice(0, 1), slice(1, 2)


def halves(cols):
    middle = (cols.start + cols.stop) // 2
    return [slice(cols.start, middle), slice(middle, cols.stop)]


HEAD = slice(0, BANK)
FIRST, SECOND, THIRD, FOURTH = [slice(n0, n0 + STRIP) for n0 in range(BANK, N, STRIP)]
HALF_A, HALF_B = halves(FOURTH)
RANGES = [HEAD, FIRST, SECOND, THIRD, HALF_A, HALF_B]
BANK_PER_TILE = [HEAD, THIRD]

PARTS = halves(HEAD) + [FIRST] + halves(SECOND) + halves(THIRD) + halves(FOURTH)

SHARE_WHOLE_PASS = 288
SHARE_FIRST_THIRD = 368
SHARE_LAST_THIRD = 192
SHARE_FIRST = 160
SHARE_THIRD = 80
SHARE_FOURTH = 16


def tile_mix_ghost_none_kernel(tc, x, xt, g, gt, out):
    nc = tc.nc
    with ExitStack() as ctx:
        ctx.enter_context(tc.manual_schedule())
        raws = ctx.enter_context(tc.tile_pool(name="raws", bufs=1))
        keep = ctx.enter_context(tc.tile_pool(name="keep", bufs=1))
        staging = ctx.enter_context(tc.tile_pool(name="staging", bufs=STAGED))
        psum = ctx.enter_context(tc.psum_pool(name="psum", bufs=BANKS))

        def rows(ap, c):
            return ap[c * K_PASS : (c + 1) * K_PASS, :].rearrange("(p t) n -> p t n", t=PACK)

        def width(cols):
            return cols.stop - cols.start

        g_raw = raws.tile([P, PACK, M], F32, align_bytes=DMA_ALIGN, name="g_raw")
        gt_raw = raws.tile([P, PACK, N], F32, align_bytes=DMA_ALIGN, name="gt_raw", tag="gt_then_res")
        middle_x_raw = raws.tile([P, LAST - 1, PACK * M], F32, align_bytes=DMA_ALIGN, name="middle_x_raw")
        first_x_raw = raws.tile([P, PACK, M], F32, align_bytes=DMA_ALIGN, name="first_x_raw")
        last_x_raw = raws.tile([P, PACK, M], F32, align_bytes=DMA_ALIGN, name="last_x_raw")
        x_raw = [first_x_raw[:]] + [middle_x_raw[:, c - 1, :].rearrange("p (t n) -> p t n", t=PACK) for c in range(1, LAST)]
        xt_raw = [raws.tile([P, PACK, N], F32, align_bytes=DMA_ALIGN, name="xt_raw%d" % c) for c in range(LAST)]
        part_raw = [raws.tile([P, PACK, width(cols)], F32, align_bytes=DMA_ALIGN, name="part_raw%d" % cols.start) for cols in PARTS]

        nc.sync.dma_start(out=g_raw[:], in_=rows(g, 0))
        nc.sync.dma_start(out=gt_raw[:], in_=rows(gt, 0))
        for c in range(LAST):
            nc.sync.dma_start(out=xt_raw[c][:], in_=rows(xt, c))
        nc.sync.dma_start(out=first_x_raw[:], in_=rows(x, 0))
        nc.sync.dma_start(out=middle_x_raw[:], in_=x[K_PASS : LAST * K_PASS, :].rearrange("(c p t) n -> p c (t n)", p=P, t=PACK))
        for raw, cols in zip(part_raw, PARTS):
            nc.sync.dma_start(out=raw[:], in_=rows(xt, LAST)[:, :, cols])
            if cols.stop == HEAD.stop:
                nc.sync.dma_start(out=last_x_raw[:], in_=rows(x, LAST))

        g_codes = keep.tile([P, M], U32, align_bytes=MX_ALIGN, name="g_codes")
        g_scales = keep.tile([P, M], U8, align_bytes=MX_ALIGN, name="g_scales")
        gt_codes = keep.tile([P, N], U32, align_bytes=MX_ALIGN, name="gt_codes")
        gt_scales = keep.tile([P, N], U8, align_bytes=MX_ALIGN, name="gt_scales")
        x_codes = keep.tile([P, PASSES, M], U32, align_bytes=MX_ALIGN, name="x_codes")
        x_scales = keep.tile([P, PASSES, M], U8, align_bytes=MX_ALIGN, name="x_scales")
        xt_codes = keep.tile([P, PASSES, N], U32, align_bytes=MX_ALIGN, name="xt_codes")
        xt_scales = keep.tile([P, PASSES, N], U8, align_bytes=MX_ALIGN, name="xt_scales")
        u = keep.tile([P, M_TILES, N], F32, align_bytes=DMA_ALIGN, name="u")
        last_grouped = keep.tile([P, N, PACK], BF16, align_bytes=MX_ALIGN, name="last_grouped")
        last_x_grouped = keep.tile([P, M, PACK], BF16, align_bytes=MX_ALIGN, name="last_x_grouped")

        def round_columns(copy, grouped, raw, cols):
            if width(cols):
                copy(
                    out=grouped[:, cols, :].rearrange("p (j i) t -> p j t i", i=LINE),
                    in_=raw[:, :, cols].rearrange("p t (j i) -> p j t i", i=LINE),
                )

        def vector_rounds(grouped, raw, share):
            round_columns(nc.vector.tensor_copy, grouped, raw, slice(0, share))

        def scalar_rounds(grouped, raw, share):
            round_columns(nc.scalar.copy, grouped, raw, slice(share, raw.shape[2]))

        def round_shared(grouped, raw, share):
            vector_rounds(grouped, raw, share)
            scalar_rounds(grouped, raw, share)

        def quantize(grouped, codes, scales, fmt, matmuls):
            nc.vector.quantize_mx(out=codes.bitcast(fmt), scales=scales, in_=grouped[:, : codes.shape[1], :].rearrange("p n t -> p (n t)"))
            for matmul in matmuls:
                matmul()

        def staging_tile():
            return staging.tile([P, BANK, PACK], BF16, align_bytes=MX_ALIGN, name="grouped")

        def round_piece(piece):
            grouped = staging_tile()
            round_shared(grouped, *piece[:2])
            return grouped

        def run(pieces):
            grouped = round_piece(pieces[0])
            for piece, following in zip(pieces, pieces[1:]):
                grouped_next = round_piece(following)
                quantize(grouped, *piece[2:])
                grouped = grouped_next
            quantize(grouped, *pieces[-1][2:])

        def u_columns(cols):
            for m in range(M_TILES):
                tile_m = slice(m * P, (m + 1) * P)
                bank = psum.tile([P, BANK], F32, name="bank")
                nc.tensor.matmul_mx(
                    out=bank[:],
                    lhsT=g_codes[:, tile_m].bitcast(E5M2X4),
                    lhsT_scale=g_scales[:, tile_m],
                    rhs=gt_codes[:, cols].bitcast(E5M2X4),
                    rhs_scale=gt_scales[:, cols],
                    start=True,
                    stop=True,
                )
                nc.scalar.copy(out=u[:, m, cols], in_=bank[:])

        range_banks = {}

        def sums(cols, tiles):
            banks = range_banks[cols.start]
            if cols in BANK_PER_TILE:
                return banks[tiles.start][:, : width(cols)]
            return banks[0][:, tiles.start * width(cols) : tiles.stop * width(cols)]

        def a_pass(c, cols, tiles=BOTH_TILES):
            own_bank = cols in BANK_PER_TILE
            if c == 0:
                range_banks[cols.start] = [psum.tile([P, BANK], F32, name="bank") for m in range(M_TILES if own_bank else 1)]
            for m in range(tiles.start, tiles.stop):
                tile_m = slice(m * P, (m + 1) * P)
                nc.tensor.matmul_mx(
                    out=sums(cols, slice(m, m + 1)),
                    lhsT=x_codes[:, c, tile_m].bitcast(E4M3X4),
                    lhsT_scale=x_scales[:, c, tile_m],
                    rhs=xt_codes[:, c, cols].bitcast(E4M3X4),
                    rhs_scale=xt_scales[:, c, cols],
                    start=c == 0 and (own_bank or m == 0),
                    stop=c == LAST and (own_bank or m == M_TILES - 1),
                )

        def closing_matmuls(cols, *later, tiles=BOTH_TILES):
            return [partial(a_pass, LAST, cols, tiles)] + [partial(a_pass, c, held) for c in range(1, LAST) for held in later]

        def products(cols, tiles):
            of_range = res[:, M_TILES * cols.start : M_TILES * cols.stop].rearrange("p (m n) -> p m n", m=M_TILES)
            return of_range[:, tiles, :]

        def multiply(cols, tiles):
            in_psum = sums(cols, tiles).rearrange("p (m n) -> p m n", n=width(cols))
            nc.vector.tensor_tensor(out=products(cols, tiles), in0=in_psum, in1=u[:, tiles, cols], op=MULT)

        def store(cols, tiles):
            nc.sync.dma_start(out=out.rearrange("(m p) n -> p m n", p=P)[:, tiles, cols], in_=products(cols, tiles))

        def x_piece(c, ranges):
            return (x_raw[c], M, x_codes[:, c, :], x_scales[:, c, :], E4M3X4, [partial(a_pass, c, cols) for cols in ranges])

        def xt_pieces(c, shares):
            columns = [slice(n0, n0 + BANK) for n0 in range(0, N, BANK)]
            return [(xt_raw[c][:, :, cols], share, xt_codes[:, c, cols], xt_scales[:, c, cols], E4M3X4, []) for cols, share in zip(columns, shares)]

        def round_part(cols, share):
            round_shared(last_grouped[:, cols, :], part_raw[PARTS.index(cols)][:], share)

        def round_halves(cols, share):
            first_half, second_half = halves(cols)
            round_part(first_half, 0)
            round_part(second_half, share)

        def quantize_range(cols, matmuls):
            quantize(last_grouped[:, cols, :], xt_codes[:, LAST, cols], xt_scales[:, LAST, cols], E4M3X4, matmuls)

        def quantize_last_x(tiles, matmuls):
            cols = slice(tiles.start * P, tiles.stop * P)
            quantize(last_x_grouped[:, cols, :], x_codes[:, LAST, cols], x_scales[:, LAST, cols], E4M3X4, matmuls)

        u_pieces = [(g_raw[:], M // 2, g_codes[:], g_scales[:], E5M2X4, [])]
        for n0 in range(0, N, BANK):
            cols = slice(n0, n0 + BANK)
            u_pieces.append((gt_raw[:, :, cols], BANK // 2, gt_codes[:, cols], gt_scales[:, cols], E5M2X4, [partial(u_columns, cols)]))
        run(u_pieces)
        res = raws.tile([P, M_TILES * N], F32, align_bytes=DMA_ALIGN, name="res", tag="gt_then_res")
        for c in range(LAST - 1):
            run(xt_pieces(c, [SHARE_WHOLE_PASS] * (N // BANK)))

        thirds = xt_pieces(LAST - 1, [SHARE_FIRST_THIRD, 0, SHARE_LAST_THIRD])
        x_pieces = [x_piece(c, RANGES if c == 0 else (HEAD, FIRST)) for c in range(LAST)]
        first_third = round_piece(thirds[0])
        second_third = round_piece(thirds[1])
        x_first = round_piece(x_pieces[0])
        quantize(first_third, *thirds[0][2:])
        quantize(x_first, *x_pieces[0][2:])
        last_third = round_piece(thirds[2])
        quantize(second_third, *thirds[1][2:])
        x_second = round_piece(x_pieces[1])
        x_third = round_piece(x_pieces[2])
        quantize(x_second, *x_pieces[1][2:])
        quantize(last_third, *thirds[2][2:])
        quantize(x_third, *x_pieces[2][2:])

        round_halves(HEAD, 0)
        quantize_range(halves(HEAD)[0], [])
        round_shared(last_x_grouped[:], last_x_raw[:], P)
        quantize_range(halves(HEAD)[1], [])
        quantize_last_x(TOP, closing_matmuls(HEAD, tiles=TOP))
        round_part(FIRST, SHARE_FIRST)
        quantize_last_x(BOTTOM, closing_matmuls(HEAD, SECOND, tiles=BOTTOM))

        quantize_range(FIRST, closing_matmuls(FIRST, THIRD))
        multiply(HEAD, TOP)
        round_halves(SECOND, 0)
        multiply(HEAD, BOTTOM)
        store(HEAD, BOTH_TILES)
        quantize_range(SECOND, closing_matmuls(SECOND, HALF_A))
        round_halves(THIRD, SHARE_THIRD)
        multiply(FIRST, BOTH_TILES)
        store(FIRST, BOTH_TILES)
        quantize_range(THIRD, closing_matmuls(THIRD, HALF_B))
        round_halves(FOURTH, SHARE_FOURTH)
        multiply(SECOND, BOTH_TILES)
        store(SECOND, BOTH_TILES)
        quantize_range(HALF_A, closing_matmuls(HALF_A))
        quantize_range(HALF_B, closing_matmuls(HALF_B))
        for tiles in (TOP, BOTTOM):
            multiply(THIRD, tiles)
            store(THIRD, tiles)
        for half in (HALF_A, HALF_B):
            multiply(half, BOTH_TILES)
            store(half, BOTH_TILES)
